import numpy as np
import ml_dtypes


def mxq(x, axis, fmt="e4m3"):
    dtype, down = {"e4m3": (ml_dtypes.float8_e4m3fn, 7), "e5m2": (ml_dtypes.float8_e5m2, 14)}[fmt]
    v = np.moveaxis(np.asarray(x, np.float32).astype(ml_dtypes.bfloat16).astype(np.float64), axis, -1)
    blocks = v.reshape(v.shape[:-1] + (-1, 32))
    amax = np.abs(blocks).max(-1, keepdims=True)
    byte = np.maximum(np.where(amax > 0, np.frexp(amax)[1] - 1 + 127, 0) - down, 1)
    scale = np.exp2(byte - 127.0)
    codes = (blocks / scale).astype(np.float32).astype(dtype).astype(np.float64)
    return np.moveaxis((codes * scale).reshape(v.shape), -1, axis)


WIDE = False


def mx_kscale(k):
    if not WIDE:
        return np.ones(k)
    levels = np.array([10, -10, 5, -5, 0])
    if k % 512:
        return np.exp2(np.random.permutation(np.resize(levels, k // 32))).repeat(32)
    a = np.empty((k // 512, 16))
    for p in range(k // 512):
        a[p, :8] = np.random.permutation(np.resize(levels, 8))
        for g in range(8):
            far = levels[np.abs(levels - a[p, g]) >= 10]
            a[p, g + 8] = far[np.random.randint(len(far))]
    return np.exp2(a.ravel()).repeat(32)


def f64(x):
    return np.asarray(x).astype(np.float64)


def striped(idx):
    return np.tile(idx.reshape(-1, 16).T, (8, 1)).astype(np.uint16)


def unstriped(offs):
    return offs[:16].T.reshape(-1).astype(np.int64)


E2M1 = np.array([0.0, 0.5, 1.0, 1.5, 2.0, 3.0, 4.0, 6.0, -0.0, -0.5, -1.0, -1.5, -2.0, -3.0, -4.0, -6.0])


def pack_weight(w, fmt):
    k, n = w.shape
    w = f64(np.asarray(w, np.float32).astype(ml_dtypes.bfloat16)).reshape(k // 32, 32, n)
    amax = np.abs(w).max(1)
    if fmt == "e4m3":
        byte = np.frexp(amax)[1] - 1 + 127 - 7
    else:
        mant, ex = np.frexp(amax / 6.0)
        byte = np.where(mant > 0.5, ex, ex - 1) + 127
    byte = np.clip(np.where(amax > 0, byte, 1), 1, 254)
    scaled = (w * np.exp2(127.0 - byte)[:, None, :]).reshape(k, n).astype(np.float32)
    by_word = np.ascontiguousarray(scaled.reshape(k // 512, 128, 4, n).transpose(0, 1, 3, 2))
    if fmt == "e4m3":
        words = by_word.astype(ml_dtypes.float8_e4m3fn).view(np.uint8)
    else:
        c = by_word.astype(ml_dtypes.float4_e2m1fn).view(np.uint8) & 0xF
        words = (c[..., 0::2] | (c[..., 1::2] << 4)).reshape(k // 512, 128, 2 * n)
    return np.ascontiguousarray(words), np.ascontiguousarray(byte.astype(np.uint8).reshape(k // 512, 16, n))


def unpack_weight(words, scales, fmt):
    g, _, n = scales.shape
    words = np.ascontiguousarray(words).reshape(g, 128, n, -1)
    if fmt == "e4m3":
        vals = words.view(ml_dtypes.float8_e4m3fn).astype(np.float64)
    else:
        nib = np.empty((g, 128, n, 4), np.uint8)
        nib[..., 0::2] = words & 0xF
        nib[..., 1::2] = words >> 4
        vals = E2M1[nib]
    vals = vals * np.repeat(np.exp2(scales.astype(np.float64) - 127.0), 8, axis=1)[..., None]
    return vals.transpose(0, 1, 3, 2).reshape(g * 512, n)


def gelu(v):
    return 0.5 * v * (1.0 + np.tanh(np.sqrt(2.0 / np.pi) * (v + 0.044715 * v**3)))


K, H, N, T, S = 1024, 512, 256, 2048, 1024

def setup_inputs():
    n = np.random.standard_normal
    s = mx_kscale(K)[:, None]
    u = mx_kscale(H)[:, None]
    tab_words, tab_scales = pack_weight(n((K, T)) * s, "e4m3")
    wr_words, wr_scales = pack_weight(n((K, H)) / np.sqrt(K) / s, "e2m1")
    wk_words, wk_scales = pack_weight(0.5 * n((K, H)) / np.sqrt(K) / s * u.T, "e4m3")
    return {
        "tab_words": tab_words, "tab_scales": tab_scales,
        "offs": striped(np.random.permutation(T)[:S]),
        "offs2": striped(np.random.permutation(T)[:S]),
        "offs3": striped(np.random.permutation(T)[:S]),
        "wl": (n((K, H)) / np.sqrt(K) / s).astype(np.float32),
        "wr_words": wr_words, "wr_scales": wr_scales,
        "wk_words": wk_words, "wk_scales": wk_scales,
        "g": (np.exp(0.3 * n(H)) * u[:, 0]).astype(np.float32),
        "wo": (1.5 * n((H, N)) / np.sqrt(H) / u).astype(np.float32),
    }

def reference(tab_words, tab_scales, offs, offs2, offs3, wl, wr_words, wr_scales, wk_words, wk_scales, g, wo):
    left = unpack_weight(tab_words, tab_scales, "e4m3")[:, unstriped(offs)]
    right = unpack_weight(tab_words, tab_scales, "e4m3")[:, unstriped(offs2)]
    key = unpack_weight(tab_words, tab_scales, "e4m3")[:, unstriped(offs3)]
    a = mxq(f64(wl), 0, "e4m3").T @ left
    b = unpack_weight(wr_words, wr_scales, "e2m1").T @ right
    c = unpack_weight(wk_words, wk_scales, "e4m3").T @ key
    h = np.tanh(a) * np.tanh(b) * f64(g)[:, None] - c
    return mxq(f64(wo), 0, "e4m3").T @ mxq(h, 0, "e4m3")

@@ -1,0 +1,270 @@
+from contextlib import ExitStack
+
+import concourse.mybir as mybir
+
+K, H, N, T, S = 1024, 512, 256, 2048, 1024
+FLOPS = 2 * S * H * (3 * K + N)
+
+F32 = mybir.dt.float32
+BF16 = mybir.dt.bfloat16
+I32 = mybir.dt.int32
+U32 = mybir.dt.uint32
+U16 = mybir.dt.uint16
+U8 = mybir.dt.uint8
+FP8X4 = mybir.dt.float8_e4m3fn_x4
+FP4X4 = mybir.dt.float4_e2m1fn_x4
+ALU = mybir.AluOpType
+ACT = mybir.ActivationFunctionType
+
+P = 128
+PASSES = K // 512
+HALF = S // 2
+
+
+def tile_list_record_match_scores_kernel(
+    tc, tab_words, tab_scales, offs, offs2, offs3, wl, wr_words, wr_scales, wk_words, wk_scales, g, wo, out
+):
+    nc = tc.nc
+    with ExitStack() as ctx:
+        keep = ctx.enter_context(tc.tile_pool(name="keep", bufs=1))
+        res_pool = ctx.enter_context(tc.tile_pool(name="res", bufs=5))
+        acc_pool = ctx.enter_context(tc.psum_pool(name="acc", bufs=1))
+        out_pool = ctx.enter_context(tc.psum_pool(name="outp", bufs=2))
+
+        def held(shape, dtype, name, slot=None):
+            return keep.tile(shape, dtype, name=name, tag=slot or name, align_bytes=64)
+
+        list_l = keep.tile([P, S // 16], U16, name="list_l")
+        list_r = keep.tile([P, S // 16], U16, name="list_r")
+        list_k = keep.tile([P, S // 16], U16, name="list_k")
+        tab_sc = held([P, T // 4], I32, "tab_sc")
+        tab_w = [held([P, T], I32, "tab_w%d" % a) for a in range(PASSES)]
+        wr_raw = held([P, PASSES, H // 2], I32, "wr_raw")
+        wr_sc_raw = held([P, PASSES, H // 4], I32, "wr_sc_raw")
+        wk_raw = held([P, PASSES, H], I32, "wk_raw")
+        wk_sc_raw = held([P, H // 4], I32, "wk_sc_raw")
+        wl_raw = [held([P, 4, H], F32, "wl_raw%d" % a) for a in range(PASSES)]
+        wo_raw = held([P, 4, N], F32, "wo_raw")
+        gain = [held([P, 1], F32, "gain%d" % t) for t in range(4)]
+        right_sc1 = held([P, S // 4], I32, "right_sc1")
+
+        nc.vector.memset(tab_sc[:], 0)
+        nc.vector.memset(wr_sc_raw[:], 0)
+        nc.vector.memset(right_sc1[:], 0)
+        nc.vector.memset(wk_sc_raw[:], 0)
+
+        def load_table(a):
+            nc.sync.dma_start(tab_w[a][:], tab_words[a].rearrange("p t i -> p (t i)").bitcast(I32))
+
+        nc.sync.dma_start(list_r[:], offs2)
+        for q in range(4):
+            nc.sync.dma_start(tab_sc[32 * q : 32 * q + 8, :], tab_scales[:, 4 * q : 4 * q + 4, :].bitcast(I32))
+        load_table(0)
+        nc.sync.dma_start(list_l[:], offs)
+        for q in range(4):
+            nc.sync.dma_start(
+                wr_sc_raw[32 * q : 32 * q + 4, :, :],
+                wr_scales[:, 4 * q : 4 * q + 4, :].bitcast(I32).rearrange("a r w -> r a w"),
+            )
+
+        def gather_scales(dst, lst, j0, j1):
+            nc.vector.tensor_copy(dst, tab_sc[:].bitcast(U8).indirect(lst[:, j0 // 16 : j1 // 16]))
+
+        def gather_words(dst, lst, a, j0, j1):
+            nc.vector.tensor_copy(dst, tab_w[a][:].bitcast(U32).indirect(lst[:, j0 // 16 : j1 // 16]))
+
+        right_sc = held([P, S], U8, "right_sc")
+        gather_scales(right_sc[:], list_r, 0, S)
+        right_planes = [right_sc[:], right_sc1[:].bitcast(U8)]
+
+        for a in range(PASSES):
+            nc.sync.dma_start(wl_raw[a][:], wl[512 * a : 512 * (a + 1), :].rearrange("(p j) r -> p j r", j=4))
+        nc.sync.dma_start(wr_raw[:], wr_words.bitcast(I32).rearrange("a p w -> p a w"))
+        load_table(1)
+        for q in range(4):
+            nc.sync.dma_start(right_sc1[32 * q : 32 * q + 4, :], right_sc[32 * q + 4 : 32 * q + 8, :].bitcast(I32))
+        with nc.allow_non_contiguous_dma(reason="one gain to a partition"):
+            for t in range(4):
+                nc.sync.dma_start(gain[t][:], g.rearrange("(u t e) -> t u e", t=4, e=4)[t])
+        nc.sync.dma_start(wk_raw[:], wk_words.rearrange("a p r i -> p a (r i)").bitcast(I32))
+        nc.sync.dma_start(list_k[:], offs3)
+        for q in range(4):
+            nc.sync.dma_start(wk_sc_raw[32 * q : 32 * q + 8, :], wk_scales[:, 4 * q : 4 * q + 4, :].bitcast(I32))
+        for t in range(4):
+            nc.sync.dma_start(wo_raw[:, t, :], wo.rearrange("(u t e) n -> t u e n", t=4, e=4)[t])
+
+        left_w, right_w, key_w, left_sc = {}, {}, {}, {}
+        for half in range(2):
+            right_w[0, half] = held([P, HALF], U32, "right_w0%d" % half)
+            gather_words(right_w[0, half][:], list_r, 0, half * HALF, (half + 1) * HALF)
+        for half in range(2):
+            left_w[0, half] = held([P, HALF], U32, "left_w0%d" % half)
+            gather_words(left_w[0, half][:], list_l, 0, half * HALF, (half + 1) * HALF)
+
+        wl_w = held([P, PASSES, H], U32, "wl_w")
+        wl_sc = held([P, PASSES, H], U8, "wl_sc")
+        wl_bf = {}
+        for a in range(PASSES):
+            for t0 in range(0, 4, 2):
+                wl_bf[a, t0] = held([P, 2, 4 * P], BF16, "wl_bf%d%d" % (a, t0))
+                for t in range(t0, t0 + 2):
+                    nc.scalar.copy(
+                        wl_bf[a, t0][:, t - t0, :].rearrange("p (u e j) -> p u j e", e=4, j=4),
+                        wl_raw[a][:].rearrange("p j (u t e) -> p t u j e", t=4, e=4)[:, t],
+                    )
+
+        def quantize_wl(a):
+            for t0 in range(0, 4, 2):
+                cols = slice(t0 * P, (t0 + 2) * P)
+                nc.vector.quantize_mx(
+                    out=wl_w[:, a, cols].bitcast(FP8X4),
+                    scales=wl_sc[:, a, cols],
+                    in_=wl_bf[a, t0][:].rearrange("p t x -> p (t x)"),
+                )
+
+        left_sc[0] = held([P, HALF], U8, "left_sc0")
+        gather_scales(left_sc[0][:], list_l, 0, HALF)
+        quantize_wl(0)
+        wr_w = held([P, PASSES, 4, 2 * P], U8, "wr_w")
+        wr_sc = held([P, PASSES, 4, P], U8, "wr_sc")
+        nc.vector.tensor_copy(
+            wr_w[:].bitcast(I32).rearrange("p a t (u w) -> p a t u w", w=2),
+            wr_raw[:].rearrange("p a (u t w) -> p a t u w", t=4, w=2),
+        )
+        nc.vector.tensor_copy(wr_sc[:].bitcast(I32), wr_sc_raw[:].rearrange("p a (u t) -> p a t u", t=4))
+
+        agree = []
+        for half in range(2):
+            j0 = half * HALF
+            cols = slice(j0, j0 + HALF)
+            right_w[1, half] = held([P, HALF], U32, "right_w1%d" % half, "wl_bf12" if half else None)
+            gather_words(right_w[1, half][:], list_r, 1, j0, j0 + HALF)
+            tanh_b = held([P, 4, HALF], F32, "tanh_b%d" % half)
+            gated_b = held([P, 4, HALF], F32, "gated_b%d" % half)
+            for t in range(4):
+                acc = acc_pool.tile([P, HALF], F32, name="acc", tag="bank%d" % t)
+                for a in range(PASSES):
+                    nc.tensor.matmul_mx(
+                        out=acc[:],
+                        lhsT=wr_w[:, a, t, :].bitcast(FP4X4),
+                        lhsT_scale=wr_sc[:, a, t, :],
+                        rhs=right_w[a, half][:].bitcast(FP8X4),
+                        rhs_scale=right_planes[a][:, cols],
+                        start=(a == 0),
+                        stop=(a == PASSES - 1),
+                    )
+                nc.scalar.activation(tanh_b[:, t, :], acc[:], ACT.Tanh)
+                if half == 0:
+                    nc.gpsimd.tensor_scalar(gated_b[:, t, :], tanh_b[:, t, :], gain[t][:], 0.0, ALU.mult, ALU.add)
+                else:
+                    nc.scalar.activation(gated_b[:, t, :], tanh_b[:, t, :], ACT.Copy, scale=gain[t][:])
+
+            if half == 0:
+                quantize_wl(1)
+            else:
+                left_sc[1] = held([P, HALF], U8, "left_sc1", "wr_raw")
+                gather_scales(left_sc[1][:], list_l, j0, j0 + HALF)
+            left_w[1, half] = held([P, HALF], U32, "left_w1%d" % half, "wl_bf10" if half else None)
+            for c0 in range(0, HALF, 256):
+                part = slice(c0, c0 + 256)
+                tanh_a = held([P, 4, 256], F32, "tanh_a%d" % (j0 + c0))
+                agree.append(held([P, 4, 256], F32, "agree%d" % (j0 + c0)))
+                gather_words(left_w[1, half][:, part], list_l, 1, j0 + c0, j0 + c0 + 256)
+                for t0 in range(0, 4, 2):
+                    acc = acc_pool.tile([P, 2, 256], F32, name="acc", tag="bank%d" % (c0 // P + t0 // 2))
+                    for t in range(t0, t0 + 2):
+                        for a in range(PASSES):
+                            nc.tensor.matmul_mx(
+                                out=acc[:, t - t0, :],
+                                lhsT=wl_w[:, a, t * P : (t + 1) * P].bitcast(FP8X4),
+                                lhsT_scale=wl_sc[:, a, t * P : (t + 1) * P],
+                                rhs=left_w[a, half][:, part].bitcast(FP8X4),
+                                rhs_scale=left_sc[half][4 * a : P, part],
+                                start=(a == 0),
+                                stop=(a == PASSES - 1),
+                            )
+                    nc.scalar.activation(tanh_a[:, t0 : t0 + 2, :], acc[:], ACT.Tanh)
+                    nc.gpsimd.tensor_tensor(
+                        agree[-1][:, t0 : t0 + 2, :], tanh_a[:, t0 : t0 + 2, :], gated_b[:, t0 : t0 + 2, part], ALU.mult
+                    )
+
+        wk_w = held([P, PASSES, 4, P], I32, "wk_w")
+        wk_sc = held([P, 4, P], U8, "wk_sc")
+        nc.vector.tensor_copy(
+            wk_w[:].rearrange("p a t (u e) -> p a t u e", e=4),
+            wk_raw[:].rearrange("p a (u t e) -> p a t u e", t=4, e=4),
+        )
+        nc.vector.tensor_copy(wk_sc[:].bitcast(I32), wk_sc_raw[:].rearrange("p (u t) -> p t u", t=4))
+        wo_bf = held([P, 4 * N], BF16, "wo_bf", "tanh_b0")
+        wo_w = held([P, N], U32, "wo_w")
+        wo_sc = held([P, N], U8, "wo_sc")
+        nc.scalar.copy(
+            wo_bf[:].rearrange("p (c i t) -> p c t i", i=4, t=4),
+            wo_raw[:].rearrange("p t (c i) -> p c t i", i=4),
+        )
+        nc.vector.quantize_mx(out=wo_w[:].bitcast(FP8X4), scales=wo_sc[:], in_=wo_bf[:])
+
+        key_sc = held([P, S], U8, "key_sc", "left_sc0")
+        gather_scales(key_sc[:], list_k, 0, S)
+        for half in range(2):
+            j0 = half * HALF
+            for a in range(PASSES):
+                key_w[a, half] = held([P, HALF], U32, "key_w%d%d" % (a, half), "%s_w%d0" % (("right", "left")[half], a))
+            gather_words(key_w[0, half][:], list_k, 0, j0, j0 + HALF)
+            for c0 in range(0, HALF, 256):
+                gather_words(key_w[1, half][:, c0 : c0 + 256], list_k, 1, j0 + c0, j0 + c0 + 256)
+
+        h_bf = held([P, 4 * S], BF16, "h_bf")
+        h_w = held([P, S], U32, "h_w")
+        h_sc = held([P, S], U8, "h_sc")
+        out_v = out.rearrange("(m p) j -> p m j", p=P)
+
+        def subtract_key(j0):
+            cols = slice(j0, j0 + P)
+            half, c0 = divmod(j0, HALF)
+            acc = acc_pool.tile([P, 4, P], F32, name="acc", tag="bank%d" % ((j0 // P + 4) % 6))
+            for t in range(4):
+                for a in range(PASSES):
+                    nc.tensor.matmul_mx(
+                        out=acc[:, t, :],
+                        lhsT=wk_w[:, a, t, :].bitcast(FP8X4),
+                        lhsT_scale=wk_sc[4 * a : P, t, :],
+                        rhs=key_w[a, half][:, c0 : c0 + P].bitcast(FP8X4),
+                        rhs_scale=key_sc[4 * a : P, cols],
+                        start=(a == 0),
+                        stop=(a == PASSES - 1),
+                    )
+            nc.vector.tensor_tensor(
+                h_bf[:, 4 * j0 : 4 * (j0 + P)].rearrange("p (c i t) -> p c t i", i=2, t=4),
+                agree[j0 // 256][:, :, j0 % 256 : j0 % 256 + P].rearrange("p t (c i) -> p c t i", i=2),
+                acc[:].rearrange("p t (c i) -> p c t i", i=2),
+                ALU.subtract,
+            )
+
+        def score(j0, j1):
+            cols = slice(j0, j1)
+            nc.vector.quantize_mx(out=h_w[:, cols].bitcast(FP8X4), scales=h_sc[:, cols], in_=h_bf[:, 4 * j0 : 4 * j1])
+            acc = out_pool.tile([P, 2, j1 - j0], F32, name="scores")
+            for m in range(2):
+                nc.tensor.matmul_mx(
+                    out=acc[:, m, :],
+                    lhsT=wo_w[:, m * P : (m + 1) * P].bitcast(FP8X4),
+                    lhsT_scale=wo_sc[:, m * P : (m + 1) * P],
+                    rhs=h_w[:, cols].bitcast(FP8X4),
+                    rhs_scale=h_sc[:, cols],
+                    start=True,
+                    stop=True,
+                )
+            res = res_pool.tile([P, 2, j1 - j0], F32, name="res")
+            nc.scalar.copy(res[:], acc[:])
+            nc.sync.dma_start(out_v[:, :, cols], res[:])
+
+        edges = [0, 256, 512, 768, 896, 1024]
+        done = 0
+        for j0 in range(0, S, P):
+            subtract_key(j0)
+            if edges[done + 1] <= j0:
+                score(edges[done], edges[done + 1])
+                done += 1
+        for i in range(done, len(edges) - 1):
+            score(edges[i], edges[i + 1])

@@ -27,9 +27,8 @@ def tile_list_record_match_scores_kernel(
     nc = tc.nc
     with ExitStack() as ctx:
         keep = ctx.enter_context(tc.tile_pool(name="keep", bufs=1))
-        res_pool = ctx.enter_context(tc.tile_pool(name="res", bufs=5))
+        res_pool = ctx.enter_context(tc.tile_pool(name="res", bufs=6))
         acc_pool = ctx.enter_context(tc.psum_pool(name="acc", bufs=1))
-        out_pool = ctx.enter_context(tc.psum_pool(name="outp", bufs=2))
 
         def held(shape, dtype, name, slot=None):
             return keep.tile(shape, dtype, name=name, tag=slot or name, align_bytes=64)
@@ -140,7 +139,8 @@ def tile_list_record_match_scores_kernel(
             right_w[1, half] = held([P, HALF], U32, "right_w1%d" % half, "wl_bf12" if half else None)
             gather_words(right_w[1, half][:], list_r, 1, j0, j0 + HALF)
             tanh_b = held([P, 4, HALF], F32, "tanh_b%d" % half)
-            gated_b = held([P, 4, HALF], F32, "gated_b%d" % half)
+            tanh_a = held([P, 4, HALF], F32, "tanh_a%d" % half)
+            agree.append(held([P, 4, HALF], F32, "agree%d" % half))
             for t in range(4):
                 acc = acc_pool.tile([P, HALF], F32, name="acc", tag="bank%d" % t)
                 for a in range(PASSES):
@@ -154,10 +154,6 @@ def tile_list_record_match_scores_kernel(
                         stop=(a == PASSES - 1),
                     )
                 nc.scalar.activation(tanh_b[:, t, :], acc[:], ACT.Tanh)
-                if half == 0:
-                    nc.gpsimd.tensor_scalar(gated_b[:, t, :], tanh_b[:, t, :], gain[t][:], 0.0, ALU.mult, ALU.add)
-                else:
-                    nc.scalar.activation(gated_b[:, t, :], tanh_b[:, t, :], ACT.Copy, scale=gain[t][:])
 
             if half == 0:
                 quantize_wl(1)
@@ -167,8 +163,6 @@ def tile_list_record_match_scores_kernel(
             left_w[1, half] = held([P, HALF], U32, "left_w1%d" % half, "wl_bf10" if half else None)
             for c0 in range(0, HALF, 256):
                 part = slice(c0, c0 + 256)
-                tanh_a = held([P, 4, 256], F32, "tanh_a%d" % (j0 + c0))
-                agree.append(held([P, 4, 256], F32, "agree%d" % (j0 + c0)))
                 gather_words(left_w[1, half][:, part], list_l, 1, j0 + c0, j0 + c0 + 256)
                 for t0 in range(0, 4, 2):
                     acc = acc_pool.tile([P, 2, 256], F32, name="acc", tag="bank%d" % (c0 // P + t0 // 2))
@@ -183,10 +177,11 @@ def tile_list_record_match_scores_kernel(
                                 start=(a == 0),
                                 stop=(a == PASSES - 1),
                             )
-                    nc.scalar.activation(tanh_a[:, t0 : t0 + 2, :], acc[:], ACT.Tanh)
-                    nc.gpsimd.tensor_tensor(
-                        agree[-1][:, t0 : t0 + 2, :], tanh_a[:, t0 : t0 + 2, :], gated_b[:, t0 : t0 + 2, part], ALU.mult
-                    )
+                    nc.scalar.activation(tanh_a[:, t0 : t0 + 2, part], acc[:], ACT.Tanh)
+            for t in range(4):
+                nc.vector.scalar_tensor_tensor(
+                    agree[half][:, t, :], tanh_a[:, t, :], gain[t][:], tanh_b[:, t, :], ALU.mult, ALU.mult
+                )
 
         wk_w = held([P, PASSES, 4, P], I32, "wk_w")
         wk_sc = held([P, 4, P], U8, "wk_sc")
@@ -195,8 +190,8 @@ def tile_list_record_match_scores_kernel(
             wk_raw[:].rearrange("p a (u t e) -> p a t u e", t=4, e=4),
         )
         nc.vector.tensor_copy(wk_sc[:].bitcast(I32), wk_sc_raw[:].rearrange("p (u t) -> p t u", t=4))
-        wo_bf = held([P, 4 * N], BF16, "wo_bf", "tanh_b0")
-        wo_w = held([P, N], U32, "wo_w")
+        wo_bf = held([P, 4 * N], BF16, "wo_bf", "right_w01")
+        wo_w = held([P, N], U32, "wo_w", "wl_bf10")
         wo_sc = held([P, N], U8, "wo_sc")
         nc.scalar.copy(
             wo_bf[:].rearrange("p (c i t) -> p c t i", i=4, t=4),
@@ -219,8 +214,9 @@ def tile_list_record_match_scores_kernel(
         h_sc = held([P, S], U8, "h_sc")
         out_v = out.rearrange("(m p) j -> p m j", p=P)
 
-        def subtract_key(j0):
-            cols = slice(j0, j0 + P)
+        key_sum = {}
+
+        def key_product(j0):
             half, c0 = divmod(j0, HALF)
             acc = acc_pool.tile([P, 4, P], F32, name="acc", tag="bank%d" % ((j0 // P + 4) % 6))
             for t in range(4):
@@ -230,21 +226,28 @@ def tile_list_record_match_scores_kernel(
                         lhsT=wk_w[:, a, t, :].bitcast(FP8X4),
                         lhsT_scale=wk_sc[4 * a : P, t, :],
                         rhs=key_w[a, half][:, c0 : c0 + P].bitcast(FP8X4),
-                        rhs_scale=key_sc[4 * a : P, cols],
+                        rhs_scale=key_sc[4 * a : P, j0 : j0 + P],
                         start=(a == 0),
                         stop=(a == PASSES - 1),
                     )
+            key_sum[j0] = acc
+
+        def subtract_key(j0, j1):
+            half, c0 = divmod(j0, HALF)
+            b0 = j0 % P
+            if b0 == 0:
+                key_product(j0)
             nc.vector.tensor_tensor(
-                h_bf[:, 4 * j0 : 4 * (j0 + P)].rearrange("p (c i t) -> p c t i", i=2, t=4),
-                agree[j0 // 256][:, :, j0 % 256 : j0 % 256 + P].rearrange("p t (c i) -> p c t i", i=2),
-                acc[:].rearrange("p t (c i) -> p c t i", i=2),
+                h_bf[:, 4 * j0 : 4 * j1].rearrange("p (c i t) -> p c t i", i=2, t=4),
+                agree[half][:, :, c0 : c0 + j1 - j0].rearrange("p t (c i) -> p c t i", i=2),
+                key_sum[j0 - b0][:, :, b0 : b0 + j1 - j0].rearrange("p t (c i) -> p c t i", i=2),
                 ALU.subtract,
             )
 
-        def score(j0, j1):
+        def score(j0, j1, bank):
             cols = slice(j0, j1)
             nc.vector.quantize_mx(out=h_w[:, cols].bitcast(FP8X4), scales=h_sc[:, cols], in_=h_bf[:, 4 * j0 : 4 * j1])
-            acc = out_pool.tile([P, 2, j1 - j0], F32, name="scores")
+            acc = acc_pool.tile([P, 2, j1 - j0], F32, name="scores", tag="bank%d" % bank)
             for m in range(2):
                 nc.tensor.matmul_mx(
                     out=acc[:, m, :],
@@ -259,12 +262,17 @@ def tile_list_record_match_scores_kernel(
             nc.scalar.copy(res[:], acc[:])
             nc.sync.dma_start(out_v[:, :, cols], res[:])
 
-        edges = [0, 256, 512, 768, 896, 1024]
-        done = 0
-        for j0 in range(0, S, P):
-            subtract_key(j0)
-            if edges[done + 1] <= j0:
-                score(edges[done], edges[done + 1])
-                done += 1
-        for i in range(done, len(edges) - 1):
-            score(edges[i], edges[i + 1])
+        for j0 in (0, 128, 256):
+            subtract_key(j0, j0 + P)
+        score(0, 256, 6)
+        for j0 in (384, 512):
+            subtract_key(j0, j0 + P)
+        score(256, 512, 7)
+        for j0 in (640, 768):
+            subtract_key(j0, j0 + P)
+        score(512, 768, 0)
+        subtract_key(896, 960)
+        score(768, 896, 1)
+        subtract_key(960, 1024)
+        score(896, 960, 2)
+        score(960, 1024, 3)

@@ -56,10 +56,11 @@ def tile_list_record_match_scores_kernel(
             nc.sync.dma_start(tab_w[a][:], tab_words[a].rearrange("p t i -> p (t i)").bitcast(I32))
 
         nc.sync.dma_start(list_r[:], offs2)
+        nc.sync.dma_start(wr_raw[:], wr_words.bitcast(I32).rearrange("a p w -> p a w"))
+        nc.sync.dma_start(list_l[:], offs)
         for q in range(4):
             nc.sync.dma_start(tab_sc[32 * q : 32 * q + 8, :], tab_scales[:, 4 * q : 4 * q + 4, :].bitcast(I32))
         load_table(0)
-        nc.sync.dma_start(list_l[:], offs)
         for q in range(4):
             nc.sync.dma_start(
                 wr_sc_raw[32 * q : 32 * q + 4, :, :],
@@ -78,14 +79,13 @@ def tile_list_record_match_scores_kernel(
 
         for a in range(PASSES):
             nc.sync.dma_start(wl_raw[a][:], wl[512 * a : 512 * (a + 1), :].rearrange("(p j) r -> p j r", j=4))
-        nc.sync.dma_start(wr_raw[:], wr_words.bitcast(I32).rearrange("a p w -> p a w"))
         load_table(1)
         for q in range(4):
             nc.sync.dma_start(right_sc1[32 * q : 32 * q + 4, :], right_sc[32 * q + 4 : 32 * q + 8, :].bitcast(I32))
+        nc.sync.dma_start(wk_raw[:], wk_words.rearrange("a p r i -> p a (r i)").bitcast(I32))
         with nc.allow_non_contiguous_dma(reason="one gain to a partition"):
             for t in range(4):
                 nc.sync.dma_start(gain[t][:], g.rearrange("(u t e) -> t u e", t=4, e=4)[t])
-        nc.sync.dma_start(wk_raw[:], wk_words.rearrange("a p r i -> p a (r i)").bitcast(I32))
         nc.sync.dma_start(list_k[:], offs3)
         for q in range(4):
             nc.sync.dma_start(wk_sc_raw[32 * q : 32 * q + 8, :], wk_scales[:, 4 * q : 4 * q + 4, :].bitcast(I32))
@@ -260,7 +260,7 @@ def tile_list_record_match_scores_kernel(
                 )
             res = res_pool.tile([P, 2, j1 - j0], F32, name="res")
             nc.scalar.copy(res[:], acc[:])
-            nc.sync.dma_start(out_v[:, :, cols], res[:])
+            (nc.scalar if j1 == S else nc.sync).dma_start(out_v[:, :, cols], res[:])
 
         for j0 in (0, 128, 256):
             subtract_key(j0, j0 + P)

@@ -33,17 +33,23 @@ def tile_list_record_match_scores_kernel(
         def held(shape, dtype, name, slot=None):
             return keep.tile(shape, dtype, name=name, tag=slot or name, align_bytes=64)
 
+        banks_used = []
+
+        def bank(shape):
+            banks_used.append(0)
+            return acc_pool.tile(shape, F32, name="acc", tag="bank%d" % ((len(banks_used) - 1) % 8))
+
         list_l = keep.tile([P, S // 16], U16, name="list_l")
         list_r = keep.tile([P, S // 16], U16, name="list_r")
         list_k = keep.tile([P, S // 16], U16, name="list_k")
         tab_sc = held([P, T // 4], I32, "tab_sc")
         tab_w = [held([P, T], I32, "tab_w%d" % a) for a in range(PASSES)]
+        wk_raw = held([P, PASSES, H], I32, "wk_raw")
+        wo_raw = held([P, 4, N], F32, "wo_raw")
         wr_raw = held([P, PASSES, H // 2], I32, "wr_raw")
         wr_sc_raw = held([P, PASSES, H // 4], I32, "wr_sc_raw")
-        wk_raw = held([P, PASSES, H], I32, "wk_raw")
         wk_sc_raw = held([P, H // 4], I32, "wk_sc_raw")
         wl_raw = [held([P, 4, H], F32, "wl_raw%d" % a) for a in range(PASSES)]
-        wo_raw = held([P, 4, N], F32, "wo_raw")
         gain = [held([P, 1], F32, "gain%d" % t) for t in range(4)]
         right_sc1 = held([P, S // 4], I32, "right_sc1")
 
@@ -55,199 +61,144 @@ def tile_list_record_match_scores_kernel(
         def load_table(a):
             nc.sync.dma_start(tab_w[a][:], tab_words[a].rearrange("p t i -> p (t i)").bitcast(I32))
 
-        nc.sync.dma_start(list_r[:], offs2)
-        nc.sync.dma_start(wr_raw[:], wr_words.bitcast(I32).rearrange("a p w -> p a w"))
+        def load_wl(a):
+            nc.sync.dma_start(wl_raw[a][:], wl[512 * a : 512 * (a + 1), :].rearrange("(p j) r -> p j r", j=4))
+
         nc.sync.dma_start(list_l[:], offs)
         for q in range(4):
             nc.sync.dma_start(tab_sc[32 * q : 32 * q + 8, :], tab_scales[:, 4 * q : 4 * q + 4, :].bitcast(I32))
+        nc.sync.dma_start(list_r[:], offs2)
+        nc.sync.dma_start(list_k[:], offs3)
+        load_wl(0)
+        load_wl(1)
         load_table(0)
+        load_table(1)
+        nc.sync.dma_start(wr_raw[:], wr_words.bitcast(I32).rearrange("a p w -> p a w"))
         for q in range(4):
             nc.sync.dma_start(
                 wr_sc_raw[32 * q : 32 * q + 4, :, :],
                 wr_scales[:, 4 * q : 4 * q + 4, :].bitcast(I32).rearrange("a r w -> r a w"),
             )
 
-        def gather_scales(dst, lst, j0, j1):
-            nc.vector.tensor_copy(dst, tab_sc[:].bitcast(U8).indirect(lst[:, j0 // 16 : j1 // 16]))
+        def gather_scales(name, lst):
+            dst = held([P, S], U8, name)
+            nc.vector.tensor_copy(dst[:], tab_sc[:].bitcast(U8).indirect(lst[:]))
+            return dst
 
-        def gather_words(dst, lst, a, j0, j1):
-            nc.vector.tensor_copy(dst, tab_w[a][:].bitcast(U32).indirect(lst[:, j0 // 16 : j1 // 16]))
+        def gather_words(name, lst, a, j0, j1, slot=None):
+            dst = held([P, j1 - j0], U32, name, slot)
+            nc.vector.tensor_copy(dst[:], tab_w[a][:].bitcast(U32).indirect(lst[:, j0 // 16 : j1 // 16]))
+            return dst
 
-        right_sc = held([P, S], U8, "right_sc")
-        gather_scales(right_sc[:], list_r, 0, S)
+        left_sc = gather_scales("left_sc", list_l)
+        right_sc = gather_scales("right_sc", list_r)
+        key_sc = gather_scales("key_sc", list_k)
         right_planes = [right_sc[:], right_sc1[:].bitcast(U8)]
-
-        for a in range(PASSES):
-            nc.sync.dma_start(wl_raw[a][:], wl[512 * a : 512 * (a + 1), :].rearrange("(p j) r -> p j r", j=4))
-        load_table(1)
-        for q in range(4):
-            nc.sync.dma_start(right_sc1[32 * q : 32 * q + 4, :], right_sc[32 * q + 4 : 32 * q + 8, :].bitcast(I32))
+        nc.sync.dma_start(right_sc1[0:100, :], right_sc[4:104, :].bitcast(I32))
         nc.sync.dma_start(wk_raw[:], wk_words.rearrange("a p r i -> p a (r i)").bitcast(I32))
-        with nc.allow_non_contiguous_dma(reason="one gain to a partition"):
-            for t in range(4):
-                nc.sync.dma_start(gain[t][:], g.rearrange("(u t e) -> t u e", t=4, e=4)[t])
-        nc.sync.dma_start(list_k[:], offs3)
         for q in range(4):
             nc.sync.dma_start(wk_sc_raw[32 * q : 32 * q + 8, :], wk_scales[:, 4 * q : 4 * q + 4, :].bitcast(I32))
         for t in range(4):
             nc.sync.dma_start(wo_raw[:, t, :], wo.rearrange("(u t e) n -> t u e n", t=4, e=4)[t])
-
-        left_w, right_w, key_w, left_sc = {}, {}, {}, {}
-        for half in range(2):
-            right_w[0, half] = held([P, HALF], U32, "right_w0%d" % half)
-            gather_words(right_w[0, half][:], list_r, 0, half * HALF, (half + 1) * HALF)
-        for half in range(2):
-            left_w[0, half] = held([P, HALF], U32, "left_w0%d" % half)
-            gather_words(left_w[0, half][:], list_l, 0, half * HALF, (half + 1) * HALF)
+        with nc.allow_non_contiguous_dma(reason="one gain to a partition"):
+            for t in range(4):
+                nc.sync.dma_start(gain[t][:], g.rearrange("(u t e) -> t u e", t=4, e=4)[t])
 
         wl_w = held([P, PASSES, H], U32, "wl_w")
         wl_sc = held([P, PASSES, H], U8, "wl_sc")
-        wl_bf = {}
-        for a in range(PASSES):
-            for t0 in range(0, 4, 2):
-                wl_bf[a, t0] = held([P, 2, 4 * P], BF16, "wl_bf%d%d" % (a, t0))
-                for t in range(t0, t0 + 2):
-                    nc.scalar.copy(
-                        wl_bf[a, t0][:, t - t0, :].rearrange("p (u e j) -> p u j e", e=4, j=4),
-                        wl_raw[a][:].rearrange("p j (u t e) -> p t u j e", t=4, e=4)[:, t],
-                    )
+
+        wl_bf = [held([P, 4, 4 * P], BF16, "wl_bf%d" % a) for a in range(PASSES)]
+
+        def round_wl(a):
+            for t in range(4):
+                nc.scalar.copy(
+                    wl_bf[a][:, t, :].rearrange("p (u e j) -> p u j e", e=4, j=4),
+                    wl_raw[a][:].rearrange("p j (u t e) -> p t u j e", t=4, e=4)[:, t],
+                )
 
         def quantize_wl(a):
-            for t0 in range(0, 4, 2):
-                cols = slice(t0 * P, (t0 + 2) * P)
-                nc.vector.quantize_mx(
-                    out=wl_w[:, a, cols].bitcast(FP8X4),
-                    scales=wl_sc[:, a, cols],
-                    in_=wl_bf[a, t0][:].rearrange("p t x -> p (t x)"),
+            nc.vector.quantize_mx(
+                out=wl_w[:, a, :].bitcast(FP8X4), scales=wl_sc[:, a, :], in_=wl_bf[a][:].rearrange("p t x -> p (t x)")
+            )
+
+        def product(acc, weight, weight_sc, words, planes):
+            for a in range(PASSES):
+                nc.tensor.matmul_mx(
+                    out=acc,
+                    lhsT=weight[a],
+                    lhsT_scale=weight_sc[a],
+                    rhs=words[a].bitcast(FP8X4),
+                    rhs_scale=planes[a],
+                    start=(a == 0),
+                    stop=(a == PASSES - 1),
                 )
 
-        left_sc[0] = held([P, HALF], U8, "left_sc0")
-        gather_scales(left_sc[0][:], list_l, 0, HALF)
-        quantize_wl(0)
         wr_w = held([P, PASSES, 4, 2 * P], U8, "wr_w")
         wr_sc = held([P, PASSES, 4, P], U8, "wr_sc")
-        nc.vector.tensor_copy(
-            wr_w[:].bitcast(I32).rearrange("p a t (u w) -> p a t u w", w=2),
-            wr_raw[:].rearrange("p a (u t w) -> p a t u w", t=4, w=2),
-        )
-        nc.vector.tensor_copy(wr_sc[:].bitcast(I32), wr_sc_raw[:].rearrange("p a (u t) -> p a t u", t=4))
-
-        agree = []
-        for half in range(2):
-            j0 = half * HALF
-            cols = slice(j0, j0 + HALF)
-            right_w[1, half] = held([P, HALF], U32, "right_w1%d" % half, "wl_bf12" if half else None)
-            gather_words(right_w[1, half][:], list_r, 1, j0, j0 + HALF)
-            tanh_b = held([P, 4, HALF], F32, "tanh_b%d" % half)
-            tanh_a = held([P, 4, HALF], F32, "tanh_a%d" % half)
-            agree.append(held([P, 4, HALF], F32, "agree%d" % half))
-            for t in range(4):
-                acc = acc_pool.tile([P, HALF], F32, name="acc", tag="bank%d" % t)
-                for a in range(PASSES):
-                    nc.tensor.matmul_mx(
-                        out=acc[:],
-                        lhsT=wr_w[:, a, t, :].bitcast(FP4X4),
-                        lhsT_scale=wr_sc[:, a, t, :],
-                        rhs=right_w[a, half][:].bitcast(FP8X4),
-                        rhs_scale=right_planes[a][:, cols],
-                        start=(a == 0),
-                        stop=(a == PASSES - 1),
-                    )
-                nc.scalar.activation(tanh_b[:, t, :], acc[:], ACT.Tanh)
-
-            if half == 0:
-                quantize_wl(1)
-            else:
-                left_sc[1] = held([P, HALF], U8, "left_sc1", "wr_raw")
-                gather_scales(left_sc[1][:], list_l, j0, j0 + HALF)
-            left_w[1, half] = held([P, HALF], U32, "left_w1%d" % half, "wl_bf10" if half else None)
-            for c0 in range(0, HALF, 256):
-                part = slice(c0, c0 + 256)
-                gather_words(left_w[1, half][:, part], list_l, 1, j0 + c0, j0 + c0 + 256)
-                for t0 in range(0, 4, 2):
-                    acc = acc_pool.tile([P, 2, 256], F32, name="acc", tag="bank%d" % (c0 // P + t0 // 2))
-                    for t in range(t0, t0 + 2):
-                        for a in range(PASSES):
-                            nc.tensor.matmul_mx(
-                                out=acc[:, t - t0, :],
-                                lhsT=wl_w[:, a, t * P : (t + 1) * P].bitcast(FP8X4),
-                                lhsT_scale=wl_sc[:, a, t * P : (t + 1) * P],
-                                rhs=left_w[a, half][:, part].bitcast(FP8X4),
-                                rhs_scale=left_sc[half][4 * a : P, part],
-                                start=(a == 0),
-                                stop=(a == PASSES - 1),
-                            )
-                    nc.scalar.activation(tanh_a[:, t0 : t0 + 2, part], acc[:], ACT.Tanh)
-            for t in range(4):
-                nc.vector.scalar_tensor_tensor(
-                    agree[half][:, t, :], tanh_a[:, t, :], gain[t][:], tanh_b[:, t, :], ALU.mult, ALU.mult
-                )
-
         wk_w = held([P, PASSES, 4, P], I32, "wk_w")
         wk_sc = held([P, 4, P], U8, "wk_sc")
-        nc.vector.tensor_copy(
-            wk_w[:].rearrange("p a t (u e) -> p a t u e", e=4),
-            wk_raw[:].rearrange("p a (u t e) -> p a t u e", t=4, e=4),
-        )
-        nc.vector.tensor_copy(wk_sc[:].bitcast(I32), wk_sc_raw[:].rearrange("p (u t) -> p t u", t=4))
-        wo_bf = held([P, 4 * N], BF16, "wo_bf", "right_w01")
-        wo_w = held([P, N], U32, "wo_w", "wl_bf10")
-        wo_sc = held([P, N], U8, "wo_sc")
-        nc.scalar.copy(
-            wo_bf[:].rearrange("p (c i t) -> p c t i", i=4, t=4),
-            wo_raw[:].rearrange("p t (c i) -> p c t i", i=4),
-        )
-        nc.vector.quantize_mx(out=wo_w[:].bitcast(FP8X4), scales=wo_sc[:], in_=wo_bf[:])
+        tanh_b, tanh_a, agree = {}, {}, {}
 
-        key_sc = held([P, S], U8, "key_sc", "left_sc0")
-        gather_scales(key_sc[:], list_k, 0, S)
-        for half in range(2):
-            j0 = half * HALF
-            for a in range(PASSES):
-                key_w[a, half] = held([P, HALF], U32, "key_w%d%d" % (a, half), "%s_w%d0" % (("right", "left")[half], a))
-            gather_words(key_w[0, half][:], list_k, 0, j0, j0 + HALF)
-            for c0 in range(0, HALF, 256):
-                gather_words(key_w[1, half][:, c0 : c0 + 256], list_k, 1, j0 + c0, j0 + c0 + 256)
+        def right_product(half, words):
+            cols = slice(half * HALF, (half + 1) * HALF)
+            for t in range(4):
+                acc = bank([P, HALF])
+                product(
+                    acc[:],
+                    [wr_w[:, a, t, :].bitcast(FP4X4) for a in range(PASSES)],
+                    [wr_sc[:, a, t, :] for a in range(PASSES)],
+                    words,
+                    [plane[:, cols] for plane in right_planes],
+                )
+                tanh_b[half, t] = held([P, HALF], F32, "tanh_b%d%d" % (half, t))
+                nc.scalar.activation(tanh_b[half, t][:], acc[:], ACT.Tanh)
 
-        h_bf = held([P, 4 * S], BF16, "h_bf")
+        def left_product(j0, width, words):
+            per_bank = 512 // width
+            for t0 in range(0, 4, per_bank):
+                acc = bank([P, per_bank, width])
+                for t in range(t0, t0 + per_bank):
+                    product(
+                        acc[:, t - t0, :],
+                        [wl_w[:, a, t * P : (t + 1) * P].bitcast(FP8X4) for a in range(PASSES)],
+                        [wl_sc[:, a, t * P : (t + 1) * P] for a in range(PASSES)],
+                        words,
+                        [left_sc[4 * a : P, j0 : j0 + width] for a in range(PASSES)],
+                    )
+                tile = held([P, per_bank, width], F32, "tanh_a%d_%d" % (j0, t0))
+                nc.scalar.activation(tile[:], acc[:], ACT.Tanh)
+                for t in range(t0, t0 + per_bank):
+                    tanh_a[j0, t] = tile[:, t - t0, :]
+
+        def agreement(j0, width):
+            half, c0 = divmod(j0, HALF)
+            agree[j0] = held([P, 4, width], F32, "agree%d" % j0)
+            for t in range(4):
+                nc.vector.scalar_tensor_tensor(
+                    agree[j0][:, t, :], tanh_a[j0, t], gain[t][:], tanh_b[half, t][:, c0 : c0 + width], ALU.mult, ALU.mult
+                )
+
+        def key_product(acc, t, words, j0, width):
+            product(
+                acc,
+                [wk_w[:, a, t, :].bitcast(FP8X4) for a in range(PASSES)],
+                [wk_sc[4 * a : P, t, :] for a in range(PASSES)],
+                words,
+                [key_sc[4 * a : P, j0 : j0 + width] for a in range(PASSES)],
+            )
+
+        h_bf = [held([P, 4 * 256], BF16, "h_bf%d" % q) for q in range(4)]
         h_w = held([P, S], U32, "h_w")
         h_sc = held([P, S], U8, "h_sc")
         out_v = out.rearrange("(m p) j -> p m j", p=P)
 
-        key_sum = {}
-
-        def key_product(j0):
-            half, c0 = divmod(j0, HALF)
-            acc = acc_pool.tile([P, 4, P], F32, name="acc", tag="bank%d" % ((j0 // P + 4) % 6))
-            for t in range(4):
-                for a in range(PASSES):
-                    nc.tensor.matmul_mx(
-                        out=acc[:, t, :],
-                        lhsT=wk_w[:, a, t, :].bitcast(FP8X4),
-                        lhsT_scale=wk_sc[4 * a : P, t, :],
-                        rhs=key_w[a, half][:, c0 : c0 + P].bitcast(FP8X4),
-                        rhs_scale=key_sc[4 * a : P, j0 : j0 + P],
-                        start=(a == 0),
-                        stop=(a == PASSES - 1),
-                    )
-            key_sum[j0] = acc
-
-        def subtract_key(j0, j1):
-            half, c0 = divmod(j0, HALF)
-            b0 = j0 % P
-            if b0 == 0:
-                key_product(j0)
-            nc.vector.tensor_tensor(
-                h_bf[:, 4 * j0 : 4 * j1].rearrange("p (c i t) -> p c t i", i=2, t=4),
-                agree[half][:, :, c0 : c0 + j1 - j0].rearrange("p t (c i) -> p c t i", i=2),
-                key_sum[j0 - b0][:, :, b0 : b0 + j1 - j0].rearrange("p t (c i) -> p c t i", i=2),
-                ALU.subtract,
-            )
-
-        def score(j0, j1, bank):
+        def score(j0, j1):
             cols = slice(j0, j1)
-            nc.vector.quantize_mx(out=h_w[:, cols].bitcast(FP8X4), scales=h_sc[:, cols], in_=h_bf[:, 4 * j0 : 4 * j1])
-            acc = acc_pool.tile([P, 2, j1 - j0], F32, name="scores", tag="bank%d" % bank)
+            q, c0 = divmod(j0, 256)
+            nc.vector.quantize_mx(
+                out=h_w[:, cols].bitcast(FP8X4), scales=h_sc[:, cols], in_=h_bf[q][:, 4 * c0 : 4 * (c0 + j1 - j0)]
+            )
+            acc = bank([P, 2, j1 - j0])
             for m in range(2):
                 nc.tensor.matmul_mx(
                     out=acc[:, m, :],
@@ -262,17 +213,65 @@ def tile_list_record_match_scores_kernel(
             nc.scalar.copy(res[:], acc[:])
             (nc.scalar if j1 == S else nc.sync).dma_start(out_v[:, :, cols], res[:])
 
+        key_sum = {}
+
+        def subtract_key(j0, j1, words):
+            b0 = j0 % P
+            if b0 == 0:
+                key_sum[j0] = bank([P, 4, P])
+                for t in range(4):
+                    key_product(key_sum[j0][:, t, :], t, [w[:, j0 : j0 + P] for w in words], j0, P)
+            q, c0 = divmod(j0, 256)
+            half, d0 = divmod(j0, HALF)
+            nc.vector.tensor_tensor(
+                h_bf[q][:, 4 * c0 : 4 * (c0 + j1 - j0)].rearrange("p (c i t) -> p c t i", i=2, t=4),
+                agree[half * HALF][:, :, d0 : d0 + j1 - j0].rearrange("p t (c i) -> p c t i", i=2),
+                key_sum[j0 - b0][:, :, b0 : b0 + j1 - j0].rearrange("p t (c i) -> p c t i", i=2),
+                ALU.subtract,
+            )
+
+        for a in range(PASSES):
+            round_wl(a)
+            quantize_wl(a)
+        left0 = gather_words("left0", list_l, 0, 0, S)
+        right0 = gather_words("right0", list_r, 0, 0, S)
+        nc.vector.tensor_copy(
+            wr_w[:].bitcast(I32).rearrange("p a t (u w) -> p a t u w", w=2),
+            wr_raw[:].rearrange("p a (u t w) -> p a t u w", t=4, w=2),
+        )
+        nc.vector.tensor_copy(wr_sc[:].bitcast(I32), wr_sc_raw[:].rearrange("p a (u t) -> p a t u", t=4))
+        for j0 in (0, HALF):
+            left1 = gather_words("left1_%d" % j0, list_l, 1, j0, j0 + HALF)
+            left_product(j0, HALF, [left0[:, j0 : j0 + HALF], left1[:]])
+            right1 = gather_words("right1_%d" % j0, list_r, 1, j0, j0 + HALF)
+            right_product(j0 // HALF, [right0[:, j0 : j0 + HALF], right1[:]])
+        key = [gather_words("key%d" % a, list_k, a, 0, S, ("wr_raw", "wr_sc_raw")[a]) for a in range(PASSES)]
+        nc.vector.tensor_copy(
+            wk_w[:].rearrange("p a t (u e) -> p a t u e", e=4),
+            wk_raw[:].rearrange("p a (u t e) -> p a t u e", t=4, e=4),
+        )
+        nc.vector.tensor_copy(wk_sc[:].bitcast(I32), wk_sc_raw[:].rearrange("p (u t) -> p t u", t=4))
+        wo_bf = held([P, 4 * N], BF16, "wo_bf")
+        wo_w = held([P, N], U32, "wo_w")
+        wo_sc = held([P, N], U8, "wo_sc")
+        nc.scalar.copy(
+            wo_bf[:].rearrange("p (c i t) -> p c t i", i=4, t=4),
+            wo_raw[:].rearrange("p t (c i) -> p c t i", i=4),
+        )
+        agreement(0, HALF)
+        nc.vector.quantize_mx(out=wo_w[:].bitcast(FP8X4), scales=wo_sc[:], in_=wo_bf[:])
+        agreement(HALF, HALF)
         for j0 in (0, 128, 256):
-            subtract_key(j0, j0 + P)
-        score(0, 256, 6)
+            subtract_key(j0, j0 + P, key)
+        score(0, 256)
         for j0 in (384, 512):
-            subtract_key(j0, j0 + P)
-        score(256, 512, 7)
+            subtract_key(j0, j0 + P, key)
+        score(256, 512)
         for j0 in (640, 768):
-            subtract_key(j0, j0 + P)
-        score(512, 768, 0)
-        subtract_key(896, 960)
-        score(768, 896, 1)
-        subtract_key(960, 1024)
-        score(896, 960, 2)
-        score(960, 1024, 3)
+            subtract_key(j0, j0 + P, key)
+        score(512, 768)
+        subtract_key(896, 960, key)
+        score(768, 896)
+        subtract_key(960, 1024, key)
+        score(896, 960)
+        score(960, 1024)

@@ -19,6 +19,8 @@ ACT = mybir.ActivationFunctionType
 P = 128
 PASSES = K // 512
 HALF = S // 2
+QUARTER = S // 4
+POOL_COLS = 384
 
 
 def tile_list_record_match_scores_kernel(
@@ -33,11 +35,8 @@ def tile_list_record_match_scores_kernel(
         def held(shape, dtype, name, slot=None):
             return keep.tile(shape, dtype, name=name, tag=slot or name, align_bytes=64)
 
-        banks_used = []
-
-        def bank(shape):
-            banks_used.append(0)
-            return acc_pool.tile(shape, F32, name="acc", tag="bank%d" % ((len(banks_used) - 1) % 8))
+        def bank(shape, number):
+            return acc_pool.tile(shape, F32, name="acc", tag="bank%d" % number)
 
         list_l = keep.tile([P, S // 16], U16, name="list_l")
         list_r = keep.tile([P, S // 16], U16, name="list_r")
@@ -64,24 +63,24 @@ def tile_list_record_match_scores_kernel(
         def load_wl(a):
             nc.sync.dma_start(wl_raw[a][:], wl[512 * a : 512 * (a + 1), :].rearrange("(p j) r -> p j r", j=4))
 
+        nc.sync.dma_start(list_r[:], offs2)
+        nc.sync.dma_start(wr_raw[:], wr_words.bitcast(I32).rearrange("a p w -> p a w"))
         nc.sync.dma_start(list_l[:], offs)
         for q in range(4):
             nc.sync.dma_start(tab_sc[32 * q : 32 * q + 8, :], tab_scales[:, 4 * q : 4 * q + 4, :].bitcast(I32))
-        nc.sync.dma_start(list_r[:], offs2)
-        nc.sync.dma_start(list_k[:], offs3)
-        load_wl(0)
-        load_wl(1)
         load_table(0)
-        load_table(1)
-        nc.sync.dma_start(wr_raw[:], wr_words.bitcast(I32).rearrange("a p w -> p a w"))
         for q in range(4):
             nc.sync.dma_start(
                 wr_sc_raw[32 * q : 32 * q + 4, :, :],
                 wr_scales[:, 4 * q : 4 * q + 4, :].bitcast(I32).rearrange("a r w -> r a w"),
             )
+        load_wl(0)
+        load_wl(1)
+        load_table(1)
+        nc.sync.dma_start(list_k[:], offs3)
 
-        def gather_scales(name, lst):
-            dst = held([P, S], U8, name)
+        def gather_scales(name, lst, slot=None):
+            dst = held([P, S], U8, name, slot)
             nc.vector.tensor_copy(dst[:], tab_sc[:].bitcast(U8).indirect(lst[:]))
             return dst
 
@@ -90,16 +89,16 @@ def tile_list_record_match_scores_kernel(
             nc.vector.tensor_copy(dst[:], tab_w[a][:].bitcast(U32).indirect(lst[:, j0 // 16 : j1 // 16]))
             return dst
 
-        left_sc = gather_scales("left_sc", list_l)
         right_sc = gather_scales("right_sc", list_r)
-        key_sc = gather_scales("key_sc", list_k)
+        left_sc = gather_scales("left_sc", list_l)
         right_planes = [right_sc[:], right_sc1[:].bitcast(U8)]
-        nc.sync.dma_start(right_sc1[0:100, :], right_sc[4:104, :].bitcast(I32))
+        for q in range(4):
+            nc.sync.dma_start(right_sc1[32 * q : 32 * q + 4, :], right_sc[32 * q + 4 : 32 * q + 8, :].bitcast(I32))
+        for t in range(4):
+            nc.sync.dma_start(wo_raw[:, t, :], wo.rearrange("(u t e) n -> t u e n", t=4, e=4)[t])
         nc.sync.dma_start(wk_raw[:], wk_words.rearrange("a p r i -> p a (r i)").bitcast(I32))
         for q in range(4):
             nc.sync.dma_start(wk_sc_raw[32 * q : 32 * q + 8, :], wk_scales[:, 4 * q : 4 * q + 4, :].bitcast(I32))
-        for t in range(4):
-            nc.sync.dma_start(wo_raw[:, t, :], wo.rearrange("(u t e) n -> t u e n", t=4, e=4)[t])
         with nc.allow_non_contiguous_dma(reason="one gain to a partition"):
             for t in range(4):
                 nc.sync.dma_start(gain[t][:], g.rearrange("(u t e) -> t u e", t=4, e=4)[t])
@@ -135,14 +134,13 @@ def tile_list_record_match_scores_kernel(
 
         wr_w = held([P, PASSES, 4, 2 * P], U8, "wr_w")
         wr_sc = held([P, PASSES, 4, P], U8, "wr_sc")
-        wk_w = held([P, PASSES, 4, P], I32, "wk_w")
         wk_sc = held([P, 4, P], U8, "wk_sc")
-        tanh_b, tanh_a, agree = {}, {}, {}
+        tanh_b, tanh_a, agree, gained = {}, {}, {}, {}
 
         def right_product(half, words):
             cols = slice(half * HALF, (half + 1) * HALF)
             for t in range(4):
-                acc = bank([P, HALF])
+                acc = bank([P, HALF], t)
                 product(
                     acc[:],
                     [wr_w[:, a, t, :].bitcast(FP4X4) for a in range(PASSES)],
@@ -153,30 +151,50 @@ def tile_list_record_match_scores_kernel(
                 tanh_b[half, t] = held([P, HALF], F32, "tanh_b%d%d" % (half, t))
                 nc.scalar.activation(tanh_b[half, t][:], acc[:], ACT.Tanh)
 
-        def left_product(j0, width, words):
-            per_bank = 512 // width
-            for t0 in range(0, 4, per_bank):
-                acc = bank([P, per_bank, width])
-                for t in range(t0, t0 + per_bank):
+        def left_product(q, words):
+            cols = slice(q * QUARTER, (q + 1) * QUARTER)
+            for s in range(2):
+                acc = bank([P, 2, QUARTER], 2 * (q % 2) + s)
+                for t in range(2 * s, 2 * s + 2):
                     product(
-                        acc[:, t - t0, :],
+                        acc[:, t % 2, :],
                         [wl_w[:, a, t * P : (t + 1) * P].bitcast(FP8X4) for a in range(PASSES)],
                         [wl_sc[:, a, t * P : (t + 1) * P] for a in range(PASSES)],
                         words,
-                        [left_sc[4 * a : P, j0 : j0 + width] for a in range(PASSES)],
+                        [left_sc[4 * a : P, cols] for a in range(PASSES)],
                     )
-                tile = held([P, per_bank, width], F32, "tanh_a%d_%d" % (j0, t0))
-                nc.scalar.activation(tile[:], acc[:], ACT.Tanh)
-                for t in range(t0, t0 + per_bank):
-                    tanh_a[j0, t] = tile[:, t - t0, :]
+                tanh_a[q, s] = held([P, 2 * QUARTER], F32, "tanh_a%d%d" % (q, s))
+                nc.scalar.activation(tanh_a[q, s][:], acc[:].rearrange("p t c -> p (t c)"), ACT.Tanh)
 
-        def agreement(j0, width):
-            half, c0 = divmod(j0, HALF)
-            agree[j0] = held([P, 4, width], F32, "agree%d" % j0)
-            for t in range(4):
-                nc.vector.scalar_tensor_tensor(
-                    agree[j0][:, t, :], tanh_a[j0, t], gain[t][:], tanh_b[half, t][:, c0 : c0 + width], ALU.mult, ALU.mult
+        def apply_gain(q):
+            half, c0 = divmod(q * QUARTER, HALF)
+            gained[q] = held([P, POOL_COLS], F32, "gained%d" % q)
+            for t in range(2):
+                width = min(QUARTER, POOL_COLS - t * QUARTER)
+                nc.scalar.activation(
+                    gained[q][:, t * QUARTER : t * QUARTER + width],
+                    tanh_b[half, t][:, c0 : c0 + width],
+                    ACT.Copy,
+                    scale=gain[t][:],
                 )
+
+        def agreement(q, slot):
+            half, c0 = divmod(q * QUARTER, HALF)
+            agree[q] = held([P, 4 * QUARTER], F32, "agree%d" % q, slot)
+            first = POOL_COLS if q in gained else 0
+            if first:
+                nc.gpsimd.tensor_tensor(agree[q][:, :first], tanh_a[q, 0][:, :first], gained[q][:], ALU.mult)
+            for t in range(4):
+                skip = max(0, first - t * QUARTER)
+                if skip < QUARTER:
+                    nc.vector.scalar_tensor_tensor(
+                        agree[q][:, t * QUARTER + skip : (t + 1) * QUARTER],
+                        tanh_a[q, t // 2][:, t % 2 * QUARTER + skip : (t % 2 + 1) * QUARTER],
+                        gain[t][:],
+                        tanh_b[half, t][:, c0 + skip : c0 + QUARTER],
+                        ALU.mult,
+                        ALU.mult,
+                    )
 
         def key_product(acc, t, words, j0, width):
             product(
@@ -192,13 +210,13 @@ def tile_list_record_match_scores_kernel(
         h_sc = held([P, S], U8, "h_sc")
         out_v = out.rearrange("(m p) j -> p m j", p=P)
 
-        def score(j0, j1):
+        def score(j0, j1, number):
             cols = slice(j0, j1)
             q, c0 = divmod(j0, 256)
             nc.vector.quantize_mx(
                 out=h_w[:, cols].bitcast(FP8X4), scales=h_sc[:, cols], in_=h_bf[q][:, 4 * c0 : 4 * (c0 + j1 - j0)]
             )
-            acc = bank([P, 2, j1 - j0])
+            acc = bank([P, 2, j1 - j0], number)
             for m in range(2):
                 nc.tensor.matmul_mx(
                     out=acc[:, m, :],
@@ -218,60 +236,66 @@ def tile_list_record_match_scores_kernel(
         def subtract_key(j0, j1, words):
             b0 = j0 % P
             if b0 == 0:
-                key_sum[j0] = bank([P, 4, P])
+                key_sum[j0] = bank([P, 4, P], j0 // P % 4)
                 for t in range(4):
                     key_product(key_sum[j0][:, t, :], t, [w[:, j0 : j0 + P] for w in words], j0, P)
             q, c0 = divmod(j0, 256)
-            half, d0 = divmod(j0, HALF)
             nc.vector.tensor_tensor(
                 h_bf[q][:, 4 * c0 : 4 * (c0 + j1 - j0)].rearrange("p (c i t) -> p c t i", i=2, t=4),
-                agree[half * HALF][:, :, d0 : d0 + j1 - j0].rearrange("p t (c i) -> p c t i", i=2),
+                agree[q][:].rearrange("p (t c) -> p t c", t=4)[:, :, c0 : c0 + j1 - j0].rearrange("p t (c i) -> p c t i", i=2),
                 key_sum[j0 - b0][:, :, b0 : b0 + j1 - j0].rearrange("p t (c i) -> p c t i", i=2),
                 ALU.subtract,
             )
 
-        for a in range(PASSES):
-            round_wl(a)
-            quantize_wl(a)
-        left0 = gather_words("left0", list_l, 0, 0, S)
-        right0 = gather_words("right0", list_r, 0, 0, S)
         nc.vector.tensor_copy(
             wr_w[:].bitcast(I32).rearrange("p a t (u w) -> p a t u w", w=2),
             wr_raw[:].rearrange("p a (u t w) -> p a t u w", t=4, w=2),
         )
+        left0 = gather_words("left0", list_l, 0, 0, S)
+        right0 = gather_words("right0", list_r, 0, 0, S)
         nc.vector.tensor_copy(wr_sc[:].bitcast(I32), wr_sc_raw[:].rearrange("p a (u t) -> p a t u", t=4))
-        for j0 in (0, HALF):
-            left1 = gather_words("left1_%d" % j0, list_l, 1, j0, j0 + HALF)
-            left_product(j0, HALF, [left0[:, j0 : j0 + HALF], left1[:]])
-            right1 = gather_words("right1_%d" % j0, list_r, 1, j0, j0 + HALF)
-            right_product(j0 // HALF, [right0[:, j0 : j0 + HALF], right1[:]])
-        key = [gather_words("key%d" % a, list_k, a, 0, S, ("wr_raw", "wr_sc_raw")[a]) for a in range(PASSES)]
+        for a in range(PASSES):
+            round_wl(a)
+            quantize_wl(a)
+        wo_bf = held([P, 4 * N], BF16, "wo_bf")
+        wo_sc = held([P, N], U8, "wo_sc")
+        for half in range(2):
+            j0 = half * HALF
+            left1 = gather_words("left1_%d" % half, list_l, 1, j0, j0 + HALF, (None, "wl_bf1")[half])
+            for q in (2 * half, 2 * half + 1):
+                c0 = q * QUARTER - j0
+                left_product(q, [left0[:, j0 + c0 : j0 + c0 + QUARTER], left1[:, c0 : c0 + QUARTER]])
+            if half == 0:
+                right1 = gather_words("right1", list_r, 1, 0, S, "wl_raw1")
+            right_product(half, [right0[:, j0 : j0 + HALF], right1[:, j0 : j0 + HALF]])
+            for q in range(max(1, 2 * half), 2 * half + 2):
+                apply_gain(q)
+            if half == 0:
+                nc.scalar.copy(
+                    wo_bf[:].rearrange("p (c i t) -> p c t i", i=4, t=4),
+                    wo_raw[:].rearrange("p t (c i) -> p c t i", i=4),
+                )
+        key_sc = gather_scales("key_sc", list_k, "left1_0")
+        wk_w = held([P, PASSES, 4, P], I32, "wk_w", "left0")
         nc.vector.tensor_copy(
             wk_w[:].rearrange("p a t (u e) -> p a t u e", e=4),
             wk_raw[:].rearrange("p a (u t e) -> p a t u e", t=4, e=4),
         )
         nc.vector.tensor_copy(wk_sc[:].bitcast(I32), wk_sc_raw[:].rearrange("p (u t) -> p t u", t=4))
-        wo_bf = held([P, 4 * N], BF16, "wo_bf")
-        wo_w = held([P, N], U32, "wo_w")
-        wo_sc = held([P, N], U8, "wo_sc")
-        nc.scalar.copy(
-            wo_bf[:].rearrange("p (c i t) -> p c t i", i=4, t=4),
-            wo_raw[:].rearrange("p t (c i) -> p c t i", i=4),
-        )
-        agreement(0, HALF)
+        key = [held([P, S], U32, "key%d" % a, ("wo_raw", "wl_bf1")[a]) for a in range(PASSES)]
+        for a, j0, j1 in ((0, 0, S), (1, 0, QUARTER), (1, QUARTER, S)):
+            nc.vector.tensor_copy(key[a][:, j0:j1], tab_w[a][:].bitcast(U32).indirect(list_k[:, j0 // 16 : j1 // 16]))
+        agreement(0, "wl_raw1")
+        wo_w = held([P, N], U32, "wo_w", "tanh_a00")
         nc.vector.quantize_mx(out=wo_w[:].bitcast(FP8X4), scales=wo_sc[:], in_=wo_bf[:])
-        agreement(HALF, HALF)
-        for j0 in (0, 128, 256):
-            subtract_key(j0, j0 + P, key)
-        score(0, 256)
-        for j0 in (384, 512):
-            subtract_key(j0, j0 + P, key)
-        score(256, 512)
-        for j0 in (640, 768):
-            subtract_key(j0, j0 + P, key)
-        score(512, 768)
+        for q in range(3):
+            subtract_key(q * QUARTER, q * QUARTER + P, key)
+            subtract_key(q * QUARTER + P, (q + 1) * QUARTER, key)
+            agreement(q + 1, "tanh_a%d1" % q)
+            score(q * QUARTER, (q + 1) * QUARTER, 4 + q)
+        subtract_key(768, 896, key)
         subtract_key(896, 960, key)
-        score(768, 896)
+        score(768, 896, 7)
         subtract_key(960, 1024, key)
-        score(896, 960)
-        score(960, 1024)
+        score(896, 960, 4)
+        score(960, 1024, 5)

@@ -20,7 +20,7 @@ P = 128
 PASSES = K // 512
 HALF = S // 2
 QUARTER = S // 4
-POOL_COLS = 384
+POOL_COLS = {2: 896, 3: 384}
 
 
 def tile_list_record_match_scores_kernel(
@@ -151,47 +151,51 @@ def tile_list_record_match_scores_kernel(
                 tanh_b[half, t] = held([P, HALF], F32, "tanh_b%d%d" % (half, t))
                 nc.scalar.activation(tanh_b[half, t][:], acc[:], ACT.Tanh)
 
-        def left_product(q, words):
-            cols = slice(q * QUARTER, (q + 1) * QUARTER)
-            for s in range(2):
-                acc = bank([P, 2, QUARTER], 2 * (q % 2) + s)
-                for t in range(2 * s, 2 * s + 2):
+        def left_product(j0, width, words):
+            tanh_a[j0] = held([P, 4 * width], F32, "tanh_a%d" % j0)
+            per_bank = HALF // width
+            for t0 in range(0, 4, per_bank):
+                acc = bank([P, per_bank, width], (4 * j0 + t0 * width) // HALF % 4)
+                for t in range(t0, t0 + per_bank):
                     product(
-                        acc[:, t % 2, :],
+                        acc[:, t - t0, :],
                         [wl_w[:, a, t * P : (t + 1) * P].bitcast(FP8X4) for a in range(PASSES)],
                         [wl_sc[:, a, t * P : (t + 1) * P] for a in range(PASSES)],
                         words,
-                        [left_sc[4 * a : P, cols] for a in range(PASSES)],
+                        [left_sc[4 * a : P, j0 : j0 + width] for a in range(PASSES)],
                     )
-                tanh_a[q, s] = held([P, 2 * QUARTER], F32, "tanh_a%d%d" % (q, s))
-                nc.scalar.activation(tanh_a[q, s][:], acc[:].rearrange("p t c -> p (t c)"), ACT.Tanh)
-
-        def apply_gain(q):
-            half, c0 = divmod(q * QUARTER, HALF)
-            gained[q] = held([P, POOL_COLS], F32, "gained%d" % q)
-            for t in range(2):
-                width = min(QUARTER, POOL_COLS - t * QUARTER)
                 nc.scalar.activation(
-                    gained[q][:, t * QUARTER : t * QUARTER + width],
-                    tanh_b[half, t][:, c0 : c0 + width],
-                    ACT.Copy,
-                    scale=gain[t][:],
+                    tanh_a[j0][:, t0 * width : t0 * width + HALF], acc[:].rearrange("p t c -> p (t c)"), ACT.Tanh
                 )
 
-        def agreement(q, slot):
-            half, c0 = divmod(q * QUARTER, HALF)
-            agree[q] = held([P, 4 * QUARTER], F32, "agree%d" % q, slot)
-            first = POOL_COLS if q in gained else 0
-            if first:
-                nc.gpsimd.tensor_tensor(agree[q][:, :first], tanh_a[q, 0][:, :first], gained[q][:], ALU.mult)
+        def apply_gain(q):
+            c0 = q * QUARTER - HALF
+            gained[q] = held([P, POOL_COLS[q]], F32, "gained%d" % q)
             for t in range(4):
-                skip = max(0, first - t * QUARTER)
-                if skip < QUARTER:
+                width = min(QUARTER, POOL_COLS[q] - t * QUARTER)
+                if width > 0:
+                    nc.scalar.activation(
+                        gained[q][:, t * QUARTER : t * QUARTER + width],
+                        tanh_b[1, t][:, c0 : c0 + width],
+                        ACT.Copy,
+                        scale=gain[t][:],
+                    )
+
+        def agreement(j0, width, slot):
+            half, c0 = divmod(j0, HALF)
+            agree[j0] = held([P, 4 * width], F32, "agree%d" % j0, slot)
+            first = POOL_COLS.get(j0 // QUARTER, 0)
+            if first:
+                nc.gpsimd.tensor_tensor(agree[j0][:, :first], tanh_a[j0][:, :first], gained[j0 // QUARTER][:], ALU.mult)
+            for t in range(4):
+                skip = max(0, first - t * width)
+                if skip < width:
+                    cols = slice(t * width + skip, (t + 1) * width)
                     nc.vector.scalar_tensor_tensor(
-                        agree[q][:, t * QUARTER + skip : (t + 1) * QUARTER],
-                        tanh_a[q, t // 2][:, t % 2 * QUARTER + skip : (t % 2 + 1) * QUARTER],
+                        agree[j0][:, cols],
+                        tanh_a[j0][:, cols],
                         gain[t][:],
-                        tanh_b[half, t][:, c0 + skip : c0 + QUARTER],
+                        tanh_b[half, t][:, c0 + skip : c0 + width],
                         ALU.mult,
                         ALU.mult,
                     )
@@ -205,17 +209,17 @@ def tile_list_record_match_scores_kernel(
                 [key_sc[4 * a : P, j0 : j0 + width] for a in range(PASSES)],
             )
 
-        h_bf = [held([P, 4 * 256], BF16, "h_bf%d" % q) for q in range(4)]
+        h_bf = held([P, 4 * S], BF16, "h_bf")
         h_w = held([P, S], U32, "h_w")
         h_sc = held([P, S], U8, "h_sc")
         out_v = out.rearrange("(m p) j -> p m j", p=P)
 
+        def quantize_h(j0, j1):
+            cols = slice(j0, j1)
+            nc.vector.quantize_mx(out=h_w[:, cols].bitcast(FP8X4), scales=h_sc[:, cols], in_=h_bf[:, 4 * j0 : 4 * j1])
+
         def score(j0, j1, number):
             cols = slice(j0, j1)
-            q, c0 = divmod(j0, 256)
-            nc.vector.quantize_mx(
-                out=h_w[:, cols].bitcast(FP8X4), scales=h_sc[:, cols], in_=h_bf[q][:, 4 * c0 : 4 * (c0 + j1 - j0)]
-            )
             acc = bank([P, 2, j1 - j0], number)
             for m in range(2):
                 nc.tensor.matmul_mx(
@@ -231,19 +235,15 @@ def tile_list_record_match_scores_kernel(
             nc.scalar.copy(res[:], acc[:])
             (nc.scalar if j1 == S else nc.sync).dma_start(out_v[:, :, cols], res[:])
 
-        key_sum = {}
-
-        def subtract_key(j0, j1, words):
-            b0 = j0 % P
-            if b0 == 0:
-                key_sum[j0] = bank([P, 4, P], j0 // P % 4)
-                for t in range(4):
-                    key_product(key_sum[j0][:, t, :], t, [w[:, j0 : j0 + P] for w in words], j0, P)
-            q, c0 = divmod(j0, 256)
+        def subtract_key(j0, start):
+            acc = bank([P, 4, P], j0 // P % (4 if j0 < HALF else 2))
+            for t in range(4):
+                key_product(acc[:, t, :], t, [w[:, j0 : j0 + P] for w in key], j0, P)
+            c0 = j0 - start
             nc.vector.tensor_tensor(
-                h_bf[q][:, 4 * c0 : 4 * (c0 + j1 - j0)].rearrange("p (c i t) -> p c t i", i=2, t=4),
-                agree[q][:].rearrange("p (t c) -> p t c", t=4)[:, :, c0 : c0 + j1 - j0].rearrange("p t (c i) -> p c t i", i=2),
-                key_sum[j0 - b0][:, :, b0 : b0 + j1 - j0].rearrange("p t (c i) -> p c t i", i=2),
+                h_bf[:, 4 * j0 : 4 * (j0 + P)].rearrange("p (c i t) -> p c t i", i=2, t=4),
+                agree[start][:].rearrange("p (t c) -> p t c", t=4)[:, :, c0 : c0 + P].rearrange("p t (c i) -> p c t i", i=2),
+                acc[:].rearrange("p t (c i) -> p c t i", i=2),
                 ALU.subtract,
             )
 
@@ -262,19 +262,19 @@ def tile_list_record_match_scores_kernel(
         for half in range(2):
             j0 = half * HALF
             left1 = gather_words("left1_%d" % half, list_l, 1, j0, j0 + HALF, (None, "wl_bf1")[half])
-            for q in (2 * half, 2 * half + 1):
-                c0 = q * QUARTER - j0
-                left_product(q, [left0[:, j0 + c0 : j0 + c0 + QUARTER], left1[:, c0 : c0 + QUARTER]])
+            width = (HALF, QUARTER)[half]
+            for c0 in range(0, HALF, width):
+                left_product(j0 + c0, width, [left0[:, j0 + c0 : j0 + c0 + width], left1[:, c0 : c0 + width]])
             if half == 0:
                 right1 = gather_words("right1", list_r, 1, 0, S, "wl_raw1")
             right_product(half, [right0[:, j0 : j0 + HALF], right1[:, j0 : j0 + HALF]])
-            for q in range(max(1, 2 * half), 2 * half + 2):
-                apply_gain(q)
             if half == 0:
                 nc.scalar.copy(
                     wo_bf[:].rearrange("p (c i t) -> p c t i", i=4, t=4),
                     wo_raw[:].rearrange("p t (c i) -> p c t i", i=4),
                 )
+        for q in POOL_COLS:
+            apply_gain(q)
         key_sc = gather_scales("key_sc", list_k, "left1_0")
         wk_w = held([P, PASSES, 4, P], I32, "wk_w", "left0")
         nc.vector.tensor_copy(
@@ -285,17 +285,23 @@ def tile_list_record_match_scores_kernel(
         key = [held([P, S], U32, "key%d" % a, ("wo_raw", "wl_bf1")[a]) for a in range(PASSES)]
         for a, j0, j1 in ((0, 0, S), (1, 0, QUARTER), (1, QUARTER, S)):
             nc.vector.tensor_copy(key[a][:, j0:j1], tab_w[a][:].bitcast(U32).indirect(list_k[:, j0 // 16 : j1 // 16]))
-        agreement(0, "wl_raw1")
-        wo_w = held([P, N], U32, "wo_w", "tanh_a00")
+        agreement(0, HALF, "wl_raw1")
+        wo_w = held([P, N], U32, "wo_w", "tanh_b01")
         nc.vector.quantize_mx(out=wo_w[:].bitcast(FP8X4), scales=wo_sc[:], in_=wo_bf[:])
-        for q in range(3):
-            subtract_key(q * QUARTER, q * QUARTER + P, key)
-            subtract_key(q * QUARTER + P, (q + 1) * QUARTER, key)
-            agreement(q + 1, "tanh_a%d1" % q)
-            score(q * QUARTER, (q + 1) * QUARTER, 4 + q)
-        subtract_key(768, 896, key)
-        subtract_key(896, 960, key)
+        for j0 in range(0, HALF, P):
+            subtract_key(j0, 0)
+        agreement(512, QUARTER, "tanh_a0")
+        quantize_h(0, 512)
+        score(0, 256, 4)
+        score(256, 512, 5)
+        for j0 in (512, 640):
+            subtract_key(j0, 512)
+        agreement(768, QUARTER, "tanh_a512")
+        quantize_h(512, 768)
+        score(512, 768, 6)
+        for j0 in (768, 896):
+            subtract_key(j0, 768)
+        quantize_h(768, 896)
         score(768, 896, 7)
-        subtract_key(960, 1024, key)
-        score(896, 960, 4)
-        score(960, 1024, 5)
+        quantize_h(896, 1024)
+        score(896, 1024, 4)

@@ -236,7 +236,7 @@ def tile_list_record_match_scores_kernel(
             (nc.scalar if j1 == S else nc.sync).dma_start(out_v[:, :, cols], res[:])
 
         def subtract_key(j0, start):
-            acc = bank([P, 4, P], j0 // P % (4 if j0 < HALF else 2))
+            acc = bank([P, 4, P], j0 // P % 4)
             for t in range(4):
                 key_product(acc[:, t, :], t, [w[:, j0 : j0 + P] for w in key], j0, P)
             c0 = j0 - start

@@ -43,13 +43,11 @@ def tile_list_record_match_scores_kernel(
         list_k = keep.tile([P, S // 16], U16, name="list_k")
         tab_sc = held([P, T // 4], I32, "tab_sc")
         tab_w = [held([P, T], I32, "tab_w%d" % a) for a in range(PASSES)]
-        wk_raw = held([P, PASSES, H], I32, "wk_raw")
         wo_raw = held([P, 4, N], F32, "wo_raw")
         wr_raw = held([P, PASSES, H // 2], I32, "wr_raw")
         wr_sc_raw = held([P, PASSES, H // 4], I32, "wr_sc_raw")
         wk_sc_raw = held([P, H // 4], I32, "wk_sc_raw")
         wl_raw = [held([P, 4, H], F32, "wl_raw%d" % a) for a in range(PASSES)]
-        gain = [held([P, 1], F32, "gain%d" % t) for t in range(4)]
         right_sc1 = held([P, S // 4], I32, "right_sc1")
 
         nc.vector.memset(tab_sc[:], 0)
@@ -96,12 +94,8 @@ def tile_list_record_match_scores_kernel(
             nc.sync.dma_start(right_sc1[32 * q : 32 * q + 4, :], right_sc[32 * q + 4 : 32 * q + 8, :].bitcast(I32))
         for t in range(4):
             nc.sync.dma_start(wo_raw[:, t, :], wo.rearrange("(u t e) n -> t u e n", t=4, e=4)[t])
-        nc.sync.dma_start(wk_raw[:], wk_words.rearrange("a p r i -> p a (r i)").bitcast(I32))
         for q in range(4):
             nc.sync.dma_start(wk_sc_raw[32 * q : 32 * q + 8, :], wk_scales[:, 4 * q : 4 * q + 4, :].bitcast(I32))
-        with nc.allow_non_contiguous_dma(reason="one gain to a partition"):
-            for t in range(4):
-                nc.sync.dma_start(gain[t][:], g.rearrange("(u t e) -> t u e", t=4, e=4)[t])
 
         wl_w = held([P, PASSES, H], U32, "wl_w")
         wl_sc = held([P, PASSES, H], U8, "wl_sc")
@@ -134,7 +128,6 @@ def tile_list_record_match_scores_kernel(
 
         wr_w = held([P, PASSES, 4, 2 * P], U8, "wr_w")
         wr_sc = held([P, PASSES, 4, P], U8, "wr_sc")
-        wk_sc = held([P, 4, P], U8, "wk_sc")
         tanh_b, tanh_a, agree, gained = {}, {}, {}, {}
 
         def right_product(half, words):
@@ -178,7 +171,7 @@ def tile_list_record_match_scores_kernel(
                         gained[q][:, t * QUARTER : t * QUARTER + width],
                         tanh_b[1, t][:, c0 : c0 + width],
                         ACT.Copy,
-                        scale=gain[t][:],
+                        scale=gain[:, t, 0:1],
                     )
 
         def agreement(j0, width, slot):
@@ -194,7 +187,7 @@ def tile_list_record_match_scores_kernel(
                     nc.vector.scalar_tensor_tensor(
                         agree[j0][:, cols],
                         tanh_a[j0][:, cols],
-                        gain[t][:],
+                        gain[:, t, 0:1],
                         tanh_b[half, t][:, c0 + skip : c0 + width],
                         ALU.mult,
                         ALU.mult,
@@ -235,15 +228,19 @@ def tile_list_record_match_scores_kernel(
             nc.scalar.copy(res[:], acc[:])
             (nc.scalar if j1 == S else nc.sync).dma_start(out_v[:, :, cols], res[:])
 
-        def subtract_key(j0, start):
-            acc = bank([P, 4, P], j0 // P % 4)
-            for t in range(4):
-                key_product(acc[:, t, :], t, [w[:, j0 : j0 + P] for w in key], j0, P)
+        key_sum = {}
+
+        def subtract_key(j0, start, width=P):
+            b0 = j0 % P
+            if b0 == 0:
+                key_sum[j0] = bank([P, 4, P], j0 // P % 4)
+                for t in range(4):
+                    key_product(key_sum[j0][:, t, :], t, [w[:, j0 : j0 + P] for w in key], j0, P)
             c0 = j0 - start
             nc.vector.tensor_tensor(
-                h_bf[:, 4 * j0 : 4 * (j0 + P)].rearrange("p (c i t) -> p c t i", i=2, t=4),
-                agree[start][:].rearrange("p (t c) -> p t c", t=4)[:, :, c0 : c0 + P].rearrange("p t (c i) -> p c t i", i=2),
-                acc[:].rearrange("p t (c i) -> p c t i", i=2),
+                h_bf[:, 4 * j0 : 4 * (j0 + width)].rearrange("p (c i t) -> p c t i", i=2, t=4),
+                agree[start][:].rearrange("p (t c) -> p t c", t=4)[:, :, c0 : c0 + width].rearrange("p t (c i) -> p c t i", i=2),
+                key_sum[j0 - b0][:, :, b0 : b0 + width].rearrange("p t (c i) -> p c t i", i=2),
                 ALU.subtract,
             )
 
@@ -257,6 +254,12 @@ def tile_list_record_match_scores_kernel(
         for a in range(PASSES):
             round_wl(a)
             quantize_wl(a)
+        wk_raw = held([P, PASSES, H], I32, "wk_raw", "wl_raw0")
+        nc.sync.dma_start(wk_raw[:], wk_words.rearrange("a p r i -> p a (r i)").bitcast(I32))
+        gain = held([P, 4, 8], F32, "gain", "wl_bf0")
+        with nc.allow_non_contiguous_dma(reason="one gain to a partition"):
+            for t in range(4):
+                nc.sync.dma_start(gain[:, t, 0:1], g.rearrange("(u t e) -> t u e", t=4, e=4)[t])
         wo_bf = held([P, 4 * N], BF16, "wo_bf")
         wo_sc = held([P, N], U8, "wo_sc")
         for half in range(2):
@@ -276,12 +279,17 @@ def tile_list_record_match_scores_kernel(
         for q in POOL_COLS:
             apply_gain(q)
         key_sc = gather_scales("key_sc", list_k, "left1_0")
-        wk_w = held([P, PASSES, 4, P], I32, "wk_w", "left0")
+        wk_dealt = held([P, PASSES * H + P], I32, "wk_dealt", "left0")
+        wk_w = wk_dealt[:, : PASSES * H].rearrange("p (a t c) -> p a t c", a=PASSES, t=4)
+        wk_sc = wk_dealt[:, PASSES * H :].bitcast(U8).rearrange("p (t c) -> p t c", t=4)
         nc.vector.tensor_copy(
-            wk_w[:].rearrange("p a t (u e) -> p a t u e", e=4),
+            wk_w.rearrange("p a t (u e) -> p a t u e", e=4),
             wk_raw[:].rearrange("p a (u t e) -> p a t u e", t=4, e=4),
         )
-        nc.vector.tensor_copy(wk_sc[:].bitcast(I32), wk_sc_raw[:].rearrange("p (u t) -> p t u", t=4))
+        nc.vector.tensor_copy(
+            wk_dealt[:, PASSES * H :].rearrange("p (t u) -> p t u", t=4),
+            wk_sc_raw[:].rearrange("p (u t) -> p t u", t=4),
+        )
         key = [held([P, S], U32, "key%d" % a, ("wo_raw", "wl_bf1")[a]) for a in range(PASSES)]
         for a, j0, j1 in ((0, 0, S), (1, 0, QUARTER), (1, QUARTER, S)):
             nc.vector.tensor_copy(key[a][:, j0:j1], tab_w[a][:].bitcast(U32).indirect(list_k[:, j0 // 16 : j1 // 16]))
@@ -290,18 +298,22 @@ def tile_list_record_match_scores_kernel(
         nc.vector.quantize_mx(out=wo_w[:].bitcast(FP8X4), scales=wo_sc[:], in_=wo_bf[:])
         for j0 in range(0, HALF, P):
             subtract_key(j0, 0)
-        agreement(512, QUARTER, "tanh_a0")
-        quantize_h(0, 512)
+        quantize_h(0, 256)
         score(0, 256, 4)
+        agreement(512, QUARTER, "tanh_a0")
+        quantize_h(256, 512)
         score(256, 512, 5)
         for j0 in (512, 640):
             subtract_key(j0, 512)
         agreement(768, QUARTER, "tanh_a512")
         quantize_h(512, 768)
         score(512, 768, 6)
-        for j0 in (768, 896):
-            subtract_key(j0, 768)
+        subtract_key(768, 768)
+        subtract_key(896, 768, 64)
         quantize_h(768, 896)
         score(768, 896, 7)
-        quantize_h(896, 1024)
-        score(896, 1024, 4)
+        subtract_key(960, 768, 64)
+        quantize_h(896, 960)
+        score(896, 960, 4)
+        quantize_h(960, 1024)
+        score(960, 1024, 5)

@@ -20,7 +20,7 @@ P = 128
 PASSES = K // 512
 HALF = S // 2
 QUARTER = S // 4
-POOL_COLS = {2: 896, 3: 384}
+POOL_COLS = {2: 768, 3: 384}
 
 
 def tile_list_record_match_scores_kernel(
@@ -46,14 +46,12 @@ def tile_list_record_match_scores_kernel(
         wo_raw = held([P, 4, N], F32, "wo_raw")
         wr_raw = held([P, PASSES, H // 2], I32, "wr_raw")
         wr_sc_raw = held([P, PASSES, H // 4], I32, "wr_sc_raw")
-        wk_sc_raw = held([P, H // 4], I32, "wk_sc_raw")
         wl_raw = [held([P, 4, H], F32, "wl_raw%d" % a) for a in range(PASSES)]
         right_sc1 = held([P, S // 4], I32, "right_sc1")
 
         nc.vector.memset(tab_sc[:], 0)
         nc.vector.memset(wr_sc_raw[:], 0)
         nc.vector.memset(right_sc1[:], 0)
-        nc.vector.memset(wk_sc_raw[:], 0)
 
         def load_table(a):
             nc.sync.dma_start(tab_w[a][:], tab_words[a].rearrange("p t i -> p (t i)").bitcast(I32))
@@ -67,12 +65,12 @@ def tile_list_record_match_scores_kernel(
         for q in range(4):
             nc.sync.dma_start(tab_sc[32 * q : 32 * q + 8, :], tab_scales[:, 4 * q : 4 * q + 4, :].bitcast(I32))
         load_table(0)
+        load_wl(0)
         for q in range(4):
             nc.sync.dma_start(
                 wr_sc_raw[32 * q : 32 * q + 4, :, :],
                 wr_scales[:, 4 * q : 4 * q + 4, :].bitcast(I32).rearrange("a r w -> r a w"),
             )
-        load_wl(0)
         load_wl(1)
         load_table(1)
         nc.sync.dma_start(list_k[:], offs3)
@@ -94,8 +92,6 @@ def tile_list_record_match_scores_kernel(
             nc.sync.dma_start(right_sc1[32 * q : 32 * q + 4, :], right_sc[32 * q + 4 : 32 * q + 8, :].bitcast(I32))
         for t in range(4):
             nc.sync.dma_start(wo_raw[:, t, :], wo.rearrange("(u t e) n -> t u e n", t=4, e=4)[t])
-        for q in range(4):
-            nc.sync.dma_start(wk_sc_raw[32 * q : 32 * q + 8, :], wk_scales[:, 4 * q : 4 * q + 4, :].bitcast(I32))
 
         wl_w = held([P, PASSES, H], U32, "wl_w")
         wl_sc = held([P, PASSES, H], U8, "wl_sc")
@@ -256,6 +252,9 @@ def tile_list_record_match_scores_kernel(
             quantize_wl(a)
         wk_raw = held([P, PASSES, H], I32, "wk_raw", "wl_raw0")
         nc.sync.dma_start(wk_raw[:], wk_words.rearrange("a p r i -> p a (r i)").bitcast(I32))
+        wk_sc_raw = wr_sc_raw[:, 0, :]
+        for q in range(4):
+            nc.sync.dma_start(wk_sc_raw[32 * q : 32 * q + 8, :], wk_scales[:, 4 * q : 4 * q + 4, :].bitcast(I32))
         gain = held([P, 4, 8], F32, "gain", "wl_bf0")
         with nc.allow_non_contiguous_dma(reason="one gain to a partition"):
             for t in range(4):
@@ -288,20 +287,19 @@ def tile_list_record_match_scores_kernel(
         )
         nc.vector.tensor_copy(
             wk_dealt[:, PASSES * H :].rearrange("p (t u) -> p t u", t=4),
-            wk_sc_raw[:].rearrange("p (u t) -> p t u", t=4),
+            wk_sc_raw.rearrange("p (u t) -> p t u", t=4),
         )
         key = [held([P, S], U32, "key%d" % a, ("wo_raw", "wl_bf1")[a]) for a in range(PASSES)]
         for a, j0, j1 in ((0, 0, S), (1, 0, QUARTER), (1, QUARTER, S)):
             nc.vector.tensor_copy(key[a][:, j0:j1], tab_w[a][:].bitcast(U32).indirect(list_k[:, j0 // 16 : j1 // 16]))
         agreement(0, HALF, "wl_raw1")
-        wo_w = held([P, N], U32, "wo_w", "tanh_b01")
+        wo_w = held([P, N], U32, "wo_w", "tanh_b02")
         nc.vector.quantize_mx(out=wo_w[:].bitcast(FP8X4), scales=wo_sc[:], in_=wo_bf[:])
         for j0 in range(0, HALF, P):
             subtract_key(j0, 0)
-        quantize_h(0, 256)
-        score(0, 256, 4)
         agreement(512, QUARTER, "tanh_a0")
-        quantize_h(256, 512)
+        quantize_h(0, 512)
+        score(0, 256, 4)
         score(256, 512, 5)
         for j0 in (512, 640):
             subtract_key(j0, 512)

@@ -46,7 +46,7 @@ def tile_list_record_match_scores_kernel(
         wo_raw = held([P, 4, N], F32, "wo_raw")
         wr_raw = held([P, PASSES, H // 2], I32, "wr_raw")
         wr_sc_raw = held([P, PASSES, H // 4], I32, "wr_sc_raw")
-        wl_raw = [held([P, 4, H], F32, "wl_raw%d" % a) for a in range(PASSES)]
+        wl_raw = [[held([P, 4, H // 2], F32, "wl_raw%d%d" % (a, x)) for x in range(2)] for a in range(PASSES)]
         right_sc1 = held([P, S // 4], I32, "right_sc1")
 
         nc.vector.memset(tab_sc[:], 0)
@@ -57,23 +57,25 @@ def tile_list_record_match_scores_kernel(
             nc.sync.dma_start(tab_w[a][:], tab_words[a].rearrange("p t i -> p (t i)").bitcast(I32))
 
         def load_wl(a):
-            nc.sync.dma_start(wl_raw[a][:], wl[512 * a : 512 * (a + 1), :].rearrange("(p j) r -> p j r", j=4))
+            rows = wl[512 * a : 512 * (a + 1), :].rearrange("(p j) r -> p j r", j=4)
+            for x in range(2):
+                nc.sync.dma_start(wl_raw[a][x][:], rows[:, :, x * (H // 2) : (x + 1) * (H // 2)])
 
         nc.sync.dma_start(list_r[:], offs2)
-        nc.sync.dma_start(wr_raw[:], wr_words.bitcast(I32).rearrange("a p w -> p a w"))
+        nc.sync.dma_start(list_k[:], offs3)
         nc.sync.dma_start(list_l[:], offs)
         for q in range(4):
             nc.sync.dma_start(tab_sc[32 * q : 32 * q + 8, :], tab_scales[:, 4 * q : 4 * q + 4, :].bitcast(I32))
         load_table(0)
         load_wl(0)
+        load_wl(1)
+        nc.sync.dma_start(wr_raw[:], wr_words.bitcast(I32).rearrange("a p w -> p a w"))
         for q in range(4):
             nc.sync.dma_start(
                 wr_sc_raw[32 * q : 32 * q + 4, :, :],
                 wr_scales[:, 4 * q : 4 * q + 4, :].bitcast(I32).rearrange("a r w -> r a w"),
             )
-        load_wl(1)
         load_table(1)
-        nc.sync.dma_start(list_k[:], offs3)
 
         def gather_scales(name, lst, slot=None):
             dst = held([P, S], U8, name, slot)
@@ -99,10 +101,10 @@ def tile_list_record_match_scores_kernel(
         wl_bf = [held([P, 4, 4 * P], BF16, "wl_bf%d" % a) for a in range(PASSES)]
 
         def round_wl(a):
-            for t in range(4):
+            for x in range(2):
                 nc.scalar.copy(
-                    wl_bf[a][:, t, :].rearrange("p (u e j) -> p u j e", e=4, j=4),
-                    wl_raw[a][:].rearrange("p j (u t e) -> p t u j e", t=4, e=4)[:, t],
+                    wl_bf[a][:, :, x * 2 * P : (x + 1) * 2 * P].rearrange("p t (u e j) -> p t u j e", e=4, j=4),
+                    wl_raw[a][x][:].rearrange("p j (u t e) -> p t u j e", t=4, e=4),
                 )
 
         def quantize_wl(a):
@@ -141,7 +143,7 @@ def tile_list_record_match_scores_kernel(
                 nc.scalar.activation(tanh_b[half, t][:], acc[:], ACT.Tanh)
 
         def left_product(j0, width, words):
-            tanh_a[j0] = held([P, 4 * width], F32, "tanh_a%d" % j0)
+            tanh_a[j0] = held([P, 4 * width], F32, "tanh_a%d" % j0, "wo_raw" if j0 == 0 else None)
             per_bank = HALF // width
             for t0 in range(0, 4, per_bank):
                 acc = bank([P, per_bank, width], (4 * j0 + t0 * width) // HALF % 4)
@@ -240,17 +242,17 @@ def tile_list_record_match_scores_kernel(
                 ALU.subtract,
             )
 
+        left0 = gather_words("left0", list_l, 0, 0, S)
+        right0 = gather_words("right0", list_r, 0, 0, S)
+        for a in range(PASSES):
+            round_wl(a)
+            quantize_wl(a)
         nc.vector.tensor_copy(
             wr_w[:].bitcast(I32).rearrange("p a t (u w) -> p a t u w", w=2),
             wr_raw[:].rearrange("p a (u t w) -> p a t u w", t=4, w=2),
         )
-        left0 = gather_words("left0", list_l, 0, 0, S)
-        right0 = gather_words("right0", list_r, 0, 0, S)
         nc.vector.tensor_copy(wr_sc[:].bitcast(I32), wr_sc_raw[:].rearrange("p a (u t) -> p a t u", t=4))
-        for a in range(PASSES):
-            round_wl(a)
-            quantize_wl(a)
-        wk_raw = held([P, PASSES, H], I32, "wk_raw", "wl_raw0")
+        wk_raw = held([P, PASSES, H], I32, "wk_raw", "wl_raw00")
         nc.sync.dma_start(wk_raw[:], wk_words.rearrange("a p r i -> p a (r i)").bitcast(I32))
         wk_sc_raw = wr_sc_raw[:, 0, :]
         for q in range(4):
@@ -261,20 +263,18 @@ def tile_list_record_match_scores_kernel(
                 nc.sync.dma_start(gain[:, t, 0:1], g.rearrange("(u t e) -> t u e", t=4, e=4)[t])
         wo_bf = held([P, 4 * N], BF16, "wo_bf")
         wo_sc = held([P, N], U8, "wo_sc")
+        nc.scalar.copy(
+            wo_bf[:].rearrange("p (c i t) -> p c t i", i=4, t=4),
+            wo_raw[:].rearrange("p t (c i) -> p c t i", i=4),
+        )
         for half in range(2):
             j0 = half * HALF
             left1 = gather_words("left1_%d" % half, list_l, 1, j0, j0 + HALF, (None, "wl_bf1")[half])
             width = (HALF, QUARTER)[half]
             for c0 in range(0, HALF, width):
                 left_product(j0 + c0, width, [left0[:, j0 + c0 : j0 + c0 + width], left1[:, c0 : c0 + width]])
-            if half == 0:
-                right1 = gather_words("right1", list_r, 1, 0, S, "wl_raw1")
-            right_product(half, [right0[:, j0 : j0 + HALF], right1[:, j0 : j0 + HALF]])
-            if half == 0:
-                nc.scalar.copy(
-                    wo_bf[:].rearrange("p (c i t) -> p c t i", i=4, t=4),
-                    wo_raw[:].rearrange("p t (c i) -> p c t i", i=4),
-                )
+            right1 = gather_words("right1_%d" % half, list_r, 1, j0, j0 + HALF)
+            right_product(half, [right0[:, j0 : j0 + HALF], right1[:]])
         for q in POOL_COLS:
             apply_gain(q)
         key_sc = gather_scales("key_sc", list_k, "left1_0")
@@ -289,15 +289,15 @@ def tile_list_record_match_scores_kernel(
             wk_dealt[:, PASSES * H :].rearrange("p (t u) -> p t u", t=4),
             wk_sc_raw.rearrange("p (u t) -> p t u", t=4),
         )
-        key = [held([P, S], U32, "key%d" % a, ("wo_raw", "wl_bf1")[a]) for a in range(PASSES)]
+        key = [held([P, S], U32, "key%d" % a, ("wl_raw00", "wl_bf1")[a]) for a in range(PASSES)]
         for a, j0, j1 in ((0, 0, S), (1, 0, QUARTER), (1, QUARTER, S)):
             nc.vector.tensor_copy(key[a][:, j0:j1], tab_w[a][:].bitcast(U32).indirect(list_k[:, j0 // 16 : j1 // 16]))
-        agreement(0, HALF, "wl_raw1")
+        agreement(0, HALF, "right0")
         wo_w = held([P, N], U32, "wo_w", "tanh_b02")
         nc.vector.quantize_mx(out=wo_w[:].bitcast(FP8X4), scales=wo_sc[:], in_=wo_bf[:])
         for j0 in range(0, HALF, P):
             subtract_key(j0, 0)
-        agreement(512, QUARTER, "tanh_a0")
+        agreement(512, QUARTER, "wo_raw")
         quantize_h(0, 512)
         score(0, 256, 4)
         score(256, 512, 5)

@@ -62,20 +62,20 @@ def tile_list_record_match_scores_kernel(
                 nc.sync.dma_start(wl_raw[a][x][:], rows[:, :, x * (H // 2) : (x + 1) * (H // 2)])
 
         nc.sync.dma_start(list_r[:], offs2)
-        nc.sync.dma_start(list_k[:], offs3)
+        nc.sync.dma_start(wr_raw[:], wr_words.bitcast(I32).rearrange("a p w -> p a w"))
         nc.sync.dma_start(list_l[:], offs)
         for q in range(4):
             nc.sync.dma_start(tab_sc[32 * q : 32 * q + 8, :], tab_scales[:, 4 * q : 4 * q + 4, :].bitcast(I32))
         load_table(0)
         load_wl(0)
         load_wl(1)
-        nc.sync.dma_start(wr_raw[:], wr_words.bitcast(I32).rearrange("a p w -> p a w"))
         for q in range(4):
             nc.sync.dma_start(
                 wr_sc_raw[32 * q : 32 * q + 4, :, :],
                 wr_scales[:, 4 * q : 4 * q + 4, :].bitcast(I32).rearrange("a r w -> r a w"),
             )
         load_table(1)
+        nc.sync.dma_start(list_k[:], offs3)
 
         def gather_scales(name, lst, slot=None):
             dst = held([P, S], U8, name, slot)
@@ -93,7 +93,7 @@ def tile_list_record_match_scores_kernel(
         for q in range(4):
             nc.sync.dma_start(right_sc1[32 * q : 32 * q + 4, :], right_sc[32 * q + 4 : 32 * q + 8, :].bitcast(I32))
         for t in range(4):
-            nc.sync.dma_start(wo_raw[:, t, :], wo.rearrange("(u t e) n -> t u e n", t=4, e=4)[t])
+            nc.sync.dma_start(wo_raw[:, t, :], wo.rearrange("(b t e) n -> t b e n", t=4, e=8)[t])
 
         wl_w = held([P, PASSES, H], U32, "wl_w")
         wl_sc = held([P, PASSES, H], U8, "wl_sc")
@@ -102,10 +102,10 @@ def tile_list_record_match_scores_kernel(
 
         def round_wl(a):
             for x in range(2):
-                nc.scalar.copy(
-                    wl_bf[a][:, :, x * 2 * P : (x + 1) * 2 * P].rearrange("p t (u e j) -> p t u j e", e=4, j=4),
-                    wl_raw[a][x][:].rearrange("p j (u t e) -> p t u j e", t=4, e=4),
-                )
+                dst = wl_bf[a][:, :, x * 2 * P : (x + 1) * 2 * P].rearrange("p t (b y e j) -> p y t b j e", y=2, e=4, j=4)
+                src = wl_raw[a][x][:].rearrange("p j (b t y e) -> p y t b j e", t=4, y=2, e=4)
+                for y in range(2):
+                    nc.scalar.copy(dst[:, y], src[:, y])
 
         def quantize_wl(a):
             nc.vector.quantize_mx(
@@ -242,25 +242,31 @@ def tile_list_record_match_scores_kernel(
                 ALU.subtract,
             )
 
+        nc.vector.tensor_copy(
+            wr_w[:].bitcast(I32).rearrange("p a t (b w) -> p a t b w", w=4),
+            wr_raw[:].rearrange("p a (b t w) -> p a t b w", t=4, w=4),
+        )
         left0 = gather_words("left0", list_l, 0, 0, S)
         right0 = gather_words("right0", list_r, 0, 0, S)
         for a in range(PASSES):
             round_wl(a)
             quantize_wl(a)
         nc.vector.tensor_copy(
-            wr_w[:].bitcast(I32).rearrange("p a t (u w) -> p a t u w", w=2),
-            wr_raw[:].rearrange("p a (u t w) -> p a t u w", t=4, w=2),
+            wr_sc[:].bitcast(I32).rearrange("p a t (b w) -> p a t b w", w=2),
+            wr_sc_raw[:].rearrange("p a (b t w) -> p a t b w", t=4, w=2),
         )
-        nc.vector.tensor_copy(wr_sc[:].bitcast(I32), wr_sc_raw[:].rearrange("p a (u t) -> p a t u", t=4))
-        wk_raw = held([P, PASSES, H], I32, "wk_raw", "wl_raw00")
-        nc.sync.dma_start(wk_raw[:], wk_words.rearrange("a p r i -> p a (r i)").bitcast(I32))
         wk_sc_raw = wr_sc_raw[:, 0, :]
         for q in range(4):
             nc.sync.dma_start(wk_sc_raw[32 * q : 32 * q + 8, :], wk_scales[:, 4 * q : 4 * q + 4, :].bitcast(I32))
         gain = held([P, 4, 8], F32, "gain", "wl_bf0")
         with nc.allow_non_contiguous_dma(reason="one gain to a partition"):
             for t in range(4):
-                nc.sync.dma_start(gain[:, t, 0:1], g.rearrange("(u t e) -> t u e", t=4, e=4)[t])
+                nc.sync.dma_start(gain[:, t, 0:1], g.rearrange("(b t e) -> t b e", t=4, e=8)[t])
+        wk_w = held([P, PASSES, 4, P], I32, "wk_w", "wl_raw11")
+        for t in range(4):
+            for a in range(PASSES):
+                runs = wk_words[a].rearrange("p r i -> p (r i)").bitcast(I32).rearrange("p (b t e) -> p t b e", t=4, e=8)
+                nc.sync.dma_start(wk_w[:, a, t, :].rearrange("p (b e) -> p b e", e=8), runs[:, t])
         wo_bf = held([P, 4 * N], BF16, "wo_bf")
         wo_sc = held([P, N], U8, "wo_sc")
         nc.scalar.copy(
@@ -278,20 +284,19 @@ def tile_list_record_match_scores_kernel(
         for q in POOL_COLS:
             apply_gain(q)
         key_sc = gather_scales("key_sc", list_k, "left1_0")
-        wk_dealt = held([P, PASSES * H + P], I32, "wk_dealt", "left0")
-        wk_w = wk_dealt[:, : PASSES * H].rearrange("p (a t c) -> p a t c", a=PASSES, t=4)
-        wk_sc = wk_dealt[:, PASSES * H :].bitcast(U8).rearrange("p (t c) -> p t c", t=4)
-        nc.vector.tensor_copy(
-            wk_w.rearrange("p a t (u e) -> p a t u e", e=4),
-            wk_raw[:].rearrange("p a (u t e) -> p a t u e", t=4, e=4),
-        )
-        nc.vector.tensor_copy(
-            wk_dealt[:, PASSES * H :].rearrange("p (t u) -> p t u", t=4),
-            wk_sc_raw.rearrange("p (u t) -> p t u", t=4),
-        )
-        key = [held([P, S], U32, "key%d" % a, ("wl_raw00", "wl_bf1")[a]) for a in range(PASSES)]
-        for a, j0, j1 in ((0, 0, S), (1, 0, QUARTER), (1, QUARTER, S)):
+        key = [held([P, S], U32, "key%d" % a, ("right1_0", "wl_bf1")[a]) for a in range(PASSES)]
+
+        def gather_key(a, j0, j1):
             nc.vector.tensor_copy(key[a][:, j0:j1], tab_w[a][:].bitcast(U32).indirect(list_k[:, j0 // 16 : j1 // 16]))
+
+        gather_key(0, 0, S)
+        wk_sc = held([P, 4, P], U8, "wk_sc")
+        nc.vector.tensor_copy(
+            wk_sc[:].bitcast(I32).rearrange("p t (b w) -> p t b w", w=2),
+            wk_sc_raw.rearrange("p (b t w) -> p t b w", t=4, w=2),
+        )
+        gather_key(1, 0, QUARTER)
+        gather_key(1, QUARTER, S)
         agreement(0, HALF, "right0")
         wo_w = held([P, N], U32, "wo_w", "tanh_b02")
         nc.vector.quantize_mx(out=wo_w[:].bitcast(FP8X4), scales=wo_sc[:], in_=wo_bf[:])

@@ -262,11 +262,8 @@ def tile_list_record_match_scores_kernel(
         with nc.allow_non_contiguous_dma(reason="one gain to a partition"):
             for t in range(4):
                 nc.sync.dma_start(gain[:, t, 0:1], g.rearrange("(b t e) -> t b e", t=4, e=8)[t])
-        wk_w = held([P, PASSES, 4, P], I32, "wk_w", "wl_raw11")
-        for t in range(4):
-            for a in range(PASSES):
-                runs = wk_words[a].rearrange("p r i -> p (r i)").bitcast(I32).rearrange("p (b t e) -> p t b e", t=4, e=8)
-                nc.sync.dma_start(wk_w[:, a, t, :].rearrange("p (b e) -> p b e", e=8), runs[:, t])
+        wk_raw = held([P, PASSES, H], I32, "wk_raw", "wl_raw00")
+        nc.sync.dma_start(wk_raw[:], wk_words.rearrange("a p r i -> p a (r i)").bitcast(I32))
         wo_bf = held([P, 4 * N], BF16, "wo_bf")
         wo_sc = held([P, N], U8, "wo_sc")
         nc.scalar.copy(
@@ -290,6 +287,11 @@ def tile_list_record_match_scores_kernel(
             nc.vector.tensor_copy(key[a][:, j0:j1], tab_w[a][:].bitcast(U32).indirect(list_k[:, j0 // 16 : j1 // 16]))
 
         gather_key(0, 0, S)
+        wk_w = held([P, PASSES, 4, P], I32, "wk_w")
+        nc.vector.tensor_copy(
+            wk_w[:].rearrange("p a t (b e) -> p a t b e", e=8),
+            wk_raw[:].rearrange("p a (b t e) -> p a t b e", t=4, e=8),
+        )
         wk_sc = held([P, 4, P], U8, "wk_sc")
         nc.vector.tensor_copy(
             wk_sc[:].bitcast(I32).rearrange("p t (b w) -> p t b w", w=2),

@@ -46,7 +46,7 @@ def tile_list_record_match_scores_kernel(
         wo_raw = held([P, 4, N], F32, "wo_raw")
         wr_raw = held([P, PASSES, H // 2], I32, "wr_raw")
         wr_sc_raw = held([P, PASSES, H // 4], I32, "wr_sc_raw")
-        wl_raw = [[held([P, 4, H // 2], F32, "wl_raw%d%d" % (a, x)) for x in range(2)] for a in range(PASSES)]
+        wl_raw = [held([P, 4, H], F32, "wl_raw%d" % a) for a in range(PASSES)]
         right_sc1 = held([P, S // 4], I32, "right_sc1")
 
         nc.vector.memset(tab_sc[:], 0)
@@ -57,9 +57,7 @@ def tile_list_record_match_scores_kernel(
             nc.sync.dma_start(tab_w[a][:], tab_words[a].rearrange("p t i -> p (t i)").bitcast(I32))
 
         def load_wl(a):
-            rows = wl[512 * a : 512 * (a + 1), :].rearrange("(p j) r -> p j r", j=4)
-            for x in range(2):
-                nc.sync.dma_start(wl_raw[a][x][:], rows[:, :, x * (H // 2) : (x + 1) * (H // 2)])
+            nc.sync.dma_start(wl_raw[a][:], wl[512 * a : 512 * (a + 1), :].rearrange("(p j) r -> p j r", j=4))
 
         nc.sync.dma_start(list_r[:], offs2)
         nc.sync.dma_start(wr_raw[:], wr_words.bitcast(I32).rearrange("a p w -> p a w"))
@@ -67,6 +65,7 @@ def tile_list_record_match_scores_kernel(
         for q in range(4):
             nc.sync.dma_start(tab_sc[32 * q : 32 * q + 8, :], tab_scales[:, 4 * q : 4 * q + 4, :].bitcast(I32))
         load_table(0)
+        nc.sync.dma_start(list_k[:], offs3)
         load_wl(0)
         load_wl(1)
         for q in range(4):
@@ -75,11 +74,10 @@ def tile_list_record_match_scores_kernel(
                 wr_scales[:, 4 * q : 4 * q + 4, :].bitcast(I32).rearrange("a r w -> r a w"),
             )
         load_table(1)
-        nc.sync.dma_start(list_k[:], offs3)
 
-        def gather_scales(name, lst, slot=None):
-            dst = held([P, S], U8, name, slot)
-            nc.vector.tensor_copy(dst[:], tab_sc[:].bitcast(U8).indirect(lst[:]))
+        def gather_scales(name, lst, j0=0, j1=S, slot=None):
+            dst = held([P, j1 - j0], U8, name, slot)
+            nc.vector.tensor_copy(dst[:], tab_sc[:].bitcast(U8).indirect(lst[:, j0 // 16 : j1 // 16]))
             return dst
 
         def gather_words(name, lst, a, j0, j1, slot=None):
@@ -101,11 +99,10 @@ def tile_list_record_match_scores_kernel(
         wl_bf = [held([P, 4, 4 * P], BF16, "wl_bf%d" % a) for a in range(PASSES)]
 
         def round_wl(a):
-            for x in range(2):
-                dst = wl_bf[a][:, :, x * 2 * P : (x + 1) * 2 * P].rearrange("p t (b y e j) -> p y t b j e", y=2, e=4, j=4)
-                src = wl_raw[a][x][:].rearrange("p j (b t y e) -> p y t b j e", t=4, y=2, e=4)
-                for y in range(2):
-                    nc.scalar.copy(dst[:, y], src[:, y])
+            dst = wl_bf[a][:].rearrange("p t (b y e j) -> p y t b j e", y=2, e=4, j=4)
+            src = wl_raw[a][:].rearrange("p j (b t y e) -> p y t b j e", t=4, y=2, e=4)
+            for y in range(2):
+                nc.scalar.copy(dst[:, y], src[:, y])
 
         def quantize_wl(a):
             nc.vector.quantize_mx(
@@ -197,7 +194,7 @@ def tile_list_record_match_scores_kernel(
                 [wk_w[:, a, t, :].bitcast(FP8X4) for a in range(PASSES)],
                 [wk_sc[4 * a : P, t, :] for a in range(PASSES)],
                 words,
-                [key_sc[4 * a : P, j0 : j0 + width] for a in range(PASSES)],
+                [key_sc[j0 // HALF][4 * a : P, j0 % HALF : j0 % HALF + width] for a in range(PASSES)],
             )
 
         h_bf = held([P, 4 * S], BF16, "h_bf")
@@ -248,6 +245,7 @@ def tile_list_record_match_scores_kernel(
         )
         left0 = gather_words("left0", list_l, 0, 0, S)
         right0 = gather_words("right0", list_r, 0, 0, S)
+        key_sc = [gather_scales("key_sc0", list_k, 0, HALF)]
         for a in range(PASSES):
             round_wl(a)
             quantize_wl(a)
@@ -262,7 +260,7 @@ def tile_list_record_match_scores_kernel(
         with nc.allow_non_contiguous_dma(reason="one gain to a partition"):
             for t in range(4):
                 nc.sync.dma_start(gain[:, t, 0:1], g.rearrange("(b t e) -> t b e", t=4, e=8)[t])
-        wk_raw = held([P, PASSES, H], I32, "wk_raw", "wl_raw00")
+        wk_raw = held([P, PASSES, H], I32, "wk_raw", "wl_raw0")
         nc.sync.dma_start(wk_raw[:], wk_words.rearrange("a p r i -> p a (r i)").bitcast(I32))
         wo_bf = held([P, 4 * N], BF16, "wo_bf")
         wo_sc = held([P, N], U8, "wo_sc")
@@ -280,7 +278,7 @@ def tile_list_record_match_scores_kernel(
             right_product(half, [right0[:, j0 : j0 + HALF], right1[:]])
         for q in POOL_COLS:
             apply_gain(q)
-        key_sc = gather_scales("key_sc", list_k, "left1_0")
+        key_sc.append(gather_scales("key_sc1", list_k, HALF, S, "left1_0"))
         key = [held([P, S], U32, "key%d" % a, ("right1_0", "wl_bf1")[a]) for a in range(PASSES)]
 
         def gather_key(a, j0, j1):

@@ -1,6 +1,7 @@
 from contextlib import ExitStack
 
 import concourse.mybir as mybir
+from concourse.masks import make_identity
 
 K, H, N, T, S = 1024, 512, 256, 2048, 1024
 FLOPS = 2 * S * H * (3 * K + N)
@@ -20,7 +21,6 @@ P = 128
 PASSES = K // 512
 HALF = S // 2
 QUARTER = S // 4
-POOL_COLS = {2: 768, 3: 384}
 
 
 def tile_list_record_match_scores_kernel(
@@ -29,29 +29,44 @@ def tile_list_record_match_scores_kernel(
     nc = tc.nc
     with ExitStack() as ctx:
         keep = ctx.enter_context(tc.tile_pool(name="keep", bufs=1))
-        res_pool = ctx.enter_context(tc.tile_pool(name="res", bufs=6))
+        laid = ctx.enter_context(tc.tile_pool(name="laid", bufs=1))
+        res_pool = ctx.enter_context(tc.tile_pool(name="res", bufs=7))
         acc_pool = ctx.enter_context(tc.psum_pool(name="acc", bufs=1))
+        upper_pool = ctx.enter_context(tc.psum_pool(name="upper", bufs=1))
 
         def held(shape, dtype, name, slot=None):
             return keep.tile(shape, dtype, name=name, tag=slot or name, align_bytes=64)
 
+        def placed(shape, dtype, name, offset):
+            return laid.tile(shape, dtype, name=name, tag=name, align_bytes=64, offset=offset)
+
         def bank(shape, number):
             return acc_pool.tile(shape, F32, name="acc", tag="bank%d" % number)
+
+        def upper(shape, name, number):
+            return upper_pool.tile(shape, F32, name=name, tag=name, offset=2048 * number)
 
         list_l = keep.tile([P, S // 16], U16, name="list_l")
         list_r = keep.tile([P, S // 16], U16, name="list_r")
         list_k = keep.tile([P, S // 16], U16, name="list_k")
         tab_sc = held([P, T // 4], I32, "tab_sc")
-        tab_w = [held([P, T], I32, "tab_w%d" % a) for a in range(PASSES)]
+        tab_w = [held([P, T], I32, "tab_w0"), placed([P, T], I32, "tab_w1", 10240)]
         wo_raw = held([P, 4, N], F32, "wo_raw")
         wr_raw = held([P, PASSES, H // 2], I32, "wr_raw")
         wr_sc_raw = held([P, PASSES, H // 4], I32, "wr_sc_raw")
-        wl_raw = [held([P, 4, H], F32, "wl_raw%d" % a) for a in range(PASSES)]
+        wl_raw = [held([P, 4, H], F32, "wl_raw0"), placed([P, 4, H], F32, "wl_raw1", 0)]
         right_sc1 = held([P, S // 4], I32, "right_sc1")
+        wk_sc_raw = placed([P, H // 4], I32, "wk_sc_raw", 18432)
+        wo_bf = placed([P, 4 * N], BF16, "wo_bf", 18944)
+        wk_raw = placed([P, PASSES, H], I32, "wk_raw", 20992)
+        gain = held([P, 4, 8], F32, "gain")
+        ident = held([P, P], F32, "ident")
 
         nc.vector.memset(tab_sc[:], 0)
         nc.vector.memset(wr_sc_raw[:], 0)
         nc.vector.memset(right_sc1[:], 0)
+        nc.vector.memset(wk_sc_raw[:], 0)
+        make_identity(nc, ident[:])
 
         def load_table(a):
             nc.sync.dma_start(tab_w[a][:], tab_words[a].rearrange("p t i -> p (t i)").bitcast(I32))
@@ -65,226 +80,171 @@ def tile_list_record_match_scores_kernel(
         for q in range(4):
             nc.sync.dma_start(tab_sc[32 * q : 32 * q + 8, :], tab_scales[:, 4 * q : 4 * q + 4, :].bitcast(I32))
         load_table(0)
-        nc.sync.dma_start(list_k[:], offs3)
-        load_wl(0)
-        load_wl(1)
         for q in range(4):
             nc.sync.dma_start(
                 wr_sc_raw[32 * q : 32 * q + 4, :, :],
                 wr_scales[:, 4 * q : 4 * q + 4, :].bitcast(I32).rearrange("a r w -> r a w"),
             )
+        nc.sync.dma_start(list_k[:], offs3)
+        load_wl(0)
+        load_wl(1)
         load_table(1)
-
-        def gather_scales(name, lst, j0=0, j1=S, slot=None):
-            dst = held([P, j1 - j0], U8, name, slot)
-            nc.vector.tensor_copy(dst[:], tab_sc[:].bitcast(U8).indirect(lst[:, j0 // 16 : j1 // 16]))
-            return dst
-
-        def gather_words(name, lst, a, j0, j1, slot=None):
-            dst = held([P, j1 - j0], U32, name, slot)
-            nc.vector.tensor_copy(dst[:], tab_w[a][:].bitcast(U32).indirect(lst[:, j0 // 16 : j1 // 16]))
-            return dst
-
-        right_sc = gather_scales("right_sc", list_r)
-        left_sc = gather_scales("left_sc", list_l)
-        right_planes = [right_sc[:], right_sc1[:].bitcast(U8)]
-        for q in range(4):
-            nc.sync.dma_start(right_sc1[32 * q : 32 * q + 4, :], right_sc[32 * q + 4 : 32 * q + 8, :].bitcast(I32))
         for t in range(4):
             nc.sync.dma_start(wo_raw[:, t, :], wo.rearrange("(b t e) n -> t b e n", t=4, e=8)[t])
 
-        wl_w = held([P, PASSES, H], U32, "wl_w")
-        wl_sc = held([P, PASSES, H], U8, "wl_sc")
+        def gather_scales(dst, lst, j0, j1):
+            nc.vector.tensor_copy(dst, tab_sc[:].bitcast(U8).indirect(lst[:, j0 // 16 : j1 // 16]))
 
-        wl_bf = [held([P, 4, 4 * P], BF16, "wl_bf%d" % a) for a in range(PASSES)]
-
-        def round_wl(a):
-            dst = wl_bf[a][:].rearrange("p t (b y e j) -> p y t b j e", y=2, e=4, j=4)
-            src = wl_raw[a][:].rearrange("p j (b t y e) -> p y t b j e", t=4, y=2, e=4)
-            for y in range(2):
-                nc.scalar.copy(dst[:, y], src[:, y])
-
-        def quantize_wl(a):
-            nc.vector.quantize_mx(
-                out=wl_w[:, a, :].bitcast(FP8X4), scales=wl_sc[:, a, :], in_=wl_bf[a][:].rearrange("p t x -> p (t x)")
-            )
-
-        def product(acc, weight, weight_sc, words, planes):
-            for a in range(PASSES):
-                nc.tensor.matmul_mx(
-                    out=acc,
-                    lhsT=weight[a],
-                    lhsT_scale=weight_sc[a],
-                    rhs=words[a].bitcast(FP8X4),
-                    rhs_scale=planes[a],
-                    start=(a == 0),
-                    stop=(a == PASSES - 1),
-                )
+        def gather_words(dst, lst, a, j0, j1):
+            nc.vector.tensor_copy(dst, tab_w[a][:].bitcast(U32).indirect(lst[:, j0 // 16 : j1 // 16]))
 
         wr_w = held([P, PASSES, 4, 2 * P], U8, "wr_w")
         wr_sc = held([P, PASSES, 4, P], U8, "wr_sc")
-        tanh_b, tanh_a, agree, gained = {}, {}, {}, {}
-
-        def right_product(half, words):
-            cols = slice(half * HALF, (half + 1) * HALF)
-            for t in range(4):
-                acc = bank([P, HALF], t)
-                product(
-                    acc[:],
-                    [wr_w[:, a, t, :].bitcast(FP4X4) for a in range(PASSES)],
-                    [wr_sc[:, a, t, :] for a in range(PASSES)],
-                    words,
-                    [plane[:, cols] for plane in right_planes],
-                )
-                tanh_b[half, t] = held([P, HALF], F32, "tanh_b%d%d" % (half, t))
-                nc.scalar.activation(tanh_b[half, t][:], acc[:], ACT.Tanh)
-
-        def left_product(j0, width, words):
-            tanh_a[j0] = held([P, 4 * width], F32, "tanh_a%d" % j0, "wo_raw" if j0 == 0 else None)
-            per_bank = HALF // width
-            for t0 in range(0, 4, per_bank):
-                acc = bank([P, per_bank, width], (4 * j0 + t0 * width) // HALF % 4)
-                for t in range(t0, t0 + per_bank):
-                    product(
-                        acc[:, t - t0, :],
-                        [wl_w[:, a, t * P : (t + 1) * P].bitcast(FP8X4) for a in range(PASSES)],
-                        [wl_sc[:, a, t * P : (t + 1) * P] for a in range(PASSES)],
-                        words,
-                        [left_sc[4 * a : P, j0 : j0 + width] for a in range(PASSES)],
-                    )
-                nc.scalar.activation(
-                    tanh_a[j0][:, t0 * width : t0 * width + HALF], acc[:].rearrange("p t c -> p (t c)"), ACT.Tanh
-                )
-
-        def apply_gain(q):
-            c0 = q * QUARTER - HALF
-            gained[q] = held([P, POOL_COLS[q]], F32, "gained%d" % q)
-            for t in range(4):
-                width = min(QUARTER, POOL_COLS[q] - t * QUARTER)
-                if width > 0:
-                    nc.scalar.activation(
-                        gained[q][:, t * QUARTER : t * QUARTER + width],
-                        tanh_b[1, t][:, c0 : c0 + width],
-                        ACT.Copy,
-                        scale=gain[:, t, 0:1],
-                    )
-
-        def agreement(j0, width, slot):
-            half, c0 = divmod(j0, HALF)
-            agree[j0] = held([P, 4 * width], F32, "agree%d" % j0, slot)
-            first = POOL_COLS.get(j0 // QUARTER, 0)
-            if first:
-                nc.gpsimd.tensor_tensor(agree[j0][:, :first], tanh_a[j0][:, :first], gained[j0 // QUARTER][:], ALU.mult)
-            for t in range(4):
-                skip = max(0, first - t * width)
-                if skip < width:
-                    cols = slice(t * width + skip, (t + 1) * width)
-                    nc.vector.scalar_tensor_tensor(
-                        agree[j0][:, cols],
-                        tanh_a[j0][:, cols],
-                        gain[:, t, 0:1],
-                        tanh_b[half, t][:, c0 + skip : c0 + width],
-                        ALU.mult,
-                        ALU.mult,
-                    )
-
-        def key_product(acc, t, words, j0, width):
-            product(
-                acc,
-                [wk_w[:, a, t, :].bitcast(FP8X4) for a in range(PASSES)],
-                [wk_sc[4 * a : P, t, :] for a in range(PASSES)],
-                words,
-                [key_sc[j0 // HALF][4 * a : P, j0 % HALF : j0 % HALF + width] for a in range(PASSES)],
-            )
-
-        h_bf = held([P, 4 * S], BF16, "h_bf")
-        h_w = held([P, S], U32, "h_w")
-        h_sc = held([P, S], U8, "h_sc")
-        out_v = out.rearrange("(m p) j -> p m j", p=P)
-
-        def quantize_h(j0, j1):
-            cols = slice(j0, j1)
-            nc.vector.quantize_mx(out=h_w[:, cols].bitcast(FP8X4), scales=h_sc[:, cols], in_=h_bf[:, 4 * j0 : 4 * j1])
-
-        def score(j0, j1, number):
-            cols = slice(j0, j1)
-            acc = bank([P, 2, j1 - j0], number)
-            for m in range(2):
-                nc.tensor.matmul_mx(
-                    out=acc[:, m, :],
-                    lhsT=wo_w[:, m * P : (m + 1) * P].bitcast(FP8X4),
-                    lhsT_scale=wo_sc[:, m * P : (m + 1) * P],
-                    rhs=h_w[:, cols].bitcast(FP8X4),
-                    rhs_scale=h_sc[:, cols],
-                    start=True,
-                    stop=True,
-                )
-            res = res_pool.tile([P, 2, j1 - j0], F32, name="res")
-            nc.scalar.copy(res[:], acc[:])
-            (nc.scalar if j1 == S else nc.sync).dma_start(out_v[:, :, cols], res[:])
-
-        key_sum = {}
-
-        def subtract_key(j0, start, width=P):
-            b0 = j0 % P
-            if b0 == 0:
-                key_sum[j0] = bank([P, 4, P], j0 // P % 4)
-                for t in range(4):
-                    key_product(key_sum[j0][:, t, :], t, [w[:, j0 : j0 + P] for w in key], j0, P)
-            c0 = j0 - start
-            nc.vector.tensor_tensor(
-                h_bf[:, 4 * j0 : 4 * (j0 + width)].rearrange("p (c i t) -> p c t i", i=2, t=4),
-                agree[start][:].rearrange("p (t c) -> p t c", t=4)[:, :, c0 : c0 + width].rearrange("p t (c i) -> p c t i", i=2),
-                key_sum[j0 - b0][:, :, b0 : b0 + width].rearrange("p t (c i) -> p c t i", i=2),
-                ALU.subtract,
-            )
-
         nc.vector.tensor_copy(
             wr_w[:].bitcast(I32).rearrange("p a t (b w) -> p a t b w", w=4),
             wr_raw[:].rearrange("p a (b t w) -> p a t b w", t=4, w=4),
         )
-        left0 = gather_words("left0", list_l, 0, 0, S)
-        right0 = gather_words("right0", list_r, 0, 0, S)
-        key_sc = [gather_scales("key_sc0", list_k, 0, HALF)]
-        for a in range(PASSES):
-            round_wl(a)
-            quantize_wl(a)
+        right_sc = held([P, S], U8, "right_sc")
+        left_sc = held([P, S], U8, "left_sc")
+        gather_scales(right_sc[:], list_r, 0, S)
+        gather_scales(left_sc[:], list_l, 0, S)
+        right_planes = [right_sc[:], right_sc1[:].bitcast(U8)]
+        for q in range(4):
+            nc.sync.dma_start(right_sc1[32 * q : 32 * q + 4, :], right_sc[32 * q + 4 : 32 * q + 8, :].bitcast(I32))
+        nc.sync.dma_start(wk_raw[:], wk_words.rearrange("a p r i -> p a (r i)").bitcast(I32))
+        for q in range(4):
+            nc.sync.dma_start(wk_sc_raw[32 * q : 32 * q + 8, :], wk_scales[:, 4 * q : 4 * q + 4, :].bitcast(I32))
+        with nc.allow_non_contiguous_dma(reason="one gain to a partition"):
+            for t in range(4):
+                nc.sync.dma_start(gain[:, t, 0:1], g.rearrange("(b t e) -> t b e", t=4, e=8)[t])
+
+        left = [held([P, S], U32, "left0")]
+        right = [held([P, S], U32, "right0")]
+        gather_words(left[0][:], list_l, 0, 0, S)
+        gather_words(right[0][:], list_r, 0, 0, S)
         nc.vector.tensor_copy(
             wr_sc[:].bitcast(I32).rearrange("p a t (b w) -> p a t b w", w=2),
             wr_sc_raw[:].rearrange("p a (b t w) -> p a t b w", t=4, w=2),
         )
-        wk_sc_raw = wr_sc_raw[:, 0, :]
-        for q in range(4):
-            nc.sync.dma_start(wk_sc_raw[32 * q : 32 * q + 8, :], wk_scales[:, 4 * q : 4 * q + 4, :].bitcast(I32))
-        gain = held([P, 4, 8], F32, "gain", "wl_bf0")
-        with nc.allow_non_contiguous_dma(reason="one gain to a partition"):
-            for t in range(4):
-                nc.sync.dma_start(gain[:, t, 0:1], g.rearrange("(b t e) -> t b e", t=4, e=8)[t])
-        wk_raw = held([P, PASSES, H], I32, "wk_raw", "wl_raw0")
-        nc.sync.dma_start(wk_raw[:], wk_words.rearrange("a p r i -> p a (r i)").bitcast(I32))
-        wo_bf = held([P, 4 * N], BF16, "wo_bf")
-        wo_sc = held([P, N], U8, "wo_sc")
+        key_sc = [held([P, HALF], U8, "key_sc0")]
+        gather_scales(key_sc[0][:], list_k, 0, HALF)
+
+        def mx(acc, a, lhs, lhs_sc, rhs, rhs_sc):
+            nc.tensor.matmul_mx(
+                out=acc, lhsT=lhs, lhsT_scale=lhs_sc, rhs=rhs, rhs_scale=rhs_sc, start=(a == 0), stop=(a == PASSES - 1)
+            )
+
+        def right_pass(acc, a, t, words, j0):
+            mx(
+                acc,
+                a,
+                wr_w[:, a, t, :].bitcast(FP4X4),
+                wr_sc[:, a, t, :],
+                words.bitcast(FP8X4),
+                right_planes[a][:, j0 : j0 + HALF],
+            )
+
+        b_first = [upper([P, HALF], "b_first%d" % t, t) for t in range(4)]
+        for t in range(4):
+            right_pass(b_first[t][:], 0, t, right[0][:, :HALF], 0)
+
+        wl_w = held([P, PASSES, H], U32, "wl_w")
+        wl_sc = held([P, PASSES, H], U8, "wl_sc")
+        wl_bf = [held([P, 4, 4 * P], BF16, "wl_bf%d" % a) for a in range(PASSES)]
+        for a in range(PASSES):
+            dst = wl_bf[a][:].rearrange("p t (b y e j) -> p y t b j e", y=2, e=4, j=4)
+            src = wl_raw[a][:].rearrange("p j (b t y e) -> p y t b j e", t=4, y=2, e=4)
+            for y in range(2):
+                nc.scalar.copy(dst[:, y], src[:, y])
+            nc.vector.quantize_mx(
+                out=wl_w[:, a, :].bitcast(FP8X4), scales=wl_sc[:, a, :], in_=wl_bf[a][:].rearrange("p t x -> p (t x)")
+            )
         nc.scalar.copy(
             wo_bf[:].rearrange("p (c i t) -> p c t i", i=4, t=4),
             wo_raw[:].rearrange("p t (c i) -> p c t i", i=4),
         )
+
+        left1 = [held([P, HALF], U32, "left1_0"), placed([P, HALF], U32, "left1_1", 0)]
+        right1 = [placed([P, HALF], U32, "right1_0", 6144), placed([P, HALF], U32, "right1_1", 2048)]
         for half in range(2):
-            j0 = half * HALF
-            left1 = gather_words("left1_%d" % half, list_l, 1, j0, j0 + HALF, (None, "wl_bf1")[half])
-            width = (HALF, QUARTER)[half]
-            for c0 in range(0, HALF, width):
-                left_product(j0 + c0, width, [left0[:, j0 + c0 : j0 + c0 + width], left1[:, c0 : c0 + width]])
-            right1 = gather_words("right1_%d" % half, list_r, 1, j0, j0 + HALF)
-            right_product(half, [right0[:, j0 : j0 + HALF], right1[:]])
-        for q in POOL_COLS:
-            apply_gain(q)
-        key_sc.append(gather_scales("key_sc1", list_k, HALF, S, "left1_0"))
-        key = [held([P, S], U32, "key%d" % a, ("right1_0", "wl_bf1")[a]) for a in range(PASSES)]
+            gather_words(left1[half][:], list_l, 1, half * HALF, (half + 1) * HALF)
+            gather_words(right1[half][:], list_r, 1, half * HALF, (half + 1) * HALF)
 
-        def gather_key(a, j0, j1):
-            nc.vector.tensor_copy(key[a][:, j0:j1], tab_w[a][:].bitcast(U32).indirect(list_k[:, j0 // 16 : j1 // 16]))
+        a_first = [bank([P, H], jb) for jb in range(4)]
+        tanh_turned = held([P, 4, H], F32, "tanh_turned", "wo_raw")
+        for a in range(PASSES):
+            for jb in range(4):
+                cols = slice(jb * P, (jb + 1) * P)
+                mx(
+                    a_first[jb][:],
+                    a,
+                    (left[0], left1[0])[a][:, cols].bitcast(FP8X4),
+                    left_sc[4 * a : P, cols],
+                    wl_w[:, a, :].bitcast(FP8X4),
+                    wl_sc[:, a, :],
+                )
+        for jb in range(4):
+            nc.scalar.activation(tanh_turned[:, jb, :], a_first[jb][:], ACT.Tanh)
+        tanh_b = [held([P, 4, HALF], F32, "tanh_b%d" % half) for half in range(2)]
+        for t in range(4):
+            right_pass(b_first[t][:], 1, t, right1[0][:], 0)
+            nc.scalar.activation(tanh_b[0][:, t, :], b_first[t][:], ACT.Tanh)
 
-        gather_key(0, 0, S)
+        tanh_a, gained, agree = {}, {}, {}
+
+        def left_quarter(q, first_bank):
+            j0 = q * QUARTER
+            tanh_a[q] = held([P, 4 * QUARTER], F32, "tanh_a%d" % q)
+            words = [left[0][:, j0 : j0 + QUARTER], left1[1][:, j0 - HALF : j0 - HALF + QUARTER]]
+            for pair in range(2):
+                acc = bank([P, 2, QUARTER], first_bank + pair)
+                for i in range(2):
+                    cols = slice((2 * pair + i) * P, (2 * pair + i + 1) * P)
+                    for a in range(PASSES):
+                        mx(
+                            acc[:, i, :],
+                            a,
+                            wl_w[:, a, cols].bitcast(FP8X4),
+                            wl_sc[:, a, cols],
+                            words[a].bitcast(FP8X4),
+                            left_sc[4 * a : P, j0 : j0 + QUARTER],
+                        )
+                nc.scalar.activation(
+                    tanh_a[q][:, pair * HALF : (pair + 1) * HALF], acc[:].rearrange("p t c -> p (t c)"), ACT.Tanh
+                )
+
+        def apply_gain(q):
+            c0 = q * QUARTER - HALF
+            gained[q] = held([P, 4 * QUARTER], F32, "gained%d" % q)
+            for t in range(4):
+                nc.scalar.activation(
+                    gained[q][:, t * QUARTER : (t + 1) * QUARTER],
+                    tanh_b[1][:, t, c0 : c0 + QUARTER],
+                    ACT.Copy,
+                    scale=gain[:, t, 0:1],
+                )
+
+        left_quarter(2, 0)
+        for t in range(4):
+            acc = bank([P, HALF], (t + 2) % 4)
+            for a in range(PASSES):
+                right_pass(acc[:], a, t, (right[0][:, HALF:], right1[1][:])[a], HALF)
+            nc.scalar.activation(tanh_b[1][:, t, :], acc[:], ACT.Tanh)
+        tanh_a_first = upper([P, 4, HALF], "tanh_a_first", 0)
+        for t in range(4):
+            for jb in range(4):
+                nc.tensor.transpose(
+                    tanh_a_first[:, t, jb * P : (jb + 1) * P], tanh_turned[:, jb, t * P : (t + 1) * P], ident[:]
+                )
+        apply_gain(2)
+        left_quarter(3, 2)
+        apply_gain(3)
+
+        key_sc.append(held([P, HALF], U8, "key_sc1", "wl_bf1"))
+        gather_scales(key_sc[1][:], list_k, HALF, S)
+        wo_w = held([P, N], U32, "wo_w")
+        wo_sc = held([P, N], U8, "wo_sc")
+        nc.vector.quantize_mx(out=wo_w[:].bitcast(FP8X4), scales=wo_sc[:], in_=wo_bf[:])
         wk_w = held([P, PASSES, 4, P], I32, "wk_w")
         nc.vector.tensor_copy(
             wk_w[:].rearrange("p a t (b e) -> p a t b e", e=8),
@@ -293,30 +253,102 @@ def tile_list_record_match_scores_kernel(
         wk_sc = held([P, 4, P], U8, "wk_sc")
         nc.vector.tensor_copy(
             wk_sc[:].bitcast(I32).rearrange("p t (b w) -> p t b w", w=2),
-            wk_sc_raw.rearrange("p (b t w) -> p t b w", t=4, w=2),
+            wk_sc_raw[:].rearrange("p (b t w) -> p t b w", t=4, w=2),
         )
-        gather_key(1, 0, QUARTER)
-        gather_key(1, QUARTER, S)
-        agreement(0, HALF, "right0")
-        wo_w = held([P, N], U32, "wo_w", "tanh_b02")
-        nc.vector.quantize_mx(out=wo_w[:].bitcast(FP8X4), scales=wo_sc[:], in_=wo_bf[:])
+        key = [held([P, S], U32, "key0", "left1_0"), placed([P, S], U32, "key1", 6144)]
+        gather_words(key[0][:], list_k, 0, 0, S)
+        gather_words(key[1][:, :QUARTER], list_k, 1, 0, QUARTER)
+        gather_words(key[1][:, QUARTER:], list_k, 1, QUARTER, S)
+
+        agree[512] = placed([P, 4 * QUARTER], F32, "agree512", 17920)
+        nc.gpsimd.tensor_tensor(agree[512][:], tanh_a[2][:], gained[2][:], ALU.mult)
+        agree[768] = held([P, 4 * QUARTER], F32, "agree768")
+        nc.gpsimd.tensor_tensor(agree[768][:], tanh_a[3][:], gained[3][:], ALU.mult)
+
+        agree[0] = held([P, 4 * HALF], F32, "agree0")
+        for t in range(4):
+            nc.vector.scalar_tensor_tensor(
+                agree[0][:, t * HALF : (t + 1) * HALF],
+                tanh_b[0][:, t, :],
+                gain[:, t, 0:1],
+                tanh_a_first[:, t, :],
+                ALU.mult,
+                ALU.mult,
+            )
+
+        early = HALF + P
+        h_bf = [held([P, 4 * early], BF16, "h_bf0"), held([P, 4 * (S - early)], BF16, "h_bf1", "tanh_a3")]
+        h_w = [held([P, early], U32, "h_w0", "gained3"), held([P, S - early], U32, "h_w1")]
+        h_sc = held([P, S], U8, "h_sc")
+        out_v = out.rearrange("(m p) j -> p m j", p=P)
+
+        def h_words(j0, j1):
+            return h_w[j0 // early][:, j0 % early : j0 % early + j1 - j0].bitcast(FP8X4)
+
+        def h_values(j0, j1):
+            return h_bf[j0 // early][:, 4 * (j0 % early) : 4 * (j0 % early + j1 - j0)]
+
+        def quantize_h(j0, j1):
+            nc.vector.quantize_mx(out=h_words(j0, j1), scales=h_sc[:, j0:j1], in_=h_values(j0, j1))
+
+        def score(j0, j1, number):
+            width = j1 - j0
+            acc = upper([P, 2, width], "score%d" % j0, number)
+            for m in range(2):
+                nc.tensor.matmul_mx(
+                    out=acc[:, m, :],
+                    lhsT=wo_w[:, m * P : (m + 1) * P].bitcast(FP8X4),
+                    lhsT_scale=wo_sc[:, m * P : (m + 1) * P],
+                    rhs=h_words(j0, j1),
+                    rhs_scale=h_sc[:, j0:j1],
+                    start=True,
+                    stop=True,
+                )
+            res = res_pool.tile([P, 2, width], F32, name="res")
+            nc.scalar.copy(res[:], acc[:])
+            (nc.scalar if j1 == S else nc.sync).dma_start(out_v[:, :, j0:j1], res[:])
+
+        key_sum = {}
+
+        def subtract_key(j0, start, width=P):
+            b0 = j0 % P
+            if b0 == 0:
+                key_sum[j0] = bank([P, 4, P], j0 // P % 4)
+                for t in range(4):
+                    for a in range(PASSES):
+                        mx(
+                            key_sum[j0][:, t, :],
+                            a,
+                            wk_w[:, a, t, :].bitcast(FP8X4),
+                            wk_sc[4 * a : P, t, :],
+                            key[a][:, j0 : j0 + P].bitcast(FP8X4),
+                            key_sc[j0 // HALF][4 * a : P, j0 % HALF : j0 % HALF + P],
+                        )
+            c0 = j0 - start
+            nc.vector.tensor_tensor(
+                h_values(j0, j0 + width).rearrange("p (c i t) -> p c t i", i=2, t=4),
+                agree[start][:].rearrange("p (t c) -> p t c", t=4)[:, :, c0 : c0 + width].rearrange("p t (c i) -> p c t i", i=2),
+                key_sum[j0 - b0][:, :, b0 : b0 + width].rearrange("p t (c i) -> p c t i", i=2),
+                ALU.subtract,
+            )
+
         for j0 in range(0, HALF, P):
             subtract_key(j0, 0)
-        agreement(512, QUARTER, "wo_raw")
+        subtract_key(512, 512)
         quantize_h(0, 512)
-        score(0, 256, 4)
-        score(256, 512, 5)
-        for j0 in (512, 640):
-            subtract_key(j0, 512)
-        agreement(768, QUARTER, "tanh_a512")
-        quantize_h(512, 768)
-        score(512, 768, 6)
+        score(0, 256, 0)
+        score(256, 512, 1)
+        subtract_key(640, 512)
+        quantize_h(512, 640)
+        score(512, 640, 2)
         subtract_key(768, 768)
+        quantize_h(640, 768)
+        score(640, 768, 3)
         subtract_key(896, 768, 64)
         quantize_h(768, 896)
-        score(768, 896, 7)
+        score(768, 896, 0)
         subtract_key(960, 768, 64)
         quantize_h(896, 960)
-        score(896, 960, 4)
+        score(896, 960, 1)
         quantize_h(960, 1024)
-        score(960, 1024, 5)
+        score(960, 1024, 2)

@@ -50,20 +50,20 @@ def tile_list_record_match_scores_kernel(
         list_r = keep.tile([P, S // 16], U16, name="list_r")
         list_k = keep.tile([P, S // 16], U16, name="list_k")
         tab_sc = held([P, T // 4], I32, "tab_sc")
-        tab_w = [held([P, T], I32, "tab_w0"), placed([P, T], I32, "tab_w1", 10240)]
+        tab_w = [held([P, T], I32, "tab_w0"), placed([P, T], I32, "tab_w1", 27648)]
         wo_raw = held([P, 4, N], F32, "wo_raw")
-        wr_raw = held([P, PASSES, H // 2], I32, "wr_raw")
-        wr_sc_raw = held([P, PASSES, H // 4], I32, "wr_sc_raw")
-        wl_raw = [held([P, 4, H], F32, "wl_raw0"), placed([P, 4, H], F32, "wl_raw1", 0)]
+        wr_w = held([P, PASSES, 2 * H], U8, "wr_w")
+        wr_sc = held([P, PASSES, H], U8, "wr_sc")
+        wl_raw = [held([P, 4, H], F32, "wl_raw0"), placed([P, 4, H], F32, "wl_raw1", 15872)]
         right_sc1 = held([P, S // 4], I32, "right_sc1")
-        wk_sc_raw = placed([P, H // 4], I32, "wk_sc_raw", 18432)
-        wo_bf = placed([P, 4 * N], BF16, "wo_bf", 18944)
-        wk_raw = placed([P, PASSES, H], I32, "wk_raw", 20992)
+        wk_sc_raw = placed([P, H // 4], I32, "wk_sc_raw", 35840)
+        wo_bf = placed([P, 4 * N], BF16, "wo_bf", 36352)
+        wk_raw = placed([P, PASSES, H], I32, "wk_raw", 38400)
         gain = held([P, 4, 8], F32, "gain")
         ident = held([P, P], F32, "ident")
 
         nc.vector.memset(tab_sc[:], 0)
-        nc.vector.memset(wr_sc_raw[:], 0)
+        nc.vector.memset(wr_sc[:].bitcast(I32), 0)
         nc.vector.memset(right_sc1[:], 0)
         nc.vector.memset(wk_sc_raw[:], 0)
         make_identity(nc, ident[:])
@@ -75,22 +75,17 @@ def tile_list_record_match_scores_kernel(
             nc.sync.dma_start(wl_raw[a][:], wl[512 * a : 512 * (a + 1), :].rearrange("(p j) r -> p j r", j=4))
 
         nc.sync.dma_start(list_r[:], offs2)
-        nc.sync.dma_start(wr_raw[:], wr_words.bitcast(I32).rearrange("a p w -> p a w"))
         nc.sync.dma_start(list_l[:], offs)
         for q in range(4):
             nc.sync.dma_start(tab_sc[32 * q : 32 * q + 8, :], tab_scales[:, 4 * q : 4 * q + 4, :].bitcast(I32))
         load_table(0)
+        nc.sync.dma_start(wr_w[:].bitcast(I32), wr_words.bitcast(I32).rearrange("a p w -> p a w"))
         for q in range(4):
             nc.sync.dma_start(
-                wr_sc_raw[32 * q : 32 * q + 4, :, :],
+                wr_sc[32 * q : 32 * q + 4, :, :].bitcast(I32),
                 wr_scales[:, 4 * q : 4 * q + 4, :].bitcast(I32).rearrange("a r w -> r a w"),
             )
-        nc.sync.dma_start(list_k[:], offs3)
-        load_wl(0)
-        load_wl(1)
         load_table(1)
-        for t in range(4):
-            nc.sync.dma_start(wo_raw[:, t, :], wo.rearrange("(b t e) n -> t b e n", t=4, e=8)[t])
 
         def gather_scales(dst, lst, j0, j1):
             nc.vector.tensor_copy(dst, tab_sc[:].bitcast(U8).indirect(lst[:, j0 // 16 : j1 // 16]))
@@ -98,12 +93,6 @@ def tile_list_record_match_scores_kernel(
         def gather_words(dst, lst, a, j0, j1):
             nc.vector.tensor_copy(dst, tab_w[a][:].bitcast(U32).indirect(lst[:, j0 // 16 : j1 // 16]))
 
-        wr_w = held([P, PASSES, 4, 2 * P], U8, "wr_w")
-        wr_sc = held([P, PASSES, 4, P], U8, "wr_sc")
-        nc.vector.tensor_copy(
-            wr_w[:].bitcast(I32).rearrange("p a t (b w) -> p a t b w", w=4),
-            wr_raw[:].rearrange("p a (b t w) -> p a t b w", t=4, w=4),
-        )
         right_sc = held([P, S], U8, "right_sc")
         left_sc = held([P, S], U8, "left_sc")
         gather_scales(right_sc[:], list_r, 0, S)
@@ -111,46 +100,37 @@ def tile_list_record_match_scores_kernel(
         right_planes = [right_sc[:], right_sc1[:].bitcast(U8)]
         for q in range(4):
             nc.sync.dma_start(right_sc1[32 * q : 32 * q + 4, :], right_sc[32 * q + 4 : 32 * q + 8, :].bitcast(I32))
+        load_wl(0)
+        load_wl(1)
+        nc.sync.dma_start(list_k[:], offs3)
         nc.sync.dma_start(wk_raw[:], wk_words.rearrange("a p r i -> p a (r i)").bitcast(I32))
         for q in range(4):
             nc.sync.dma_start(wk_sc_raw[32 * q : 32 * q + 8, :], wk_scales[:, 4 * q : 4 * q + 4, :].bitcast(I32))
+        for t in range(4):
+            nc.sync.dma_start(wo_raw[:, t, :], wo.rearrange("(b t e) n -> t b e n", t=4, e=8)[t])
         with nc.allow_non_contiguous_dma(reason="one gain to a partition"):
             for t in range(4):
                 nc.sync.dma_start(gain[:, t, 0:1], g.rearrange("(b t e) -> t b e", t=4, e=8)[t])
 
-        left = [held([P, S], U32, "left0")]
-        right = [held([P, S], U32, "right0")]
-        gather_words(left[0][:], list_l, 0, 0, S)
+        left0 = held([P, S], U32, "left0")
+        right = [held([P, S], U32, "right%d" % a) for a in range(PASSES)]
+        left1 = [held([P, HALF], U32, "left1_0"), placed([P, HALF], U32, "left1_1", 16384)]
         gather_words(right[0][:], list_r, 0, 0, S)
-        nc.vector.tensor_copy(
-            wr_sc[:].bitcast(I32).rearrange("p a t (b w) -> p a t b w", w=2),
-            wr_sc_raw[:].rearrange("p a (b t w) -> p a t b w", t=4, w=2),
-        )
-        key_sc = [held([P, HALF], U8, "key_sc0")]
-        gather_scales(key_sc[0][:], list_k, 0, HALF)
+        gather_words(left0[:], list_l, 0, 0, S)
+        for half in range(2):
+            gather_words(right[1][:, half * HALF : (half + 1) * HALF], list_r, 1, half * HALF, (half + 1) * HALF)
+        gather_words(left1[0][:], list_l, 1, 0, HALF)
 
         def mx(acc, a, lhs, lhs_sc, rhs, rhs_sc):
             nc.tensor.matmul_mx(
                 out=acc, lhsT=lhs, lhsT_scale=lhs_sc, rhs=rhs, rhs_scale=rhs_sc, start=(a == 0), stop=(a == PASSES - 1)
             )
 
-        def right_pass(acc, a, t, words, j0):
-            mx(
-                acc,
-                a,
-                wr_w[:, a, t, :].bitcast(FP4X4),
-                wr_sc[:, a, t, :],
-                words.bitcast(FP8X4),
-                right_planes[a][:, j0 : j0 + HALF],
-            )
-
-        b_first = [upper([P, HALF], "b_first%d" % t, t) for t in range(4)]
-        for t in range(4):
-            right_pass(b_first[t][:], 0, t, right[0][:, :HALF], 0)
-
         wl_w = held([P, PASSES, H], U32, "wl_w")
         wl_sc = held([P, PASSES, H], U8, "wl_sc")
         wl_bf = [held([P, 4, 4 * P], BF16, "wl_bf%d" % a) for a in range(PASSES)]
+        wk_w = held([P, PASSES, 4, P], I32, "wk_w")
+        wk_sc = held([P, 4, P], U8, "wk_sc")
         for a in range(PASSES):
             dst = wl_bf[a][:].rearrange("p t (b y e j) -> p y t b j e", y=2, e=4, j=4)
             src = wl_raw[a][:].rearrange("p j (b t y e) -> p y t b j e", t=4, y=2, e=4)
@@ -159,108 +139,100 @@ def tile_list_record_match_scores_kernel(
             nc.vector.quantize_mx(
                 out=wl_w[:, a, :].bitcast(FP8X4), scales=wl_sc[:, a, :], in_=wl_bf[a][:].rearrange("p t x -> p (t x)")
             )
+        gather_words(left1[1][:], list_l, 1, HALF, S)
+
+        b_acc = [upper([P, H], "b_first%d" % jb, jb) for jb in range(4)] + [bank([P, H], jb) for jb in range(4)]
+        tanh_turned = placed([P, 8, H], F32, "tanh_turned", 0)
+        for a in range(PASSES):
+            for jb in range(8):
+                cols = slice(jb * P, (jb + 1) * P)
+                mx(
+                    b_acc[jb][:],
+                    a,
+                    right[a][:, cols].bitcast(FP8X4),
+                    right_planes[a][:, cols],
+                    wr_w[:, a, :].bitcast(FP4X4),
+                    wr_sc[:, a, :],
+                )
+        for jb in range(8):
+            nc.scalar.activation(
+                tanh_turned[:, jb, :].rearrange("p (t b e) -> p t b e", t=4, e=8),
+                b_acc[jb][:].rearrange("p (b t e) -> p t b e", t=4, e=8),
+                ACT.Tanh,
+            )
         nc.scalar.copy(
             wo_bf[:].rearrange("p (c i t) -> p c t i", i=4, t=4),
             wo_raw[:].rearrange("p t (c i) -> p c t i", i=4),
         )
 
-        left1 = [held([P, HALF], U32, "left1_0"), placed([P, HALF], U32, "left1_1", 0)]
-        right1 = [placed([P, HALF], U32, "right1_0", 6144), placed([P, HALF], U32, "right1_1", 2048)]
-        for half in range(2):
-            gather_words(left1[half][:], list_l, 1, half * HALF, (half + 1) * HALF)
-            gather_words(right1[half][:], list_r, 1, half * HALF, (half + 1) * HALF)
+        def turn(dst, t, jb):
+            nc.tensor.transpose(dst, tanh_turned[:, jb, t * P : (t + 1) * P], ident[:])
 
-        a_first = [bank([P, H], jb) for jb in range(4)]
-        tanh_turned = held([P, 4, H], F32, "tanh_turned", "wo_raw")
-        for a in range(PASSES):
-            for jb in range(4):
-                cols = slice(jb * P, (jb + 1) * P)
-                mx(
-                    a_first[jb][:],
-                    a,
-                    (left[0], left1[0])[a][:, cols].bitcast(FP8X4),
-                    left_sc[4 * a : P, cols],
-                    wl_w[:, a, :].bitcast(FP8X4),
-                    wl_sc[:, a, :],
-                )
-        for jb in range(4):
-            nc.scalar.activation(tanh_turned[:, jb, :], a_first[jb][:], ACT.Tanh)
-        tanh_b = [held([P, 4, HALF], F32, "tanh_b%d" % half) for half in range(2)]
+        tanh_b_first = upper([P, 4, HALF], "tanh_b_first", 0)
         for t in range(4):
-            right_pass(b_first[t][:], 1, t, right1[0][:], 0)
-            nc.scalar.activation(tanh_b[0][:, t, :], b_first[t][:], ACT.Tanh)
+            for jb in range(4):
+                turn(tanh_b_first[:, t, jb * P : (jb + 1) * P], t, jb)
+
+        def left_product(acc, t, j0, width):
+            cols = slice(t * P, (t + 1) * P)
+            words = [left0[:, j0 : j0 + width], left1[j0 // HALF][:, j0 % HALF : j0 % HALF + width]]
+            for a in range(PASSES):
+                mx(
+                    acc,
+                    a,
+                    wl_w[:, a, cols].bitcast(FP8X4),
+                    wl_sc[:, a, cols],
+                    words[a].bitcast(FP8X4),
+                    left_sc[4 * a : P, j0 : j0 + width],
+                )
+
+        tanh_a_first = held([P, 4, HALF], F32, "tanh_a_first")
+        for t in range(4):
+            acc = bank([P, HALF], t)
+            left_product(acc[:], t, 0, HALF)
+            nc.scalar.activation(tanh_a_first[:, t, :], acc[:], ACT.Tanh)
 
         tanh_a, gained, agree = {}, {}, {}
-
-        def left_quarter(q, first_bank):
-            j0 = q * QUARTER
-            tanh_a[q] = held([P, 4 * QUARTER], F32, "tanh_a%d" % q)
-            words = [left[0][:, j0 : j0 + QUARTER], left1[1][:, j0 - HALF : j0 - HALF + QUARTER]]
+        for q in (2, 3):
+            gained[q] = held([P, 4 * QUARTER], F32, "gained%d" % q)
             for pair in range(2):
-                acc = bank([P, 2, QUARTER], first_bank + pair)
+                acc = bank([P, 2, QUARTER], pair)
                 for i in range(2):
-                    cols = slice((2 * pair + i) * P, (2 * pair + i + 1) * P)
-                    for a in range(PASSES):
-                        mx(
-                            acc[:, i, :],
-                            a,
-                            wl_w[:, a, cols].bitcast(FP8X4),
-                            wl_sc[:, a, cols],
-                            words[a].bitcast(FP8X4),
-                            left_sc[4 * a : P, j0 : j0 + QUARTER],
-                        )
+                    for half in range(2):
+                        turn(acc[:, i, half * P : (half + 1) * P], 2 * pair + i, 2 * q + half)
+                for i in range(2):
+                    t = 2 * pair + i
+                    nc.scalar.activation(
+                        gained[q][:, t * QUARTER : (t + 1) * QUARTER], acc[:, i, :], ACT.Copy, scale=gain[:, t, 0:1]
+                    )
+            tanh_a[q] = held([P, 4 * QUARTER], F32, "tanh_a%d" % q)
+            for pair in range(2):
+                acc = bank([P, 2, QUARTER], 2 + pair)
+                for i in range(2):
+                    left_product(acc[:, i, :], 2 * pair + i, q * QUARTER, QUARTER)
                 nc.scalar.activation(
                     tanh_a[q][:, pair * HALF : (pair + 1) * HALF], acc[:].rearrange("p t c -> p (t c)"), ACT.Tanh
                 )
 
-        def apply_gain(q):
-            c0 = q * QUARTER - HALF
-            gained[q] = held([P, 4 * QUARTER], F32, "gained%d" % q)
-            for t in range(4):
-                nc.scalar.activation(
-                    gained[q][:, t * QUARTER : (t + 1) * QUARTER],
-                    tanh_b[1][:, t, c0 : c0 + QUARTER],
-                    ACT.Copy,
-                    scale=gain[:, t, 0:1],
-                )
-
-        left_quarter(2, 0)
-        for t in range(4):
-            acc = bank([P, HALF], (t + 2) % 4)
-            for a in range(PASSES):
-                right_pass(acc[:], a, t, (right[0][:, HALF:], right1[1][:])[a], HALF)
-            nc.scalar.activation(tanh_b[1][:, t, :], acc[:], ACT.Tanh)
-        tanh_a_first = upper([P, 4, HALF], "tanh_a_first", 0)
-        for t in range(4):
-            for jb in range(4):
-                nc.tensor.transpose(
-                    tanh_a_first[:, t, jb * P : (jb + 1) * P], tanh_turned[:, jb, t * P : (t + 1) * P], ident[:]
-                )
-        apply_gain(2)
-        left_quarter(3, 2)
-        apply_gain(3)
-
-        key_sc.append(held([P, HALF], U8, "key_sc1", "wl_bf1"))
-        gather_scales(key_sc[1][:], list_k, HALF, S)
-        wo_w = held([P, N], U32, "wo_w")
-        wo_sc = held([P, N], U8, "wo_sc")
-        nc.vector.quantize_mx(out=wo_w[:].bitcast(FP8X4), scales=wo_sc[:], in_=wo_bf[:])
-        wk_w = held([P, PASSES, 4, P], I32, "wk_w")
         nc.vector.tensor_copy(
             wk_w[:].rearrange("p a t (b e) -> p a t b e", e=8),
             wk_raw[:].rearrange("p a (b t e) -> p a t b e", t=4, e=8),
         )
-        wk_sc = held([P, 4, P], U8, "wk_sc")
         nc.vector.tensor_copy(
             wk_sc[:].bitcast(I32).rearrange("p t (b w) -> p t b w", w=2),
             wk_sc_raw[:].rearrange("p (b t w) -> p t b w", t=4, w=2),
         )
-        key = [held([P, S], U32, "key0", "left1_0"), placed([P, S], U32, "key1", 6144)]
+        key_sc = placed([P, S], U8, "key_sc", 18432)
+        gather_scales(key_sc[:], list_k, 0, S)
+        wo_w = held([P, N], U32, "wo_w")
+        wo_sc = held([P, N], U8, "wo_sc")
+        nc.vector.quantize_mx(out=wo_w[:].bitcast(FP8X4), scales=wo_sc[:], in_=wo_bf[:])
+        key = [placed([P, S], U32, "key0", 19456), placed([P, S], U32, "key1", 23552)]
         gather_words(key[0][:], list_k, 0, 0, S)
         gather_words(key[1][:, :QUARTER], list_k, 1, 0, QUARTER)
         gather_words(key[1][:, QUARTER:], list_k, 1, QUARTER, S)
 
-        agree[512] = placed([P, 4 * QUARTER], F32, "agree512", 17920)
+        agree[512] = placed([P, 4 * QUARTER], F32, "agree512", 35328)
         nc.gpsimd.tensor_tensor(agree[512][:], tanh_a[2][:], gained[2][:], ALU.mult)
         agree[768] = held([P, 4 * QUARTER], F32, "agree768")
         nc.gpsimd.tensor_tensor(agree[768][:], tanh_a[3][:], gained[3][:], ALU.mult)
@@ -269,9 +241,9 @@ def tile_list_record_match_scores_kernel(
         for t in range(4):
             nc.vector.scalar_tensor_tensor(
                 agree[0][:, t * HALF : (t + 1) * HALF],
-                tanh_b[0][:, t, :],
-                gain[:, t, 0:1],
                 tanh_a_first[:, t, :],
+                gain[:, t, 0:1],
+                tanh_b_first[:, t, :],
                 ALU.mult,
                 ALU.mult,
             )
@@ -322,7 +294,7 @@ def tile_list_record_match_scores_kernel(
                             wk_w[:, a, t, :].bitcast(FP8X4),
                             wk_sc[4 * a : P, t, :],
                             key[a][:, j0 : j0 + P].bitcast(FP8X4),
-                            key_sc[j0 // HALF][4 * a : P, j0 % HALF : j0 % HALF + P],
+                            key_sc[4 * a : P, j0 : j0 + P],
                         )
             c0 = j0 - start
             nc.vector.tensor_tensor(

@@ -57,15 +57,16 @@ def tile_list_record_match_scores_kernel(
         wl_raw = [held([P, 4, H], F32, "wl_raw0"), placed([P, 4, H], F32, "wl_raw1", 15872)]
         right_sc1 = held([P, S // 4], I32, "right_sc1")
         wk_sc_raw = placed([P, H // 4], I32, "wk_sc_raw", 35840)
-        wo_bf = placed([P, 4 * N], BF16, "wo_bf", 36352)
         wk_raw = placed([P, PASSES, H], I32, "wk_raw", 38400)
         gain = held([P, 4, 8], F32, "gain")
         ident = held([P, P], F32, "ident")
+        gain_rows = held([P, P], F32, "gain_rows")
 
         nc.vector.memset(tab_sc[:], 0)
         nc.vector.memset(wr_sc[:].bitcast(I32), 0)
         nc.vector.memset(right_sc1[:], 0)
         nc.vector.memset(wk_sc_raw[:], 0)
+        nc.vector.memset(gain_rows[:], 0)
         make_identity(nc, ident[:])
 
         def load_table(a):
@@ -75,9 +76,9 @@ def tile_list_record_match_scores_kernel(
             nc.sync.dma_start(wl_raw[a][:], wl[512 * a : 512 * (a + 1), :].rearrange("(p j) r -> p j r", j=4))
 
         nc.sync.dma_start(list_r[:], offs2)
-        nc.sync.dma_start(list_l[:], offs)
         for q in range(4):
             nc.sync.dma_start(tab_sc[32 * q : 32 * q + 8, :], tab_scales[:, 4 * q : 4 * q + 4, :].bitcast(I32))
+        nc.sync.dma_start(list_l[:], offs)
         load_table(0)
         nc.sync.dma_start(wr_w[:].bitcast(I32), wr_words.bitcast(I32).rearrange("a p w -> p a w"))
         for q in range(4):
@@ -108,18 +109,18 @@ def tile_list_record_match_scores_kernel(
             nc.sync.dma_start(wk_sc_raw[32 * q : 32 * q + 8, :], wk_scales[:, 4 * q : 4 * q + 4, :].bitcast(I32))
         for t in range(4):
             nc.sync.dma_start(wo_raw[:, t, :], wo.rearrange("(b t e) n -> t b e n", t=4, e=8)[t])
+        nc.sync.dma_start(
+            gain_rows[0:4, :].rearrange("t (b e) -> t b e", e=8), g.rearrange("(b t e) -> t b e", t=4, e=8)
+        )
         with nc.allow_non_contiguous_dma(reason="one gain to a partition"):
             for t in range(4):
                 nc.sync.dma_start(gain[:, t, 0:1], g.rearrange("(b t e) -> t b e", t=4, e=8)[t])
 
-        left0 = held([P, S], U32, "left0")
+        left = [held([P, S], U32, "left%d" % a) for a in range(PASSES)]
         right = [held([P, S], U32, "right%d" % a) for a in range(PASSES)]
-        left1 = [held([P, HALF], U32, "left1_0"), placed([P, HALF], U32, "left1_1", 16384)]
-        gather_words(right[0][:], list_r, 0, 0, S)
-        gather_words(left0[:], list_l, 0, 0, S)
-        for half in range(2):
-            gather_words(right[1][:, half * HALF : (half + 1) * HALF], list_r, 1, half * HALF, (half + 1) * HALF)
-        gather_words(left1[0][:], list_l, 1, 0, HALF)
+        for a in range(PASSES):
+            gather_words(right[a][:], list_r, a, 0, S)
+            gather_words(left[a][:], list_l, a, 0, S)
 
         def mx(acc, a, lhs, lhs_sc, rhs, rhs_sc):
             nc.tensor.matmul_mx(
@@ -139,35 +140,35 @@ def tile_list_record_match_scores_kernel(
             nc.vector.quantize_mx(
                 out=wl_w[:, a, :].bitcast(FP8X4), scales=wl_sc[:, a, :], in_=wl_bf[a][:].rearrange("p t x -> p (t x)")
             )
-        gather_words(left1[1][:], list_l, 1, HALF, S)
 
-        b_acc = [upper([P, H], "b_first%d" % jb, jb) for jb in range(4)] + [bank([P, H], jb) for jb in range(4)]
         tanh_turned = placed([P, 8, H], F32, "tanh_turned", 0)
-        for a in range(PASSES):
-            for jb in range(8):
-                cols = slice(jb * P, (jb + 1) * P)
-                mx(
-                    b_acc[jb][:],
-                    a,
-                    right[a][:, cols].bitcast(FP8X4),
-                    right_planes[a][:, cols],
-                    wr_w[:, a, :].bitcast(FP4X4),
-                    wr_sc[:, a, :],
-                )
-        for jb in range(8):
-            nc.scalar.activation(
-                tanh_turned[:, jb, :].rearrange("p (t b e) -> p t b e", t=4, e=8),
-                b_acc[jb][:].rearrange("p (b t e) -> p t b e", t=4, e=8),
-                ACT.Tanh,
+
+        def right_pass(acc, a, jb):
+            cols = slice(jb * P, (jb + 1) * P)
+            mx(
+                acc[:],
+                a,
+                right[a][:, cols].bitcast(FP8X4),
+                right_planes[a][:, cols],
+                wr_w[:, a, :].bitcast(FP4X4),
+                wr_sc[:, a, :],
             )
-        nc.scalar.copy(
-            wo_bf[:].rearrange("p (c i t) -> p c t i", i=4, t=4),
-            wo_raw[:].rearrange("p t (c i) -> p c t i", i=4),
-        )
+
+        def right_blocks(accs, first):
+            for a in range(PASSES):
+                for i, acc in enumerate(accs):
+                    right_pass(acc, a, first + i)
+            for i, acc in enumerate(accs):
+                nc.scalar.activation(
+                    tanh_turned[:, first + i, :].rearrange("p (t b e) -> p t b e", t=4, e=8),
+                    acc[:].rearrange("p (b t e) -> p t b e", t=4, e=8),
+                    ACT.Tanh,
+                )
 
         def turn(dst, t, jb):
             nc.tensor.transpose(dst, tanh_turned[:, jb, t * P : (t + 1) * P], ident[:])
 
+        right_blocks([upper([P, H], "b_first%d" % jb, jb) for jb in range(4)] + [bank([P, H], i) for i in range(4)], 0)
         tanh_b_first = upper([P, 4, HALF], "tanh_b_first", 0)
         for t in range(4):
             for jb in range(4):
@@ -175,44 +176,58 @@ def tile_list_record_match_scores_kernel(
 
         def left_product(acc, t, j0, width):
             cols = slice(t * P, (t + 1) * P)
-            words = [left0[:, j0 : j0 + width], left1[j0 // HALF][:, j0 % HALF : j0 % HALF + width]]
             for a in range(PASSES):
                 mx(
                     acc,
                     a,
                     wl_w[:, a, cols].bitcast(FP8X4),
                     wl_sc[:, a, cols],
-                    words[a].bitcast(FP8X4),
+                    left[a][:, j0 : j0 + width].bitcast(FP8X4),
                     left_sc[4 * a : P, j0 : j0 + width],
                 )
 
-        tanh_a_first = held([P, 4, HALF], F32, "tanh_a_first")
-        for t in range(4):
-            acc = bank([P, HALF], t)
-            left_product(acc[:], t, 0, HALF)
-            nc.scalar.activation(tanh_a_first[:, t, :], acc[:], ACT.Tanh)
+        tanh_a, agree = {}, {}
+        gained = {2: held([P, 4 * QUARTER], F32, "gained2"), 3: placed([P, 4 * QUARTER], F32, "gained3", 44032)}
 
-        tanh_a, gained, agree = {}, {}, {}
-        for q in (2, 3):
-            gained[q] = held([P, 4 * QUARTER], F32, "gained%d" % q)
-            for pair in range(2):
-                acc = bank([P, 2, QUARTER], pair)
-                for i in range(2):
-                    for half in range(2):
-                        turn(acc[:, i, half * P : (half + 1) * P], 2 * pair + i, 2 * q + half)
-                for i in range(2):
-                    t = 2 * pair + i
-                    nc.scalar.activation(
-                        gained[q][:, t * QUARTER : (t + 1) * QUARTER], acc[:, i, :], ACT.Copy, scale=gain[:, t, 0:1]
-                    )
+        def turn_quarter(q):
+            accs = [bank([P, 2, QUARTER], pair) for pair in range(2)]
+            for t in range(4):
+                for half in range(2):
+                    turn(accs[t // 2][:, t % 2, half * P : (half + 1) * P], t, 2 * q + half)
+            for t in range(4):
+                nc.scalar.activation(
+                    gained[q][:, t * QUARTER : (t + 1) * QUARTER],
+                    accs[t // 2][:, t % 2, :],
+                    ACT.Copy,
+                    scale=gain[:, t, 0:1],
+                )
+
+        def left_quarter(q, banks):
             tanh_a[q] = held([P, 4 * QUARTER], F32, "tanh_a%d" % q)
             for pair in range(2):
-                acc = bank([P, 2, QUARTER], 2 + pair)
+                acc = bank([P, 2, QUARTER], banks[pair])
                 for i in range(2):
                     left_product(acc[:, i, :], 2 * pair + i, q * QUARTER, QUARTER)
                 nc.scalar.activation(
                     tanh_a[q][:, pair * HALF : (pair + 1) * HALF], acc[:].rearrange("p t c -> p (t c)"), ACT.Tanh
                 )
+
+        turn_quarter(2)
+        left_quarter(2, (2, 3))
+        tanh_a_first = held([P, 4, HALF], F32, "tanh_a_first")
+        for t in range(4):
+            acc = bank([P, HALF], t)
+            left_product(acc[:], t, 0, HALF)
+            nc.scalar.activation(tanh_a_first[:, t, :], acc[:], ACT.Tanh)
+        gain_acc = bank([P, P], 3)
+        nc.tensor.transpose(gain_acc[:], gain_rows[:], ident[:])
+        turn_quarter(3)
+        left_quarter(3, (2, 0))
+        wo_bf = held([P, 4 * N], BF16, "wo_bf", "left0")
+        nc.scalar.copy(
+            wo_bf[:].rearrange("p (c i t) -> p c t i", i=4, t=4),
+            wo_raw[:].rearrange("p t (c i) -> p c t i", i=4),
+        )
 
         nc.vector.tensor_copy(
             wk_w[:].rearrange("p a t (b e) -> p a t b e", e=8),
@@ -224,9 +239,6 @@ def tile_list_record_match_scores_kernel(
         )
         key_sc = placed([P, S], U8, "key_sc", 18432)
         gather_scales(key_sc[:], list_k, 0, S)
-        wo_w = held([P, N], U32, "wo_w")
-        wo_sc = held([P, N], U8, "wo_sc")
-        nc.vector.quantize_mx(out=wo_w[:].bitcast(FP8X4), scales=wo_sc[:], in_=wo_bf[:])
         key = [placed([P, S], U32, "key0", 19456), placed([P, S], U32, "key1", 23552)]
         gather_words(key[0][:], list_k, 0, 0, S)
         gather_words(key[1][:, :QUARTER], list_k, 1, 0, QUARTER)
@@ -242,15 +254,17 @@ def tile_list_record_match_scores_kernel(
             nc.vector.scalar_tensor_tensor(
                 agree[0][:, t * HALF : (t + 1) * HALF],
                 tanh_a_first[:, t, :],
-                gain[:, t, 0:1],
+                gain_acc[:, t : t + 1],
                 tanh_b_first[:, t, :],
                 ALU.mult,
                 ALU.mult,
             )
 
         early = HALF + P
+        wo_w = placed([P, N], U32, "wo_w", 46080)
+        wo_sc = held([P, N], U8, "wo_sc")
         h_bf = [held([P, 4 * early], BF16, "h_bf0"), held([P, 4 * (S - early)], BF16, "h_bf1", "tanh_a3")]
-        h_w = [held([P, early], U32, "h_w0", "gained3"), held([P, S - early], U32, "h_w1")]
+        h_w = [placed([P, early], U32, "h_w0", 43008), held([P, S - early], U32, "h_w1")]
         h_sc = held([P, S], U8, "h_sc")
         out_v = out.rearrange("(m p) j -> p m j", p=P)
 
@@ -285,7 +299,7 @@ def tile_list_record_match_scores_kernel(
         def subtract_key(j0, start, width=P):
             b0 = j0 % P
             if b0 == 0:
-                key_sum[j0] = bank([P, 4, P], j0 // P % 4)
+                key_sum[j0] = bank([P, 4, P], (1, 2, 0, 3)[j0 // P % 4])
                 for t in range(4):
                     for a in range(PASSES):
                         mx(
@@ -304,10 +318,10 @@ def tile_list_record_match_scores_kernel(
                 ALU.subtract,
             )
 
-        for j0 in range(0, HALF, P):
-            subtract_key(j0, 0)
-        subtract_key(512, 512)
+        for j0 in range(0, early, P):
+            subtract_key(j0, j0 // HALF * HALF)
         quantize_h(0, 512)
+        nc.vector.quantize_mx(out=wo_w[:].bitcast(FP8X4), scales=wo_sc[:], in_=wo_bf[:])
         score(0, 256, 0)
         score(256, 512, 1)
         subtract_key(640, 512)

@@ -50,23 +50,21 @@ def tile_list_record_match_scores_kernel(
         list_r = keep.tile([P, S // 16], U16, name="list_r")
         list_k = keep.tile([P, S // 16], U16, name="list_k")
         tab_sc = held([P, T // 4], I32, "tab_sc")
-        tab_w = [held([P, T], I32, "tab_w0"), placed([P, T], I32, "tab_w1", 27648)]
+        tab_w = [held([P, T], I32, "tab_w0"), placed([P, T], I32, "tab_w1", 32256)]
         wo_raw = held([P, 4, N], F32, "wo_raw")
         wr_w = held([P, PASSES, 2 * H], U8, "wr_w")
         wr_sc = held([P, PASSES, H], U8, "wr_sc")
-        wl_raw = [held([P, 4, H], F32, "wl_raw0"), placed([P, 4, H], F32, "wl_raw1", 15872)]
+        wl_raw = [held([P, 4, H], F32, "wl_raw0"), placed([P, 4, H], F32, "wl_raw1", 16128)]
         right_sc1 = held([P, S // 4], I32, "right_sc1")
-        wk_sc_raw = placed([P, H // 4], I32, "wk_sc_raw", 35840)
-        wk_raw = placed([P, PASSES, H], I32, "wk_raw", 38400)
+        wk_sc_raw = placed([P, H // 4], I32, "wk_sc_raw", 40448)
+        wk_raw = placed([P, PASSES, H], I32, "wk_raw", 40960)
         gain = held([P, 4, 8], F32, "gain")
         ident = held([P, P], F32, "ident")
-        gain_rows = held([P, P], F32, "gain_rows")
 
         nc.vector.memset(tab_sc[:], 0)
         nc.vector.memset(wr_sc[:].bitcast(I32), 0)
         nc.vector.memset(right_sc1[:], 0)
         nc.vector.memset(wk_sc_raw[:], 0)
-        nc.vector.memset(gain_rows[:], 0)
         make_identity(nc, ident[:])
 
         def load_table(a):
@@ -109,18 +107,28 @@ def tile_list_record_match_scores_kernel(
             nc.sync.dma_start(wk_sc_raw[32 * q : 32 * q + 8, :], wk_scales[:, 4 * q : 4 * q + 4, :].bitcast(I32))
         for t in range(4):
             nc.sync.dma_start(wo_raw[:, t, :], wo.rearrange("(b t e) n -> t b e n", t=4, e=8)[t])
-        nc.sync.dma_start(
-            gain_rows[0:4, :].rearrange("t (b e) -> t b e", e=8), g.rearrange("(b t e) -> t b e", t=4, e=8)
-        )
         with nc.allow_non_contiguous_dma(reason="one gain to a partition"):
             for t in range(4):
                 nc.sync.dma_start(gain[:, t, 0:1], g.rearrange("(b t e) -> t b e", t=4, e=8)[t])
 
-        left = [held([P, S], U32, "left%d" % a) for a in range(PASSES)]
+        left0 = held([P, S], U32, "left0")
+        left1 = [held([P, HALF], U32, "left1_0"), placed([P, HALF], U32, "left1_1", 16384)]
         right = [held([P, S], U32, "right%d" % a) for a in range(PASSES)]
-        for a in range(PASSES):
-            gather_words(right[a][:], list_r, a, 0, S)
-            gather_words(left[a][:], list_l, a, 0, S)
+        gather_words(right[0][:], list_r, 0, 0, S)
+        gather_words(left0[:], list_l, 0, 0, S)
+        wr_dealt = held([P, PASSES, 4, 2 * P], U8, "wr_dealt")
+        wr_sc_dealt = held([P, PASSES, 4, P], U8, "wr_sc_dealt")
+        nc.vector.tensor_copy(
+            wr_dealt[:].bitcast(I32).rearrange("p a t (b w) -> p a t b w", w=4),
+            wr_w[:].bitcast(I32).rearrange("p a (b t w) -> p a t b w", t=4, w=4),
+        )
+        nc.vector.tensor_copy(
+            wr_sc_dealt[:].bitcast(I32).rearrange("p a t (b w) -> p a t b w", w=2),
+            wr_sc[:].bitcast(I32).rearrange("p a (b t w) -> p a t b w", t=4, w=2),
+        )
+        gather_words(right[1][:, HALF:], list_r, 1, HALF, S)
+        gather_words(right[1][:, :HALF], list_r, 1, 0, HALF)
+        gather_words(left1[0][:], list_l, 1, 0, HALF)
 
         def mx(acc, a, lhs, lhs_sc, rhs, rhs_sc):
             nc.tensor.matmul_mx(
@@ -130,8 +138,6 @@ def tile_list_record_match_scores_kernel(
         wl_w = held([P, PASSES, H], U32, "wl_w")
         wl_sc = held([P, PASSES, H], U8, "wl_sc")
         wl_bf = [held([P, 4, 4 * P], BF16, "wl_bf%d" % a) for a in range(PASSES)]
-        wk_w = held([P, PASSES, 4, P], I32, "wk_w")
-        wk_sc = held([P, 4, P], U8, "wk_sc")
         for a in range(PASSES):
             dst = wl_bf[a][:].rearrange("p t (b y e j) -> p y t b j e", y=2, e=4, j=4)
             src = wl_raw[a][:].rearrange("p j (b t y e) -> p y t b j e", t=4, y=2, e=4)
@@ -140,13 +146,16 @@ def tile_list_record_match_scores_kernel(
             nc.vector.quantize_mx(
                 out=wl_w[:, a, :].bitcast(FP8X4), scales=wl_sc[:, a, :], in_=wl_bf[a][:].rearrange("p t x -> p (t x)")
             )
+        gather_words(left1[1][:], list_l, 1, HALF, S)
 
-        tanh_turned = placed([P, 8, H], F32, "tanh_turned", 0)
+        tanh_b = placed([P, 8, HALF], F32, "tanh_b", 0)
+        b_first = [upper([P, H], "b_first%d" % jb, jb) for jb in range(4)]
+        b_second = [bank([P, HALF], t) for t in range(4)]
 
-        def right_pass(acc, a, jb):
+        def first_pass(a, jb):
             cols = slice(jb * P, (jb + 1) * P)
             mx(
-                acc[:],
+                b_first[jb][:],
                 a,
                 right[a][:, cols].bitcast(FP8X4),
                 right_planes[a][:, cols],
@@ -154,81 +163,88 @@ def tile_list_record_match_scores_kernel(
                 wr_sc[:, a, :],
             )
 
-        def right_blocks(accs, first):
-            for a in range(PASSES):
-                for i, acc in enumerate(accs):
-                    right_pass(acc, a, first + i)
-            for i, acc in enumerate(accs):
-                nc.scalar.activation(
-                    tanh_turned[:, first + i, :].rearrange("p (t b e) -> p t b e", t=4, e=8),
-                    acc[:].rearrange("p (b t e) -> p t b e", t=4, e=8),
-                    ACT.Tanh,
-                )
+        def second_pass(a, t):
+            mx(
+                b_second[t][:],
+                a,
+                wr_dealt[:, a, t, :].bitcast(FP4X4),
+                wr_sc_dealt[:, a, t, :],
+                right[a][:, HALF:].bitcast(FP8X4),
+                right_planes[a][:, HALF:],
+            )
 
-        def turn(dst, t, jb):
-            nc.tensor.transpose(dst, tanh_turned[:, jb, t * P : (t + 1) * P], ident[:])
-
-        right_blocks([upper([P, H], "b_first%d" % jb, jb) for jb in range(4)] + [bank([P, H], i) for i in range(4)], 0)
-        tanh_b_first = upper([P, 4, HALF], "tanh_b_first", 0)
+        for step, a in ((first_pass, 0), (second_pass, 0), (second_pass, 1), (first_pass, 1)):
+            for i in range(4):
+                step(a, i)
         for t in range(4):
-            for jb in range(4):
-                turn(tanh_b_first[:, t, jb * P : (jb + 1) * P], t, jb)
+            nc.scalar.activation(tanh_b[:, 4 + t, :], b_second[t][:], ACT.Tanh)
+        for jb in range(4):
+            nc.scalar.activation(
+                tanh_b[:, jb, :].rearrange("p (t b e) -> p t b e", t=4, e=8),
+                b_first[jb][:].rearrange("p (b t e) -> p t b e", t=4, e=8),
+                ACT.Tanh,
+            )
 
         def left_product(acc, t, j0, width):
             cols = slice(t * P, (t + 1) * P)
+            words = [left0[:, j0 : j0 + width], left1[j0 // HALF][:, j0 % HALF : j0 % HALF + width]]
             for a in range(PASSES):
                 mx(
                     acc,
                     a,
                     wl_w[:, a, cols].bitcast(FP8X4),
                     wl_sc[:, a, cols],
-                    left[a][:, j0 : j0 + width].bitcast(FP8X4),
+                    words[a].bitcast(FP8X4),
                     left_sc[4 * a : P, j0 : j0 + width],
                 )
 
-        tanh_a, agree = {}, {}
-        gained = {2: held([P, 4 * QUARTER], F32, "gained2"), 3: placed([P, 4 * QUARTER], F32, "gained3", 44032)}
+        tanh_a_first = held([P, 4, HALF], F32, "tanh_a_first")
+        for t in range(4):
+            acc = bank([P, HALF], t)
+            left_product(acc[:], t, 0, HALF)
+            nc.scalar.activation(tanh_a_first[:, t, :], acc[:], ACT.Tanh)
 
-        def turn_quarter(q):
-            accs = [bank([P, 2, QUARTER], pair) for pair in range(2)]
-            for t in range(4):
-                for half in range(2):
-                    turn(accs[t // 2][:, t % 2, half * P : (half + 1) * P], t, 2 * q + half)
+        tanh_a, agree = {}, {}
+        gained = {2: held([P, 4 * QUARTER], F32, "gained2"), 3: placed([P, 4 * QUARTER], F32, "gained3", 46080)}
+
+        def apply_gain(q):
+            c0 = q * QUARTER - HALF
             for t in range(4):
                 nc.scalar.activation(
                     gained[q][:, t * QUARTER : (t + 1) * QUARTER],
-                    accs[t // 2][:, t % 2, :],
+                    tanh_b[:, 4 + t, c0 : c0 + QUARTER],
                     ACT.Copy,
                     scale=gain[:, t, 0:1],
                 )
 
-        def left_quarter(q, banks):
+        def left_quarter(q):
             tanh_a[q] = held([P, 4 * QUARTER], F32, "tanh_a%d" % q)
             for pair in range(2):
-                acc = bank([P, 2, QUARTER], banks[pair])
+                acc = bank([P, 2, QUARTER], 2 * (q - 2) + pair)
                 for i in range(2):
                     left_product(acc[:, i, :], 2 * pair + i, q * QUARTER, QUARTER)
                 nc.scalar.activation(
                     tanh_a[q][:, pair * HALF : (pair + 1) * HALF], acc[:].rearrange("p t c -> p (t c)"), ACT.Tanh
                 )
 
-        turn_quarter(2)
-        left_quarter(2, (2, 3))
-        tanh_a_first = held([P, 4, HALF], F32, "tanh_a_first")
+        apply_gain(2)
+        left_quarter(2)
+        left_quarter(3)
+        apply_gain(3)
+        tanh_b_first = upper([P, 4, HALF], "tanh_b_first", 0)
         for t in range(4):
-            acc = bank([P, HALF], t)
-            left_product(acc[:], t, 0, HALF)
-            nc.scalar.activation(tanh_a_first[:, t, :], acc[:], ACT.Tanh)
-        gain_acc = bank([P, P], 3)
-        nc.tensor.transpose(gain_acc[:], gain_rows[:], ident[:])
-        turn_quarter(3)
-        left_quarter(3, (2, 0))
+            for jb in range(4):
+                nc.tensor.transpose(
+                    tanh_b_first[:, t, jb * P : (jb + 1) * P], tanh_b[:, jb, t * P : (t + 1) * P], ident[:]
+                )
         wo_bf = held([P, 4 * N], BF16, "wo_bf", "left0")
         nc.scalar.copy(
             wo_bf[:].rearrange("p (c i t) -> p c t i", i=4, t=4),
             wo_raw[:].rearrange("p t (c i) -> p c t i", i=4),
         )
 
+        wk_w = placed([P, PASSES, 4, P], I32, "wk_w", 19456)
+        wk_sc = placed([P, 4, P], U8, "wk_sc", 23552)
         nc.vector.tensor_copy(
             wk_w[:].rearrange("p a t (b e) -> p a t b e", e=8),
             wk_raw[:].rearrange("p a (b t e) -> p a t b e", t=4, e=8),
@@ -239,12 +255,12 @@ def tile_list_record_match_scores_kernel(
         )
         key_sc = placed([P, S], U8, "key_sc", 18432)
         gather_scales(key_sc[:], list_k, 0, S)
-        key = [placed([P, S], U32, "key0", 19456), placed([P, S], U32, "key1", 23552)]
-        gather_words(key[0][:], list_k, 0, 0, S)
-        gather_words(key[1][:, :QUARTER], list_k, 1, 0, QUARTER)
-        gather_words(key[1][:, QUARTER:], list_k, 1, QUARTER, S)
+        key = placed([P, PASSES * S], U32, "key", 24064)
+        gather_words(key[:, :S], list_k, 0, 0, S)
+        gather_words(key[:, S : S + QUARTER], list_k, 1, 0, QUARTER)
+        gather_words(key[:, S + QUARTER :], list_k, 1, QUARTER, S)
 
-        agree[512] = placed([P, 4 * QUARTER], F32, "agree512", 35328)
+        agree[512] = placed([P, 4 * QUARTER], F32, "agree512", 39936)
         nc.gpsimd.tensor_tensor(agree[512][:], tanh_a[2][:], gained[2][:], ALU.mult)
         agree[768] = held([P, 4 * QUARTER], F32, "agree768")
         nc.gpsimd.tensor_tensor(agree[768][:], tanh_a[3][:], gained[3][:], ALU.mult)
@@ -254,17 +270,17 @@ def tile_list_record_match_scores_kernel(
             nc.vector.scalar_tensor_tensor(
                 agree[0][:, t * HALF : (t + 1) * HALF],
                 tanh_a_first[:, t, :],
-                gain_acc[:, t : t + 1],
+                gain[:, t, 0:1],
                 tanh_b_first[:, t, :],
                 ALU.mult,
                 ALU.mult,
             )
 
         early = HALF + P
-        wo_w = placed([P, N], U32, "wo_w", 46080)
+        wo_w = placed([P, N], U32, "wo_w", 48128)
         wo_sc = held([P, N], U8, "wo_sc")
         h_bf = [held([P, 4 * early], BF16, "h_bf0"), held([P, 4 * (S - early)], BF16, "h_bf1", "tanh_a3")]
-        h_w = [placed([P, early], U32, "h_w0", 43008), held([P, S - early], U32, "h_w1")]
+        h_w = [placed([P, early], U32, "h_w0", 45056), held([P, S - early], U32, "h_w1")]
         h_sc = held([P, S], U8, "h_sc")
         out_v = out.rearrange("(m p) j -> p m j", p=P)
 
@@ -299,7 +315,7 @@ def tile_list_record_match_scores_kernel(
         def subtract_key(j0, start, width=P):
             b0 = j0 % P
             if b0 == 0:
-                key_sum[j0] = bank([P, 4, P], (1, 2, 0, 3)[j0 // P % 4])
+                key_sum[j0] = bank([P, 4, P], j0 // P % 4)
                 for t in range(4):
                     for a in range(PASSES):
                         mx(
@@ -307,7 +323,7 @@ def tile_list_record_match_scores_kernel(
                             a,
                             wk_w[:, a, t, :].bitcast(FP8X4),
                             wk_sc[4 * a : P, t, :],
-                            key[a][:, j0 : j0 + P].bitcast(FP8X4),
+                            key[:, a * S + j0 : a * S + j0 + P].bitcast(FP8X4),
                             key_sc[4 * a : P, j0 : j0 + P],
                         )
             c0 = j0 - start

@@ -1,7 +1,6 @@
 from contextlib import ExitStack
 
 import concourse.mybir as mybir
-from concourse.masks import make_identity
 
 K, H, N, T, S = 1024, 512, 256, 2048, 1024
 FLOPS = 2 * S * H * (3 * K + N)
@@ -21,6 +20,7 @@ P = 128
 PASSES = K // 512
 HALF = S // 2
 QUARTER = S // 4
+POOL_COLS = {2: 768, 3: 384}
 
 
 def tile_list_record_match_scores_kernel(
@@ -30,7 +30,7 @@ def tile_list_record_match_scores_kernel(
     with ExitStack() as ctx:
         keep = ctx.enter_context(tc.tile_pool(name="keep", bufs=1))
         laid = ctx.enter_context(tc.tile_pool(name="laid", bufs=1))
-        res_pool = ctx.enter_context(tc.tile_pool(name="res", bufs=7))
+        res_pool = ctx.enter_context(tc.tile_pool(name="res", bufs=6))
         acc_pool = ctx.enter_context(tc.psum_pool(name="acc", bufs=1))
         upper_pool = ctx.enter_context(tc.psum_pool(name="upper", bufs=1))
 
@@ -50,22 +50,20 @@ def tile_list_record_match_scores_kernel(
         list_r = keep.tile([P, S // 16], U16, name="list_r")
         list_k = keep.tile([P, S // 16], U16, name="list_k")
         tab_sc = held([P, T // 4], I32, "tab_sc")
-        tab_w = [held([P, T], I32, "tab_w0"), placed([P, T], I32, "tab_w1", 32256)]
+        tab_w = [held([P, T], I32, "tab_w%d" % a) for a in range(PASSES)]
         wo_raw = held([P, 4, N], F32, "wo_raw")
         wr_w = held([P, PASSES, 2 * H], U8, "wr_w")
         wr_sc = held([P, PASSES, H], U8, "wr_sc")
         wl_raw = [held([P, 4, H], F32, "wl_raw0"), placed([P, 4, H], F32, "wl_raw1", 16128)]
         right_sc1 = held([P, S // 4], I32, "right_sc1")
-        wk_sc_raw = placed([P, H // 4], I32, "wk_sc_raw", 40448)
-        wk_raw = placed([P, PASSES, H], I32, "wk_raw", 40960)
+        wk_sc_raw = held([P, H // 4], I32, "wk_sc_raw")
+        wk_raw = held([P, PASSES, H], I32, "wk_raw")
         gain = held([P, 4, 8], F32, "gain")
-        ident = held([P, P], F32, "ident")
 
         nc.vector.memset(tab_sc[:], 0)
         nc.vector.memset(wr_sc[:].bitcast(I32), 0)
         nc.vector.memset(right_sc1[:], 0)
         nc.vector.memset(wk_sc_raw[:], 0)
-        make_identity(nc, ident[:])
 
         def load_table(a):
             nc.sync.dma_start(tab_w[a][:], tab_words[a].rearrange("p t i -> p (t i)").bitcast(I32))
@@ -74,11 +72,11 @@ def tile_list_record_match_scores_kernel(
             nc.sync.dma_start(wl_raw[a][:], wl[512 * a : 512 * (a + 1), :].rearrange("(p j) r -> p j r", j=4))
 
         nc.sync.dma_start(list_r[:], offs2)
+        nc.sync.dma_start(wr_w[:].bitcast(I32), wr_words.bitcast(I32).rearrange("a p w -> p a w"))
+        nc.sync.dma_start(list_l[:], offs)
         for q in range(4):
             nc.sync.dma_start(tab_sc[32 * q : 32 * q + 8, :], tab_scales[:, 4 * q : 4 * q + 4, :].bitcast(I32))
-        nc.sync.dma_start(list_l[:], offs)
         load_table(0)
-        nc.sync.dma_start(wr_w[:].bitcast(I32), wr_words.bitcast(I32).rearrange("a p w -> p a w"))
         for q in range(4):
             nc.sync.dma_start(
                 wr_sc[32 * q : 32 * q + 4, :, :].bitcast(I32),
@@ -115,7 +113,6 @@ def tile_list_record_match_scores_kernel(
         left1 = [held([P, HALF], U32, "left1_0"), placed([P, HALF], U32, "left1_1", 16384)]
         right = [held([P, S], U32, "right%d" % a) for a in range(PASSES)]
         gather_words(right[0][:], list_r, 0, 0, S)
-        gather_words(left0[:], list_l, 0, 0, S)
         wr_dealt = held([P, PASSES, 4, 2 * P], U8, "wr_dealt")
         wr_sc_dealt = held([P, PASSES, 4, P], U8, "wr_sc_dealt")
         nc.vector.tensor_copy(
@@ -126,6 +123,7 @@ def tile_list_record_match_scores_kernel(
             wr_sc_dealt[:].bitcast(I32).rearrange("p a t (b w) -> p a t b w", w=2),
             wr_sc[:].bitcast(I32).rearrange("p a (b t w) -> p a t b w", t=4, w=2),
         )
+        gather_words(left0[:], list_l, 0, 0, S)
         gather_words(right[1][:, HALF:], list_r, 1, HALF, S)
         gather_words(right[1][:, :HALF], list_r, 1, 0, HALF)
         gather_words(left1[0][:], list_l, 1, 0, HALF)
@@ -148,42 +146,31 @@ def tile_list_record_match_scores_kernel(
             )
         gather_words(left1[1][:], list_l, 1, HALF, S)
 
-        tanh_b = placed([P, 8, HALF], F32, "tanh_b", 0)
-        b_first = [upper([P, H], "b_first%d" % jb, jb) for jb in range(4)]
-        b_second = [bank([P, HALF], t) for t in range(4)]
+        tanh_b = placed([P, PASSES, 4, HALF], F32, "tanh_b", 0)
+        b_acc = [
+            [upper([P, HALF], "b_first%d" % t, t) for t in range(4)],
+            [bank([P, HALF], t) for t in range(4)],
+        ]
+        for half, a in ((0, 0), (1, 0), (1, 1), (0, 1)):
+            cols = slice(half * HALF, (half + 1) * HALF)
+            for t in range(4):
+                mx(
+                    b_acc[half][t][:],
+                    a,
+                    wr_dealt[:, a, t, :].bitcast(FP4X4),
+                    wr_sc_dealt[:, a, t, :],
+                    right[a][:, cols].bitcast(FP8X4),
+                    right_planes[a][:, cols],
+                )
+        for half in (1, 0):
+            for t in range(4):
+                nc.scalar.activation(tanh_b[:, half, t, :], b_acc[half][t][:], ACT.Tanh)
 
-        def first_pass(a, jb):
-            cols = slice(jb * P, (jb + 1) * P)
-            mx(
-                b_first[jb][:],
-                a,
-                right[a][:, cols].bitcast(FP8X4),
-                right_planes[a][:, cols],
-                wr_w[:, a, :].bitcast(FP4X4),
-                wr_sc[:, a, :],
-            )
-
-        def second_pass(a, t):
-            mx(
-                b_second[t][:],
-                a,
-                wr_dealt[:, a, t, :].bitcast(FP4X4),
-                wr_sc_dealt[:, a, t, :],
-                right[a][:, HALF:].bitcast(FP8X4),
-                right_planes[a][:, HALF:],
-            )
-
-        for step, a in ((first_pass, 0), (second_pass, 0), (second_pass, 1), (first_pass, 1)):
-            for i in range(4):
-                step(a, i)
-        for t in range(4):
-            nc.scalar.activation(tanh_b[:, 4 + t, :], b_second[t][:], ACT.Tanh)
-        for jb in range(4):
-            nc.scalar.activation(
-                tanh_b[:, jb, :].rearrange("p (t b e) -> p t b e", t=4, e=8),
-                b_first[jb][:].rearrange("p (b t e) -> p t b e", t=4, e=8),
-                ACT.Tanh,
-            )
+        wo_bf = held([P, 4 * N], BF16, "wo_bf")
+        nc.scalar.copy(
+            wo_bf[:].rearrange("p (c i t) -> p c t i", i=4, t=4),
+            wo_raw[:].rearrange("p t (c i) -> p c t i", i=4),
+        )
 
         def left_product(acc, t, j0, width):
             cols = slice(t * P, (t + 1) * P)
@@ -198,50 +185,40 @@ def tile_list_record_match_scores_kernel(
                     left_sc[4 * a : P, j0 : j0 + width],
                 )
 
-        tanh_a_first = held([P, 4, HALF], F32, "tanh_a_first")
+        tanh_a_first = [held([P, HALF], F32, "tanh_a_first%d" % t) for t in range(4)]
         for t in range(4):
             acc = bank([P, HALF], t)
             left_product(acc[:], t, 0, HALF)
-            nc.scalar.activation(tanh_a_first[:, t, :], acc[:], ACT.Tanh)
+            nc.scalar.activation(tanh_a_first[t][:], acc[:], ACT.Tanh)
 
-        tanh_a, agree = {}, {}
-        gained = {2: held([P, 4 * QUARTER], F32, "gained2"), 3: placed([P, 4 * QUARTER], F32, "gained3", 46080)}
-
-        def apply_gain(q):
-            c0 = q * QUARTER - HALF
-            for t in range(4):
-                nc.scalar.activation(
-                    gained[q][:, t * QUARTER : (t + 1) * QUARTER],
-                    tanh_b[:, 4 + t, c0 : c0 + QUARTER],
-                    ACT.Copy,
-                    scale=gain[:, t, 0:1],
-                )
+        tanh_a, gained, agree = {}, {}, {}
 
         def left_quarter(q):
             tanh_a[q] = held([P, 4 * QUARTER], F32, "tanh_a%d" % q)
             for pair in range(2):
-                acc = bank([P, 2, QUARTER], 2 * (q - 2) + pair)
+                acc = upper([P, 2, QUARTER], "a_acc%d%d" % (q, pair), 2 * (q - 2) + pair)
                 for i in range(2):
                     left_product(acc[:, i, :], 2 * pair + i, q * QUARTER, QUARTER)
                 nc.scalar.activation(
                     tanh_a[q][:, pair * HALF : (pair + 1) * HALF], acc[:].rearrange("p t c -> p (t c)"), ACT.Tanh
                 )
 
-        apply_gain(2)
-        left_quarter(2)
-        left_quarter(3)
-        apply_gain(3)
-        tanh_b_first = upper([P, 4, HALF], "tanh_b_first", 0)
-        for t in range(4):
-            for jb in range(4):
-                nc.tensor.transpose(
-                    tanh_b_first[:, t, jb * P : (jb + 1) * P], tanh_b[:, jb, t * P : (t + 1) * P], ident[:]
-                )
-        wo_bf = held([P, 4 * N], BF16, "wo_bf", "left0")
-        nc.scalar.copy(
-            wo_bf[:].rearrange("p (c i t) -> p c t i", i=4, t=4),
-            wo_raw[:].rearrange("p t (c i) -> p c t i", i=4),
-        )
+        def apply_gain(q):
+            c0 = q * QUARTER - HALF
+            gained[q] = held([P, POOL_COLS[q]], F32, "gained%d" % q)
+            for t in range(4):
+                width = min(QUARTER, POOL_COLS[q] - t * QUARTER)
+                if width > 0:
+                    nc.scalar.activation(
+                        gained[q][:, t * QUARTER : t * QUARTER + width],
+                        tanh_b[:, 1, t, c0 : c0 + width],
+                        ACT.Copy,
+                        scale=gain[:, t, 0:1],
+                    )
+
+        for q in POOL_COLS:
+            left_quarter(q)
+            apply_gain(q)
 
         wk_w = placed([P, PASSES, 4, P], I32, "wk_w", 19456)
         wk_sc = placed([P, 4, P], U8, "wk_sc", 23552)
@@ -260,35 +237,48 @@ def tile_list_record_match_scores_kernel(
         gather_words(key[:, S : S + QUARTER], list_k, 1, 0, QUARTER)
         gather_words(key[:, S + QUARTER :], list_k, 1, QUARTER, S)
 
-        agree[512] = placed([P, 4 * QUARTER], F32, "agree512", 39936)
-        nc.gpsimd.tensor_tensor(agree[512][:], tanh_a[2][:], gained[2][:], ALU.mult)
-        agree[768] = held([P, 4 * QUARTER], F32, "agree768")
-        nc.gpsimd.tensor_tensor(agree[768][:], tanh_a[3][:], gained[3][:], ALU.mult)
-
         agree[0] = held([P, 4 * HALF], F32, "agree0")
         for t in range(4):
             nc.vector.scalar_tensor_tensor(
                 agree[0][:, t * HALF : (t + 1) * HALF],
-                tanh_a_first[:, t, :],
+                tanh_a_first[t][:],
                 gain[:, t, 0:1],
-                tanh_b_first[:, t, :],
+                tanh_b[:, 0, t, :],
                 ALU.mult,
                 ALU.mult,
             )
 
-        early = HALF + P
-        wo_w = placed([P, N], U32, "wo_w", 48128)
+        def agreement(q, slot):
+            j0 = q * QUARTER
+            agree[j0] = held([P, 4 * QUARTER], F32, "agree%d" % j0, slot)
+            first = POOL_COLS[q]
+            nc.gpsimd.tensor_tensor(agree[j0][:, :first], tanh_a[q][:, :first], gained[q][:], ALU.mult)
+            for t in range(4):
+                skip = max(0, first - t * QUARTER)
+                if skip < QUARTER:
+                    cols = slice(t * QUARTER + skip, (t + 1) * QUARTER)
+                    nc.vector.scalar_tensor_tensor(
+                        agree[j0][:, cols],
+                        tanh_a[q][:, cols],
+                        gain[:, t, 0:1],
+                        tanh_b[:, 1, t, j0 - HALF + skip : j0 - HALF + QUARTER],
+                        ALU.mult,
+                        ALU.mult,
+                    )
+
+        wo_w = held([P, N], U32, "wo_w", "tanh_a_first2")
         wo_sc = held([P, N], U8, "wo_sc")
-        h_bf = [held([P, 4 * early], BF16, "h_bf0"), held([P, 4 * (S - early)], BF16, "h_bf1", "tanh_a3")]
-        h_w = [placed([P, early], U32, "h_w0", 45056), held([P, S - early], U32, "h_w1")]
+        nc.vector.quantize_mx(out=wo_w[:].bitcast(FP8X4), scales=wo_sc[:], in_=wo_bf[:])
+        h_bf = held([P, 4 * S], BF16, "h_bf")
+        h_w = held([P, S], U32, "h_w")
         h_sc = held([P, S], U8, "h_sc")
         out_v = out.rearrange("(m p) j -> p m j", p=P)
 
         def h_words(j0, j1):
-            return h_w[j0 // early][:, j0 % early : j0 % early + j1 - j0].bitcast(FP8X4)
+            return h_w[:, j0:j1].bitcast(FP8X4)
 
         def h_values(j0, j1):
-            return h_bf[j0 // early][:, 4 * (j0 % early) : 4 * (j0 % early + j1 - j0)]
+            return h_bf[:, 4 * j0 : 4 * j1]
 
         def quantize_h(j0, j1):
             nc.vector.quantize_mx(out=h_words(j0, j1), scales=h_sc[:, j0:j1], in_=h_values(j0, j1))
@@ -334,23 +324,23 @@ def tile_list_record_match_scores_kernel(
                 ALU.subtract,
             )
 
-        for j0 in range(0, early, P):
-            subtract_key(j0, j0 // HALF * HALF)
+        for j0 in range(0, HALF, P):
+            subtract_key(j0, 0)
+        agreement(2, "tanh_a_first3")
         quantize_h(0, 512)
-        nc.vector.quantize_mx(out=wo_w[:].bitcast(FP8X4), scales=wo_sc[:], in_=wo_bf[:])
         score(0, 256, 0)
         score(256, 512, 1)
-        subtract_key(640, 512)
-        quantize_h(512, 640)
-        score(512, 640, 2)
+        for j0 in (512, 640):
+            subtract_key(j0, 512)
+        agreement(3, "tanh_a2")
+        quantize_h(512, 768)
+        score(512, 768, 2)
         subtract_key(768, 768)
-        quantize_h(640, 768)
-        score(640, 768, 3)
         subtract_key(896, 768, 64)
         quantize_h(768, 896)
-        score(768, 896, 0)
+        score(768, 896, 3)
         subtract_key(960, 768, 64)
         quantize_h(896, 960)
-        score(896, 960, 1)
+        score(896, 960, 0)
         quantize_h(960, 1024)
-        score(960, 1024, 2)
+        score(960, 1024, 1)

@@ -60,10 +60,10 @@ def tile_list_record_match_scores_kernel(
         wk_raw = held([P, PASSES, H], I32, "wk_raw")
         gain = held([P, 4, 8], F32, "gain")
 
-        nc.vector.memset(tab_sc[:], 0)
-        nc.vector.memset(wr_sc[:].bitcast(I32), 0)
-        nc.vector.memset(right_sc1[:], 0)
-        nc.vector.memset(wk_sc_raw[:], 0)
+        nc.gpsimd.memset(tab_sc[:], 0)
+        nc.gpsimd.memset(wr_sc[:].bitcast(I32), 0)
+        nc.gpsimd.memset(right_sc1[:], 0)
+        nc.gpsimd.memset(wk_sc_raw[:], 0)
 
         def load_table(a):
             nc.sync.dma_start(tab_w[a][:], tab_words[a].rearrange("p t i -> p (t i)").bitcast(I32))

@@ -32,7 +32,6 @@ def tile_list_record_match_scores_kernel(
         laid = ctx.enter_context(tc.tile_pool(name="laid", bufs=1))
         res_pool = ctx.enter_context(tc.tile_pool(name="res", bufs=6))
         acc_pool = ctx.enter_context(tc.psum_pool(name="acc", bufs=1))
-        upper_pool = ctx.enter_context(tc.psum_pool(name="upper", bufs=1))
 
         def held(shape, dtype, name, slot=None):
             return keep.tile(shape, dtype, name=name, tag=slot or name, align_bytes=64)
@@ -43,27 +42,27 @@ def tile_list_record_match_scores_kernel(
         def bank(shape, number):
             return acc_pool.tile(shape, F32, name="acc", tag="bank%d" % number)
 
-        def upper(shape, name, number):
-            return upper_pool.tile(shape, F32, name=name, tag=name, offset=2048 * number)
-
         list_l = keep.tile([P, S // 16], U16, name="list_l")
         list_r = keep.tile([P, S // 16], U16, name="list_r")
         list_k = keep.tile([P, S // 16], U16, name="list_k")
-        tab_sc = held([P, T // 4], I32, "tab_sc")
-        tab_w = [held([P, T], I32, "tab_w%d" % a) for a in range(PASSES)]
-        wo_raw = held([P, 4, N], F32, "wo_raw")
-        wr_w = held([P, PASSES, 2 * H], U8, "wr_w")
-        wr_sc = held([P, PASSES, H], U8, "wr_sc")
-        wl_raw = [held([P, 4, H], F32, "wl_raw0"), placed([P, 4, H], F32, "wl_raw1", 16128)]
-        right_sc1 = held([P, S // 4], I32, "right_sc1")
-        wk_sc_raw = held([P, H // 4], I32, "wk_sc_raw")
-        wk_raw = held([P, PASSES, H], I32, "wk_raw")
-        gain = held([P, 4, 8], F32, "gain")
+        tab_sc = placed([P, T // 4], I32, "tab_sc", 36864)
+        tab_sc_flat = placed([P, T // 4], I32, "tab_sc_flat", 24064)
+        tab_w = [held([P, T], I32, "tab_w0"), placed([P, T], I32, "tab_w1", 16384)]
+        wo_raw = placed([P, 4, N], F32, "wo_raw", 8192)
+        wr_raw = held([P, PASSES, H // 2], I32, "wr_raw")
+        wr_sc_raw = held([P, PASSES, H // 4], I32, "wr_sc_raw")
+        wl_raw = [placed([P, 4, H], F32, "wl_raw0", 8192), placed([P, 4, H], F32, "wl_raw1", 0)]
+        right_sc = [placed([P, S // 4], I32, "right_sc0", 24576), placed([P, S // 4], I32, "right_sc1", 36864)]
+        wk_sc_raw = placed([P, 1, H // 4], I32, "wk_sc_raw", 12288)
+        wk_raw = placed([P, PASSES, H], I32, "wk_raw", 25600)
+        gain = placed([P, 4, 8], F32, "gain", 12800)
+
+        wr_sc = placed([P, PASSES, H // 4], I32, "wr_sc", 37888)
+        wk_sc = placed([P, 1, H // 4], I32, "wk_sc", 38912)
 
         nc.gpsimd.memset(tab_sc[:], 0)
-        nc.gpsimd.memset(wr_sc[:].bitcast(I32), 0)
-        nc.gpsimd.memset(right_sc1[:], 0)
-        nc.gpsimd.memset(wk_sc_raw[:], 0)
+        nc.vector.memset(tab_sc_flat[32:64, :], 0)
+        nc.vector.memset(tab_sc_flat[64:128, :], 0)
 
         def load_table(a):
             nc.sync.dma_start(tab_w[a][:], tab_words[a].rearrange("p t i -> p (t i)").bitcast(I32))
@@ -71,134 +70,165 @@ def tile_list_record_match_scores_kernel(
         def load_wl(a):
             nc.sync.dma_start(wl_raw[a][:], wl[512 * a : 512 * (a + 1), :].rearrange("(p j) r -> p j r", j=4))
 
-        nc.sync.dma_start(list_r[:], offs2)
-        nc.sync.dma_start(wr_w[:].bitcast(I32), wr_words.bitcast(I32).rearrange("a p w -> p a w"))
-        nc.sync.dma_start(list_l[:], offs)
-        for q in range(4):
-            nc.sync.dma_start(tab_sc[32 * q : 32 * q + 8, :], tab_scales[:, 4 * q : 4 * q + 4, :].bitcast(I32))
-        load_table(0)
-        for q in range(4):
-            nc.sync.dma_start(
-                wr_sc[32 * q : 32 * q + 4, :, :].bitcast(I32),
-                wr_scales[:, 4 * q : 4 * q + 4, :].bitcast(I32).rearrange("a r w -> r a w"),
-            )
-        load_table(1)
-
-        def gather_scales(dst, lst, j0, j1):
-            nc.vector.tensor_copy(dst, tab_sc[:].bitcast(U8).indirect(lst[:, j0 // 16 : j1 // 16]))
+        def gather_scales(dst, window, lst):
+            nc.vector.tensor_copy(dst, window[:].bitcast(U8).indirect(lst[:]))
 
         def gather_words(dst, lst, a, j0, j1):
             nc.vector.tensor_copy(dst, tab_w[a][:].bitcast(U32).indirect(lst[:, j0 // 16 : j1 // 16]))
 
-        right_sc = held([P, S], U8, "right_sc")
-        left_sc = held([P, S], U8, "left_sc")
-        gather_scales(right_sc[:], list_r, 0, S)
-        gather_scales(left_sc[:], list_l, 0, S)
-        right_planes = [right_sc[:], right_sc1[:].bitcast(U8)]
+        nc.sync.dma_start(list_r[:], offs2)
+        nc.sync.dma_start(tab_sc_flat[0:32, :], tab_scales.rearrange("a q t -> (a q) t").bitcast(I32))
+        nc.sync.dma_start(list_l[:], offs)
         for q in range(4):
-            nc.sync.dma_start(right_sc1[32 * q : 32 * q + 4, :], right_sc[32 * q + 4 : 32 * q + 8, :].bitcast(I32))
+            nc.sync.dma_start(tab_sc[32 * q : 32 * q + 8, :], tab_scales[:, 4 * q : 4 * q + 4, :].bitcast(I32))
         load_wl(0)
-        load_wl(1)
         nc.sync.dma_start(list_k[:], offs3)
-        nc.sync.dma_start(wk_raw[:], wk_words.rearrange("a p r i -> p a (r i)").bitcast(I32))
+        nc.sync.dma_start(wr_raw[:], wr_words.bitcast(I32).rearrange("a p w -> p a w"))
         for q in range(4):
-            nc.sync.dma_start(wk_sc_raw[32 * q : 32 * q + 8, :], wk_scales[:, 4 * q : 4 * q + 4, :].bitcast(I32))
+            nc.sync.dma_start(
+                wr_sc_raw[32 * q : 32 * q + 4, :, :],
+                wr_scales[:, 4 * q : 4 * q + 4, :].bitcast(I32).rearrange("a r w -> r a w"),
+            )
+        load_table(0)
+        load_wl(1)
+
+        right_flat = placed([P, S], U8, "right_flat", 38912)
+        left_sc = held([P, S], U8, "left_sc")
+        key_sc = held([P, S], U8, "key_sc")
+        gather_scales(right_flat[:], tab_sc_flat, list_r)
+        gather_scales(left_sc[:], tab_sc, list_l)
+        gather_scales(key_sc[:], tab_sc, list_k)
+
+        def place_right_rows(a):
+            for q in range(4):
+                row = 16 * a + 4 * q
+                nc.sync.dma_start(right_sc[a][32 * q : 32 * q + 4, :], right_flat[row : row + 4, :].bitcast(I32))
+
+        place_right_rows(0)
+        load_table(1)
+        nc.sync.dma_start(wk_raw[:], wk_words.rearrange("a p r i -> p a (r i)").bitcast(I32))
+        place_right_rows(1)
         for t in range(4):
             nc.sync.dma_start(wo_raw[:, t, :], wo.rearrange("(b t e) n -> t b e n", t=4, e=8)[t])
+        for q in range(4):
+            nc.sync.dma_start(wk_sc_raw[32 * q : 32 * q + 8, 0, :], wk_scales[:, 4 * q : 4 * q + 4, :].bitcast(I32))
         with nc.allow_non_contiguous_dma(reason="one gain to a partition"):
             for t in range(4):
                 nc.sync.dma_start(gain[:, t, 0:1], g.rearrange("(b t e) -> t b e", t=4, e=8)[t])
 
-        left0 = held([P, S], U32, "left0")
-        left1 = [held([P, HALF], U32, "left1_0"), placed([P, HALF], U32, "left1_1", 16384)]
-        right = [held([P, S], U32, "right%d" % a) for a in range(PASSES)]
-        gather_words(right[0][:], list_r, 0, 0, S)
-        wr_dealt = held([P, PASSES, 4, 2 * P], U8, "wr_dealt")
-        wr_sc_dealt = held([P, PASSES, 4, P], U8, "wr_sc_dealt")
-        nc.vector.tensor_copy(
-            wr_dealt[:].bitcast(I32).rearrange("p a t (b w) -> p a t b w", w=4),
-            wr_w[:].bitcast(I32).rearrange("p a (b t w) -> p a t b w", t=4, w=4),
+        wl_w = held([P, PASSES, H], U32, "wl_w")
+        wl_sc = held([P, PASSES, H], U8, "wl_sc")
+        wl_bf = [held([P, 4, 4 * P], BF16, "wl_bf%d" % a) for a in range(PASSES)]
+
+        def round_wl(a):
+            dst = wl_bf[a][:].rearrange("p t (b y e j) -> p y t b j e", y=2, e=4, j=4)
+            src = wl_raw[a][:].rearrange("p j (b t y e) -> p y t b j e", t=4, y=2, e=4)
+            for y in range(2):
+                nc.scalar.copy(dst[:, y], src[:, y])
+
+        def quantize_wl(a):
+            nc.vector.quantize_mx(
+                out=wl_w[:, a, :].bitcast(FP8X4), scales=wl_sc[:, a, :], in_=wl_bf[a][:].rearrange("p t x -> p (t x)")
+            )
+
+        def deal(dst, src, run):
+            nc.scalar.copy(
+                dst.bitcast(U32).rearrange("p a (t b w) -> p a t b w", t=4, w=run),
+                src.bitcast(U32).rearrange("p a (b t w) -> p a t b w", t=4, w=run),
+            )
+
+        wr_w = held([P, PASSES, H // 2], U32, "wr_w")
+        wk_w = held([P, PASSES, H], U32, "wk_w")
+        round_wl(0)
+        deal(wr_w[:], wr_raw[:], 4)
+        for q in range(4):
+            deal(wr_sc[32 * q : 32 * q + 4], wr_sc_raw[32 * q : 32 * q + 4], 2)
+        round_wl(1)
+        deal(wk_w[:], wk_raw[:], 8)
+        wo_bf = held([P, 4 * N], BF16, "wo_bf")
+        nc.scalar.copy(
+            wo_bf[:].rearrange("p (c i t) -> p c t i", i=4, t=4),
+            wo_raw[:].rearrange("p t (c i) -> p c t i", i=4),
         )
-        nc.vector.tensor_copy(
-            wr_sc_dealt[:].bitcast(I32).rearrange("p a t (b w) -> p a t b w", w=2),
-            wr_sc[:].bitcast(I32).rearrange("p a (b t w) -> p a t b w", t=4, w=2),
-        )
-        gather_words(left0[:], list_l, 0, 0, S)
-        gather_words(right[1][:, HALF:], list_r, 1, HALF, S)
-        gather_words(right[1][:, :HALF], list_r, 1, 0, HALF)
+        for q in range(4):
+            deal(wk_sc[32 * q : 32 * q + 8], wk_sc_raw[32 * q : 32 * q + 8], 2)
+
+        right0 = held([P, S], U32, "right0")
+        left0 = [held([P, HALF], U32, "left0_0"), held([P, HALF], U32, "left0_1")]
+        right1 = [placed([P, HALF], U32, "right1_0", 6144), placed([P, HALF], U32, "right1_1", 2048)]
+        left1 = [placed([P, HALF], U32, "left1_0", 0), placed([P, HALF], U32, "left1_1", 4096)]
+        key_words = placed([P, PASSES * S], U32, "key_words", 25600)
+        key = [key_words[:, a * S : (a + 1) * S] for a in range(PASSES)]
+        quantize_wl(0)
+        gather_words(left0[0][:], list_l, 0, 0, HALF)
+        gather_words(right0[:], list_r, 0, 0, S)
+        gather_words(left0[1][:], list_l, 0, HALF, S)
+        quantize_wl(1)
         gather_words(left1[0][:], list_l, 1, 0, HALF)
+        gather_words(right1[0][:], list_r, 1, 0, HALF)
+        gather_words(right1[1][:], list_r, 1, HALF, S)
+        gather_words(left1[1][:], list_l, 1, HALF, S)
+        gather_words(key[0], list_k, 0, 0, S)
+        gather_words(key[1][:, :QUARTER], list_k, 1, 0, QUARTER)
+        gather_words(key[1][:, QUARTER:], list_k, 1, QUARTER, S)
 
         def mx(acc, a, lhs, lhs_sc, rhs, rhs_sc):
             nc.tensor.matmul_mx(
                 out=acc, lhsT=lhs, lhsT_scale=lhs_sc, rhs=rhs, rhs_scale=rhs_sc, start=(a == 0), stop=(a == PASSES - 1)
             )
 
-        wl_w = held([P, PASSES, H], U32, "wl_w")
-        wl_sc = held([P, PASSES, H], U8, "wl_sc")
-        wl_bf = [held([P, 4, 4 * P], BF16, "wl_bf%d" % a) for a in range(PASSES)]
-        for a in range(PASSES):
-            dst = wl_bf[a][:].rearrange("p t (b y e j) -> p y t b j e", y=2, e=4, j=4)
-            src = wl_raw[a][:].rearrange("p j (b t y e) -> p y t b j e", t=4, y=2, e=4)
-            for y in range(2):
-                nc.scalar.copy(dst[:, y], src[:, y])
-            nc.vector.quantize_mx(
-                out=wl_w[:, a, :].bitcast(FP8X4), scales=wl_sc[:, a, :], in_=wl_bf[a][:].rearrange("p t x -> p (t x)")
-            )
-        gather_words(left1[1][:], list_l, 1, HALF, S)
-
-        tanh_b = placed([P, PASSES, 4, HALF], F32, "tanh_b", 0)
-        b_acc = [
-            [upper([P, HALF], "b_first%d" % t, t) for t in range(4)],
-            [bank([P, HALF], t) for t in range(4)],
-        ]
-        for half, a in ((0, 0), (1, 0), (1, 1), (0, 1)):
+        def right_pass(acc, a, t, half):
             cols = slice(half * HALF, (half + 1) * HALF)
-            for t in range(4):
-                mx(
-                    b_acc[half][t][:],
-                    a,
-                    wr_dealt[:, a, t, :].bitcast(FP4X4),
-                    wr_sc_dealt[:, a, t, :],
-                    right[a][:, cols].bitcast(FP8X4),
-                    right_planes[a][:, cols],
-                )
-        for half in (1, 0):
-            for t in range(4):
-                nc.scalar.activation(tanh_b[:, half, t, :], b_acc[half][t][:], ACT.Tanh)
+            words = [right0[:, cols], right1[half][:]]
+            mx(
+                acc,
+                a,
+                wr_w[:, a, t * 64 : (t + 1) * 64].bitcast(U8).bitcast(FP4X4),
+                wr_sc[:, a, t * 32 : (t + 1) * 32].bitcast(U8),
+                words[a].bitcast(FP8X4),
+                right_sc[a][:].bitcast(U8)[:, cols],
+            )
 
-        wo_bf = held([P, 4 * N], BF16, "wo_bf")
-        nc.scalar.copy(
-            wo_bf[:].rearrange("p (c i t) -> p c t i", i=4, t=4),
-            wo_raw[:].rearrange("p t (c i) -> p c t i", i=4),
-        )
-
-        def left_product(acc, t, j0, width):
+        def left_pass(acc, a, t, j0, width):
             cols = slice(t * P, (t + 1) * P)
-            words = [left0[:, j0 : j0 + width], left1[j0 // HALF][:, j0 % HALF : j0 % HALF + width]]
-            for a in range(PASSES):
-                mx(
-                    acc,
-                    a,
-                    wl_w[:, a, cols].bitcast(FP8X4),
-                    wl_sc[:, a, cols],
-                    words[a].bitcast(FP8X4),
-                    left_sc[4 * a : P, j0 : j0 + width],
-                )
+            words = [tiles[j0 // HALF][:, j0 % HALF : j0 % HALF + width] for tiles in (left0, left1)]
+            mx(
+                acc,
+                a,
+                wl_w[:, a, cols].bitcast(FP8X4),
+                wl_sc[:, a, cols],
+                words[a].bitcast(FP8X4),
+                left_sc[4 * a : P, j0 : j0 + width],
+            )
 
+        tanh_b = [held([P, 4, HALF], F32, "tanh_b%d" % half) for half in range(2)]
         tanh_a_first = [held([P, HALF], F32, "tanh_a_first%d" % t) for t in range(4)]
+        a_first = [bank([P, HALF], t) for t in range(4)]
+        b_first = [bank([P, HALF], 4 + t) for t in range(4)]
+        for a in range(PASSES):
+            for t in range(4):
+                left_pass(a_first[t][:], a, t, 0, HALF)
+            for t in range(4):
+                right_pass(b_first[t][:], a, t, 0)
+        for t in range(4):
+            nc.scalar.activation(tanh_a_first[t][:], a_first[t][:], ACT.Tanh)
+        for t in range(4):
+            nc.scalar.activation(tanh_b[0][:, t, :], b_first[t][:], ACT.Tanh)
         for t in range(4):
             acc = bank([P, HALF], t)
-            left_product(acc[:], t, 0, HALF)
-            nc.scalar.activation(tanh_a_first[t][:], acc[:], ACT.Tanh)
+            for a in range(PASSES):
+                right_pass(acc[:], a, t, 1)
+            nc.scalar.activation(tanh_b[1][:, t, :], acc[:], ACT.Tanh)
 
         tanh_a, gained, agree = {}, {}, {}
 
         def left_quarter(q):
             tanh_a[q] = held([P, 4 * QUARTER], F32, "tanh_a%d" % q)
             for pair in range(2):
-                acc = upper([P, 2, QUARTER], "a_acc%d%d" % (q, pair), 2 * (q - 2) + pair)
+                acc = bank([P, 2, QUARTER], 4 + 2 * (q - 2) + pair)
                 for i in range(2):
-                    left_product(acc[:, i, :], 2 * pair + i, q * QUARTER, QUARTER)
+                    for a in range(PASSES):
+                        left_pass(acc[:, i, :], a, 2 * pair + i, q * QUARTER, QUARTER)
                 nc.scalar.activation(
                     tanh_a[q][:, pair * HALF : (pair + 1) * HALF], acc[:].rearrange("p t c -> p (t c)"), ACT.Tanh
                 )
@@ -211,31 +241,15 @@ def tile_list_record_match_scores_kernel(
                 if width > 0:
                     nc.scalar.activation(
                         gained[q][:, t * QUARTER : t * QUARTER + width],
-                        tanh_b[:, 1, t, c0 : c0 + width],
+                        tanh_b[1][:, t, c0 : c0 + width],
                         ACT.Copy,
                         scale=gain[:, t, 0:1],
                     )
 
-        for q in POOL_COLS:
-            left_quarter(q)
-            apply_gain(q)
-
-        wk_w = placed([P, PASSES, 4, P], I32, "wk_w", 19456)
-        wk_sc = placed([P, 4, P], U8, "wk_sc", 23552)
-        nc.vector.tensor_copy(
-            wk_w[:].rearrange("p a t (b e) -> p a t b e", e=8),
-            wk_raw[:].rearrange("p a (b t e) -> p a t b e", t=4, e=8),
-        )
-        nc.vector.tensor_copy(
-            wk_sc[:].bitcast(I32).rearrange("p t (b w) -> p t b w", w=2),
-            wk_sc_raw[:].rearrange("p (b t w) -> p t b w", t=4, w=2),
-        )
-        key_sc = placed([P, S], U8, "key_sc", 18432)
-        gather_scales(key_sc[:], list_k, 0, S)
-        key = placed([P, PASSES * S], U32, "key", 24064)
-        gather_words(key[:, :S], list_k, 0, 0, S)
-        gather_words(key[:, S : S + QUARTER], list_k, 1, 0, QUARTER)
-        gather_words(key[:, S + QUARTER :], list_k, 1, QUARTER, S)
+        left_quarter(2)
+        apply_gain(2)
+        left_quarter(3)
+        apply_gain(3)
 
         agree[0] = held([P, 4 * HALF], F32, "agree0")
         for t in range(4):
@@ -243,7 +257,7 @@ def tile_list_record_match_scores_kernel(
                 agree[0][:, t * HALF : (t + 1) * HALF],
                 tanh_a_first[t][:],
                 gain[:, t, 0:1],
-                tanh_b[:, 0, t, :],
+                tanh_b[0][:, t, :],
                 ALU.mult,
                 ALU.mult,
             )
@@ -261,7 +275,7 @@ def tile_list_record_match_scores_kernel(
                         agree[j0][:, cols],
                         tanh_a[q][:, cols],
                         gain[:, t, 0:1],
-                        tanh_b[:, 1, t, j0 - HALF + skip : j0 - HALF + QUARTER],
+                        tanh_b[1][:, t, j0 - HALF + skip : j0 - HALF + QUARTER],
                         ALU.mult,
                         ALU.mult,
                     )
@@ -285,7 +299,7 @@ def tile_list_record_match_scores_kernel(
 
         def score(j0, j1, number):
             width = j1 - j0
-            acc = upper([P, 2, width], "score%d" % j0, number)
+            acc = bank([P, 2, width], 4 + number)
             for m in range(2):
                 nc.tensor.matmul_mx(
                     out=acc[:, m, :],
@@ -311,9 +325,9 @@ def tile_list_record_match_scores_kernel(
                         mx(
                             key_sum[j0][:, t, :],
                             a,
-                            wk_w[:, a, t, :].bitcast(FP8X4),
-                            wk_sc[4 * a : P, t, :],
-                            key[:, a * S + j0 : a * S + j0 + P].bitcast(FP8X4),
+                            wk_w[:, a, t * P : (t + 1) * P].bitcast(FP8X4),
+                            wk_sc[4 * a : P, 0, t * 32 : (t + 1) * 32].bitcast(U8),
+                            key[a][:, j0 : j0 + P].bitcast(FP8X4),
                             key_sc[4 * a : P, j0 : j0 + P],
                         )
             c0 = j0 - start

@@ -50,17 +50,15 @@ def tile_list_record_match_scores_kernel(
         tab_w = [held([P, T], I32, "tab_w0"), placed([P, T], I32, "tab_w1", 16384)]
         wo_raw = placed([P, 4, N], F32, "wo_raw", 8192)
         wr_raw = held([P, PASSES, H // 2], I32, "wr_raw")
-        wr_sc_raw = held([P, PASSES, H // 4], I32, "wr_sc_raw")
+        w_sc_raw = held([P, 3, H // 4], I32, "w_sc_raw")
         wl_raw = [placed([P, 4, H], F32, "wl_raw0", 8192), placed([P, 4, H], F32, "wl_raw1", 0)]
         right_sc = [placed([P, S // 4], I32, "right_sc0", 24576), placed([P, S // 4], I32, "right_sc1", 36864)]
-        wk_sc_raw = placed([P, 1, H // 4], I32, "wk_sc_raw", 12288)
         wk_raw = placed([P, PASSES, H], I32, "wk_raw", 25600)
         gain = placed([P, 4, 8], F32, "gain", 12800)
 
-        wr_sc = placed([P, PASSES, H // 4], I32, "wr_sc", 37888)
-        wk_sc = placed([P, 1, H // 4], I32, "wk_sc", 38912)
 
         nc.gpsimd.memset(tab_sc[:], 0)
+        nc.gpsimd.memset(w_sc_raw[:], 0)
         nc.vector.memset(tab_sc_flat[32:64, :], 0)
         nc.vector.memset(tab_sc_flat[64:128, :], 0)
 
@@ -83,16 +81,18 @@ def tile_list_record_match_scores_kernel(
             nc.sync.dma_start(tab_sc[32 * q : 32 * q + 8, :], tab_scales[:, 4 * q : 4 * q + 4, :].bitcast(I32))
         load_wl(0)
         nc.sync.dma_start(list_k[:], offs3)
+        for q in range(4):
+            nc.sync.dma_start(w_sc_raw[32 * q : 32 * q + 8, 2, :], wk_scales[:, 4 * q : 4 * q + 4, :].bitcast(I32))
+        load_table(0)
         nc.sync.dma_start(wr_raw[:], wr_words.bitcast(I32).rearrange("a p w -> p a w"))
         for q in range(4):
             nc.sync.dma_start(
-                wr_sc_raw[32 * q : 32 * q + 4, :, :],
+                w_sc_raw[32 * q : 32 * q + 4, 0:2, :],
                 wr_scales[:, 4 * q : 4 * q + 4, :].bitcast(I32).rearrange("a r w -> r a w"),
             )
-        load_table(0)
         load_wl(1)
 
-        right_flat = placed([P, S], U8, "right_flat", 38912)
+        right_flat = held([P, S], U8, "right_flat")
         left_sc = held([P, S], U8, "left_sc")
         key_sc = held([P, S], U8, "key_sc")
         gather_scales(right_flat[:], tab_sc_flat, list_r)
@@ -110,8 +110,6 @@ def tile_list_record_match_scores_kernel(
         place_right_rows(1)
         for t in range(4):
             nc.sync.dma_start(wo_raw[:, t, :], wo.rearrange("(b t e) n -> t b e n", t=4, e=8)[t])
-        for q in range(4):
-            nc.sync.dma_start(wk_sc_raw[32 * q : 32 * q + 8, 0, :], wk_scales[:, 4 * q : 4 * q + 4, :].bitcast(I32))
         with nc.allow_non_contiguous_dma(reason="one gain to a partition"):
             for t in range(4):
                 nc.sync.dma_start(gain[:, t, 0:1], g.rearrange("(b t e) -> t b e", t=4, e=8)[t])
@@ -139,19 +137,12 @@ def tile_list_record_match_scores_kernel(
 
         wr_w = held([P, PASSES, H // 2], U32, "wr_w")
         wk_w = held([P, PASSES, H], U32, "wk_w")
+        w_sc = held([P, 3, H // 4], U32, "w_sc")
         round_wl(0)
         deal(wr_w[:], wr_raw[:], 4)
-        for q in range(4):
-            deal(wr_sc[32 * q : 32 * q + 4], wr_sc_raw[32 * q : 32 * q + 4], 2)
+        deal(w_sc[:], w_sc_raw[:], 2)
         round_wl(1)
         deal(wk_w[:], wk_raw[:], 8)
-        wo_bf = held([P, 4 * N], BF16, "wo_bf")
-        nc.scalar.copy(
-            wo_bf[:].rearrange("p (c i t) -> p c t i", i=4, t=4),
-            wo_raw[:].rearrange("p t (c i) -> p c t i", i=4),
-        )
-        for q in range(4):
-            deal(wk_sc[32 * q : 32 * q + 8], wk_sc_raw[32 * q : 32 * q + 8], 2)
 
         right0 = held([P, S], U32, "right0")
         left0 = [held([P, HALF], U32, "left0_0"), held([P, HALF], U32, "left0_1")]
@@ -184,7 +175,7 @@ def tile_list_record_match_scores_kernel(
                 acc,
                 a,
                 wr_w[:, a, t * 64 : (t + 1) * 64].bitcast(U8).bitcast(FP4X4),
-                wr_sc[:, a, t * 32 : (t + 1) * 32].bitcast(U8),
+                w_sc[:, a, t * 32 : (t + 1) * 32].bitcast(U8),
                 words[a].bitcast(FP8X4),
                 right_sc[a][:].bitcast(U8)[:, cols],
             )
@@ -248,6 +239,11 @@ def tile_list_record_match_scores_kernel(
 
         left_quarter(2)
         apply_gain(2)
+        wo_bf = held([P, 4 * N], BF16, "wo_bf")
+        nc.scalar.copy(
+            wo_bf[:].rearrange("p (c i t) -> p c t i", i=4, t=4),
+            wo_raw[:].rearrange("p t (c i) -> p c t i", i=4),
+        )
         left_quarter(3)
         apply_gain(3)
 
@@ -326,7 +322,7 @@ def tile_list_record_match_scores_kernel(
                             key_sum[j0][:, t, :],
                             a,
                             wk_w[:, a, t * P : (t + 1) * P].bitcast(FP8X4),
-                            wk_sc[4 * a : P, 0, t * 32 : (t + 1) * 32].bitcast(U8),
+                            w_sc[4 * a : P, 2, t * 32 : (t + 1) * 32].bitcast(U8),
                             key[a][:, j0 : j0 + P].bitcast(FP8X4),
                             key_sc[4 * a : P, j0 : j0 + P],
                         )

@@ -20,7 +20,6 @@ P = 128
 PASSES = K // 512
 HALF = S // 2
 QUARTER = S // 4
-POOL_COLS = {2: 768, 3: 384}
 
 
 def tile_list_record_match_scores_kernel(
@@ -54,7 +53,7 @@ def tile_list_record_match_scores_kernel(
         wl_raw = [placed([P, 4, H], F32, "wl_raw0", 8192), placed([P, 4, H], F32, "wl_raw1", 0)]
         right_sc = [placed([P, S // 4], I32, "right_sc0", 24576), placed([P, S // 4], I32, "right_sc1", 36864)]
         wk_raw = placed([P, PASSES, H], I32, "wk_raw", 25600)
-        gain = placed([P, 4, 8], F32, "gain", 12800)
+        gain = [placed([P, 8], F32, "gain%d" % t, (12288, 16320, 14336, 12352)[t]) for t in range(4)]
 
 
         nc.gpsimd.memset(tab_sc[:], 0)
@@ -112,7 +111,7 @@ def tile_list_record_match_scores_kernel(
             nc.sync.dma_start(wo_raw[:, t, :], wo.rearrange("(b t e) n -> t b e n", t=4, e=8)[t])
         with nc.allow_non_contiguous_dma(reason="one gain to a partition"):
             for t in range(4):
-                nc.sync.dma_start(gain[:, t, 0:1], g.rearrange("(b t e) -> t b e", t=4, e=8)[t])
+                nc.sync.dma_start(gain[t][:, 0:1], g.rearrange("(b t e) -> t b e", t=4, e=8)[t])
 
         wl_w = held([P, PASSES, H], U32, "wl_w")
         wl_sc = held([P, PASSES, H], U8, "wl_sc")
@@ -143,6 +142,11 @@ def tile_list_record_match_scores_kernel(
         deal(w_sc[:], w_sc_raw[:], 2)
         round_wl(1)
         deal(wk_w[:], wk_raw[:], 8)
+        wo_bf = held([P, 4 * N], BF16, "wo_bf")
+        nc.scalar.copy(
+            wo_bf[:].rearrange("p (c i t) -> p c t i", i=4, t=4),
+            wo_raw[:].rearrange("p t (c i) -> p c t i", i=4),
+        )
 
         right0 = held([P, S], U32, "right0")
         left0 = [held([P, HALF], U32, "left0_0"), held([P, HALF], U32, "left0_1")]
@@ -168,9 +172,9 @@ def tile_list_record_match_scores_kernel(
                 out=acc, lhsT=lhs, lhsT_scale=lhs_sc, rhs=rhs, rhs_scale=rhs_sc, start=(a == 0), stop=(a == PASSES - 1)
             )
 
-        def right_pass(acc, a, t, half):
-            cols = slice(half * HALF, (half + 1) * HALF)
-            words = [right0[:, cols], right1[half][:]]
+        def right_pass(acc, a, t, j0, width):
+            cols = slice(j0, j0 + width)
+            words = [right0[:, cols], right1[j0 // HALF][:, j0 % HALF : j0 % HALF + width]]
             mx(
                 acc,
                 a,
@@ -192,95 +196,64 @@ def tile_list_record_match_scores_kernel(
                 left_sc[4 * a : P, j0 : j0 + width],
             )
 
-        tanh_b = [held([P, 4, HALF], F32, "tanh_b%d" % half) for half in range(2)]
-        tanh_a_first = [held([P, HALF], F32, "tanh_a_first%d" % t) for t in range(4)]
+        tanh_b_first = held([P, 4, HALF], F32, "tanh_b_first")
+        tanh_a_first = [placed([P, HALF], F32, "tanh_a_first0", 8192)]
+        tanh_a_first += [held([P, HALF], F32, "tanh_a_first%d" % t) for t in range(1, 4)]
         a_first = [bank([P, HALF], t) for t in range(4)]
         b_first = [bank([P, HALF], 4 + t) for t in range(4)]
         for a in range(PASSES):
             for t in range(4):
                 left_pass(a_first[t][:], a, t, 0, HALF)
             for t in range(4):
-                right_pass(b_first[t][:], a, t, 0)
+                right_pass(b_first[t][:], a, t, 0, HALF)
         for t in range(4):
             nc.scalar.activation(tanh_a_first[t][:], a_first[t][:], ACT.Tanh)
         for t in range(4):
-            nc.scalar.activation(tanh_b[0][:, t, :], b_first[t][:], ACT.Tanh)
-        for t in range(4):
-            acc = bank([P, HALF], t)
-            for a in range(PASSES):
-                right_pass(acc[:], a, t, 1)
-            nc.scalar.activation(tanh_b[1][:, t, :], acc[:], ACT.Tanh)
+            nc.scalar.activation(tanh_b_first[:, t, :], b_first[t][:], ACT.Tanh)
 
-        tanh_a, gained, agree = {}, {}, {}
-
-        def left_quarter(q):
-            tanh_a[q] = held([P, 4 * QUARTER], F32, "tanh_a%d" % q)
-            for pair in range(2):
-                acc = bank([P, 2, QUARTER], 4 + 2 * (q - 2) + pair)
-                for i in range(2):
+        def tanh_of(side_pass, name, j0, width, first_bank):
+            result = held([P, 4, width], F32, name)
+            tiles = HALF // width
+            for t0 in range(0, 4, tiles):
+                acc = bank([P, tiles, width], first_bank + t0 // tiles)
+                for i in range(tiles):
                     for a in range(PASSES):
-                        left_pass(acc[:, i, :], a, 2 * pair + i, q * QUARTER, QUARTER)
-                nc.scalar.activation(
-                    tanh_a[q][:, pair * HALF : (pair + 1) * HALF], acc[:].rearrange("p t c -> p (t c)"), ACT.Tanh
-                )
+                        side_pass(acc[:, i, :], a, t0 + i, j0, width)
+                nc.scalar.activation(result[:, t0 : t0 + tiles, :], acc[:], ACT.Tanh)
+            return result
 
-        def apply_gain(q):
-            c0 = q * QUARTER - HALF
-            gained[q] = held([P, POOL_COLS[q]], F32, "gained%d" % q)
+        def with_gain(tanh_b, name, width):
+            gained = held([P, 4, width], F32, name)
             for t in range(4):
-                width = min(QUARTER, POOL_COLS[q] - t * QUARTER)
-                if width > 0:
-                    nc.scalar.activation(
-                        gained[q][:, t * QUARTER : t * QUARTER + width],
-                        tanh_b[1][:, t, c0 : c0 + width],
-                        ACT.Copy,
-                        scale=gain[:, t, 0:1],
-                    )
+                nc.scalar.activation(gained[:, t, :], tanh_b[:, t, :], ACT.Copy, scale=gain[t][:, 0:1])
+            return gained
 
-        left_quarter(2)
-        apply_gain(2)
-        wo_bf = held([P, 4 * N], BF16, "wo_bf")
-        nc.scalar.copy(
-            wo_bf[:].rearrange("p (c i t) -> p c t i", i=4, t=4),
-            wo_raw[:].rearrange("p t (c i) -> p c t i", i=4),
-        )
-        left_quarter(3)
-        apply_gain(3)
+        b_third = tanh_of(right_pass, "tanh_b_third", 512, QUARTER, 0)
+        a_third = tanh_of(left_pass, "tanh_a_third", 512, QUARTER, 2)
+        gained_third = with_gain(b_third, "gained_third", QUARTER)
+        b_last = tanh_of(right_pass, "tanh_b_last", 896, P, 4)
+        a_last = tanh_of(left_pass, "tanh_a_last", 896, P, 5)
+        b_sixth = tanh_of(right_pass, "tanh_b_sixth", 768, P, 6)
+        a_sixth = tanh_of(left_pass, "tanh_a_sixth", 768, P, 7)
+        gained_sixth = with_gain(b_sixth, "gained_sixth", P)
 
-        agree[0] = held([P, 4 * HALF], F32, "agree0")
+        def product(dst, tanh_a, tanh_b, t):
+            nc.vector.scalar_tensor_tensor(dst, tanh_a, gain[t][:, 0:1], tanh_b, ALU.mult, ALU.mult)
+
+        def flat(tile):
+            return tile[:].rearrange("p t c -> p (t c)")
+
+        agree_first = held([P, 4, HALF], F32, "agree_first")
         for t in range(4):
-            nc.vector.scalar_tensor_tensor(
-                agree[0][:, t * HALF : (t + 1) * HALF],
-                tanh_a_first[t][:],
-                gain[:, t, 0:1],
-                tanh_b[0][:, t, :],
-                ALU.mult,
-                ALU.mult,
-            )
-
-        def agreement(q, slot):
-            j0 = q * QUARTER
-            agree[j0] = held([P, 4 * QUARTER], F32, "agree%d" % j0, slot)
-            first = POOL_COLS[q]
-            nc.gpsimd.tensor_tensor(agree[j0][:, :first], tanh_a[q][:, :first], gained[q][:], ALU.mult)
-            for t in range(4):
-                skip = max(0, first - t * QUARTER)
-                if skip < QUARTER:
-                    cols = slice(t * QUARTER + skip, (t + 1) * QUARTER)
-                    nc.vector.scalar_tensor_tensor(
-                        agree[j0][:, cols],
-                        tanh_a[q][:, cols],
-                        gain[:, t, 0:1],
-                        tanh_b[1][:, t, j0 - HALF + skip : j0 - HALF + QUARTER],
-                        ALU.mult,
-                        ALU.mult,
-                    )
-
+            product(agree_first[:, t, :], tanh_a_first[t][:], tanh_b_first[:, t, :], t)
         wo_w = held([P, N], U32, "wo_w", "tanh_a_first2")
         wo_sc = held([P, N], U8, "wo_sc")
         nc.vector.quantize_mx(out=wo_w[:].bitcast(FP8X4), scales=wo_sc[:], in_=wo_bf[:])
-        h_bf = held([P, 4 * S], BF16, "h_bf")
-        h_w = held([P, S], U32, "h_w")
+        agree_third = held([P, 4, QUARTER], F32, "agree_third", "tanh_a_first3")
+        nc.gpsimd.tensor_tensor(flat(agree_third), flat(a_third), flat(gained_third), ALU.mult)
+
+        h_bf = {0: held([P, 4 * HALF], BF16, "h_bf0"), 768: held([P, 4 * QUARTER], BF16, "h_bf768")}
+        h_w = placed([P, S], U32, "h_w", 16320)
         h_sc = held([P, S], U8, "h_sc")
         out_v = out.rearrange("(m p) j -> p m j", p=P)
 
@@ -288,7 +261,8 @@ def tile_list_record_match_scores_kernel(
             return h_w[:, j0:j1].bitcast(FP8X4)
 
         def h_values(j0, j1):
-            return h_bf[:, 4 * j0 : 4 * j1]
+            start = max(j for j in h_bf if j <= j0)
+            return h_bf[start][:, 4 * (j0 - start) : 4 * (j1 - start)]
 
         def quantize_h(j0, j1):
             nc.vector.quantize_mx(out=h_words(j0, j1), scales=h_sc[:, j0:j1], in_=h_values(j0, j1))
@@ -308,49 +282,56 @@ def tile_list_record_match_scores_kernel(
                 )
             res = res_pool.tile([P, 2, width], F32, name="res")
             nc.scalar.copy(res[:], acc[:])
-            (nc.scalar if j1 == S else nc.sync).dma_start(out_v[:, :, j0:j1], res[:])
+            return res
 
-        key_sum = {}
+        def store(j0, j1, res, queue):
+            queue.dma_start(out_v[:, :, j0:j1], res[:])
 
-        def subtract_key(j0, start, width=P):
-            b0 = j0 % P
-            if b0 == 0:
-                key_sum[j0] = bank([P, 4, P], j0 // P % 4)
-                for t in range(4):
-                    for a in range(PASSES):
-                        mx(
-                            key_sum[j0][:, t, :],
-                            a,
-                            wk_w[:, a, t * P : (t + 1) * P].bitcast(FP8X4),
-                            w_sc[4 * a : P, 2, t * 32 : (t + 1) * 32].bitcast(U8),
-                            key[a][:, j0 : j0 + P].bitcast(FP8X4),
-                            key_sc[4 * a : P, j0 : j0 + P],
-                        )
-            c0 = j0 - start
+        def key_product(j0, number):
+            acc = bank([P, 4, P], number)
+            for t in range(4):
+                for a in range(PASSES):
+                    mx(
+                        acc[:, t, :],
+                        a,
+                        wk_w[:, a, t * P : (t + 1) * P].bitcast(FP8X4),
+                        w_sc[4 * a : P, 2, t * 32 : (t + 1) * 32].bitcast(U8),
+                        key[a][:, j0 : j0 + P].bitcast(FP8X4),
+                        key_sc[4 * a : P, j0 : j0 + P],
+                    )
+            return acc
+
+        def subtract(j0, agree, key_sum):
+            width = agree.shape[2]
             nc.vector.tensor_tensor(
                 h_values(j0, j0 + width).rearrange("p (c i t) -> p c t i", i=2, t=4),
-                agree[start][:].rearrange("p (t c) -> p t c", t=4)[:, :, c0 : c0 + width].rearrange("p t (c i) -> p c t i", i=2),
-                key_sum[j0 - b0][:, :, b0 : b0 + width].rearrange("p t (c i) -> p c t i", i=2),
+                agree.rearrange("p t (c i) -> p c t i", i=2),
+                key_sum.rearrange("p t (c i) -> p c t i", i=2),
                 ALU.subtract,
             )
 
-        for j0 in range(0, HALF, P):
-            subtract_key(j0, 0)
-        agreement(2, "tanh_a_first3")
+        def finish(j0, j1, number, queue):
+            quantize_h(j0, j1)
+            store(j0, j1, score(j0, j1, number), queue)
+
+        for block in range(4):
+            subtract(block * P, agree_first[:, :, block * P : (block + 1) * P], key_product(block * P, block)[:])
+        agree_last = held([P, 4, P], F32, "agree_last", "agree_first")
+        for t in range(4):
+            product(agree_last[:, t, :], a_last[:, t, :], b_last[:, t, :], t)
         quantize_h(0, 512)
-        score(0, 256, 0)
-        score(256, 512, 1)
-        for j0 in (512, 640):
-            subtract_key(j0, 512)
-        agreement(3, "tanh_a2")
-        quantize_h(512, 768)
-        score(512, 768, 2)
-        subtract_key(768, 768)
-        subtract_key(896, 768, 64)
-        quantize_h(768, 896)
-        score(768, 896, 3)
-        subtract_key(960, 768, 64)
-        quantize_h(896, 960)
-        score(896, 960, 0)
-        quantize_h(960, 1024)
-        score(960, 1024, 1)
+        store(0, 256, score(0, 256, 0), nc.sync)
+        store(256, 512, score(256, 512, 1), nc.sync)
+        agree_sixth = held([P, 4, P], F32, "agree_sixth", "h_bf0")
+        nc.gpsimd.tensor_tensor(flat(agree_sixth), flat(a_sixth), flat(gained_sixth), ALU.mult)
+        h_bf[512] = placed([P, 4 * QUARTER], BF16, "h_bf512", 12416)
+        for block in range(2):
+            subtract(512 + block * P, agree_third[:, :, block * P : (block + 1) * P], key_product(512 + block * P, block)[:])
+        subtract(896, agree_last[:], key_product(896, 2)[:])
+        finish(512, 768, 2, nc.sync)
+        key_sum = key_product(768, 3)
+        subtract(768, agree_sixth[:, :, 0:64], key_sum[:, :, 0:64])
+        finish(896, 1024, 3, nc.sync)
+        subtract(832, agree_sixth[:, :, 64:128], key_sum[:, :, 64:128])
+        finish(768, 832, 0, nc.sync)
+        finish(832, 896, 1, nc.scalar)

@@ -57,7 +57,7 @@ def tile_list_record_match_scores_kernel(
 
 
         nc.gpsimd.memset(tab_sc[:], 0)
-        nc.gpsimd.memset(w_sc_raw[:], 0)
+        nc.vector.memset(w_sc_raw[:], 0)
         nc.vector.memset(tab_sc_flat[32:64, :], 0)
         nc.vector.memset(tab_sc_flat[64:128, :], 0)
 
@@ -74,7 +74,7 @@ def tile_list_record_match_scores_kernel(
             nc.vector.tensor_copy(dst, tab_w[a][:].bitcast(U32).indirect(lst[:, j0 // 16 : j1 // 16]))
 
         nc.sync.dma_start(list_r[:], offs2)
-        nc.sync.dma_start(tab_sc_flat[0:32, :], tab_scales.rearrange("a q t -> (a q) t").bitcast(I32))
+        nc.scalar.dma_start(tab_sc_flat[0:32, :], tab_scales.rearrange("a q t -> (a q) t").bitcast(I32))
         nc.sync.dma_start(list_l[:], offs)
         for q in range(4):
             nc.sync.dma_start(tab_sc[32 * q : 32 * q + 8, :], tab_scales[:, 4 * q : 4 * q + 4, :].bitcast(I32))

@@ -29,7 +29,7 @@ def tile_list_record_match_scores_kernel(
     with ExitStack() as ctx:
         keep = ctx.enter_context(tc.tile_pool(name="keep", bufs=1))
         laid = ctx.enter_context(tc.tile_pool(name="laid", bufs=1))
-        res_pool = ctx.enter_context(tc.tile_pool(name="res", bufs=6))
+        res_pool = ctx.enter_context(tc.tile_pool(name="res", bufs=7))
         acc_pool = ctx.enter_context(tc.psum_pool(name="acc", bufs=1))
 
         def held(shape, dtype, name, slot=None):
@@ -44,20 +44,21 @@ def tile_list_record_match_scores_kernel(
         list_l = keep.tile([P, S // 16], U16, name="list_l")
         list_r = keep.tile([P, S // 16], U16, name="list_r")
         list_k = keep.tile([P, S // 16], U16, name="list_k")
-        tab_sc = placed([P, T // 4], I32, "tab_sc", 36864)
-        tab_sc_flat = placed([P, T // 4], I32, "tab_sc_flat", 24064)
-        tab_w = [held([P, T], I32, "tab_w0"), placed([P, T], I32, "tab_w1", 16384)]
-        wo_raw = placed([P, 4, N], F32, "wo_raw", 8192)
+        tab_sc = placed([P, T // 4], I32, "tab_sc", 54272)
+        tab_sc_flat = placed([P, T // 4], I32, "tab_sc_flat", 44544)
+        tab_w = [held([P, T], I32, "tab_w0"), placed([P, T], I32, "tab_w1", 36864)]
+        wo_raw = placed([P, 4, N], F32, "wo_raw", 24512)
         wr_raw = held([P, PASSES, H // 2], I32, "wr_raw")
-        w_sc_raw = held([P, 3, H // 4], I32, "w_sc_raw")
-        wl_raw = [placed([P, 4, H], F32, "wl_raw0", 8192), placed([P, 4, H], F32, "wl_raw1", 0)]
-        right_sc = [placed([P, S // 4], I32, "right_sc0", 24576), placed([P, S // 4], I32, "right_sc1", 36864)]
-        wk_raw = placed([P, PASSES, H], I32, "wk_raw", 25600)
-        gain = [placed([P, 8], F32, "gain%d" % t, (12288, 16320, 14336, 12352)[t]) for t in range(4)]
+        wr_sc_raw = held([P, PASSES, H // 4], I32, "wr_sc_raw")
+        wk_sc_raw = placed([P, 1, H // 4], I32, "wk_sc_raw", 61696)
+        wl_raw = [placed([P, 4, H], F32, "wl_raw0", 16384), placed([P, 4, H], F32, "wl_raw1", 0)]
+        right_sc = [placed([P, S // 4], I32, "right_sc0", 45056), placed([P, S // 4], I32, "right_sc1", 54272)]
+        wk_raw = placed([P, PASSES, H], I32, "wk_raw", 46080)
+        gain = [placed([P, 8], F32, "gain%d" % t, (61568, 62208, 61440, 61632)[t]) for t in range(4)]
 
 
         nc.gpsimd.memset(tab_sc[:], 0)
-        nc.vector.memset(w_sc_raw[:], 0)
+        nc.vector.memset(wr_sc_raw[:], 0)
         nc.vector.memset(tab_sc_flat[32:64, :], 0)
         nc.vector.memset(tab_sc_flat[64:128, :], 0)
 
@@ -80,13 +81,11 @@ def tile_list_record_match_scores_kernel(
             nc.sync.dma_start(tab_sc[32 * q : 32 * q + 8, :], tab_scales[:, 4 * q : 4 * q + 4, :].bitcast(I32))
         load_wl(0)
         nc.sync.dma_start(list_k[:], offs3)
-        for q in range(4):
-            nc.sync.dma_start(w_sc_raw[32 * q : 32 * q + 8, 2, :], wk_scales[:, 4 * q : 4 * q + 4, :].bitcast(I32))
         load_table(0)
         nc.sync.dma_start(wr_raw[:], wr_words.bitcast(I32).rearrange("a p w -> p a w"))
         for q in range(4):
             nc.sync.dma_start(
-                w_sc_raw[32 * q : 32 * q + 4, 0:2, :],
+                wr_sc_raw[32 * q : 32 * q + 4, :, :],
                 wr_scales[:, 4 * q : 4 * q + 4, :].bitcast(I32).rearrange("a r w -> r a w"),
             )
         load_wl(1)
@@ -109,13 +108,10 @@ def tile_list_record_match_scores_kernel(
         place_right_rows(1)
         for t in range(4):
             nc.sync.dma_start(wo_raw[:, t, :], wo.rearrange("(b t e) n -> t b e n", t=4, e=8)[t])
-        with nc.allow_non_contiguous_dma(reason="one gain to a partition"):
-            for t in range(4):
-                nc.sync.dma_start(gain[t][:, 0:1], g.rearrange("(b t e) -> t b e", t=4, e=8)[t])
 
         wl_w = held([P, PASSES, H], U32, "wl_w")
         wl_sc = held([P, PASSES, H], U8, "wl_sc")
-        wl_bf = [held([P, 4, 4 * P], BF16, "wl_bf%d" % a) for a in range(PASSES)]
+        wl_bf = [placed([P, 4, 4 * P], BF16, "wl_bf0", 61440), held([P, 4, 4 * P], BF16, "wl_bf1")]
 
         def round_wl(a):
             dst = wl_bf[a][:].rearrange("p t (b y e j) -> p y t b j e", y=2, e=4, j=4)
@@ -136,10 +132,11 @@ def tile_list_record_match_scores_kernel(
 
         wr_w = held([P, PASSES, H // 2], U32, "wr_w")
         wk_w = held([P, PASSES, H], U32, "wk_w")
-        w_sc = held([P, 3, H // 4], U32, "w_sc")
+        wr_sc = held([P, PASSES, H // 4], U32, "wr_sc")
+        wk_sc = held([P, 1, H // 4], U32, "wk_sc")
         round_wl(0)
         deal(wr_w[:], wr_raw[:], 4)
-        deal(w_sc[:], w_sc_raw[:], 2)
+        deal(wr_sc[:], wr_sc_raw[:], 2)
         round_wl(1)
         deal(wk_w[:], wk_raw[:], 8)
         wo_bf = held([P, 4 * N], BF16, "wo_bf")
@@ -148,24 +145,27 @@ def tile_list_record_match_scores_kernel(
             wo_raw[:].rearrange("p t (c i) -> p c t i", i=4),
         )
 
-        right0 = held([P, S], U32, "right0")
-        left0 = [held([P, HALF], U32, "left0_0"), held([P, HALF], U32, "left0_1")]
-        right1 = [placed([P, HALF], U32, "right1_0", 6144), placed([P, HALF], U32, "right1_1", 2048)]
-        left1 = [placed([P, HALF], U32, "left1_0", 0), placed([P, HALF], U32, "left1_1", 4096)]
-        key_words = placed([P, PASSES * S], U32, "key_words", 25600)
+        right0 = placed([P, S], U32, "right0", 12352)
+        left0 = [held([P, HALF], U32, "left0_0"), placed([P, HALF], U32, "left0_1", 16448)]
+        right1 = placed([P, S], U32, "right1", 4096)
+        left1 = [placed([P, HALF], U32, "left1_%d" % half, 2048 * half) for half in range(2)]
+        key_words = placed([P, PASSES * S], U32, "key_words", 46080)
         key = [key_words[:, a * S : (a + 1) * S] for a in range(PASSES)]
-        quantize_wl(0)
         gather_words(left0[0][:], list_l, 0, 0, HALF)
+        quantize_wl(0)
+        for q in range(4):
+            nc.sync.dma_start(wk_sc_raw[32 * q : 32 * q + 8, 0, :], wk_scales[:, 4 * q : 4 * q + 4, :].bitcast(I32))
+        with nc.allow_non_contiguous_dma(reason="one gain to a partition"):
+            for t in range(4):
+                nc.sync.dma_start(gain[t][:, 0:1], g.rearrange("(b t e) -> t b e", t=4, e=8)[t])
         gather_words(right0[:], list_r, 0, 0, S)
         gather_words(left0[1][:], list_l, 0, HALF, S)
         quantize_wl(1)
         gather_words(left1[0][:], list_l, 1, 0, HALF)
-        gather_words(right1[0][:], list_r, 1, 0, HALF)
-        gather_words(right1[1][:], list_r, 1, HALF, S)
+        gather_words(right1[:], list_r, 1, 0, S)
         gather_words(left1[1][:], list_l, 1, HALF, S)
         gather_words(key[0], list_k, 0, 0, S)
-        gather_words(key[1][:, :QUARTER], list_k, 1, 0, QUARTER)
-        gather_words(key[1][:, QUARTER:], list_k, 1, QUARTER, S)
+        gather_words(key[1], list_k, 1, 0, S)
 
         def mx(acc, a, lhs, lhs_sc, rhs, rhs_sc):
             nc.tensor.matmul_mx(
@@ -174,12 +174,12 @@ def tile_list_record_match_scores_kernel(
 
         def right_pass(acc, a, t, j0, width):
             cols = slice(j0, j0 + width)
-            words = [right0[:, cols], right1[j0 // HALF][:, j0 % HALF : j0 % HALF + width]]
+            words = [right0[:, cols], right1[:, cols]]
             mx(
                 acc,
                 a,
                 wr_w[:, a, t * 64 : (t + 1) * 64].bitcast(U8).bitcast(FP4X4),
-                w_sc[:, a, t * 32 : (t + 1) * 32].bitcast(U8),
+                wr_sc[:, a, t * 32 : (t + 1) * 32].bitcast(U8),
                 words[a].bitcast(FP8X4),
                 right_sc[a][:].bitcast(U8)[:, cols],
             )
@@ -196,9 +196,10 @@ def tile_list_record_match_scores_kernel(
                 left_sc[4 * a : P, j0 : j0 + width],
             )
 
-        tanh_b_first = held([P, 4, HALF], F32, "tanh_b_first")
-        tanh_a_first = [placed([P, HALF], F32, "tanh_a_first0", 8192)]
-        tanh_a_first += [held([P, HALF], F32, "tanh_a_first%d" % t) for t in range(1, 4)]
+        tanh_b_first = placed([P, 4, HALF], F32, "tanh_b_first", 26688)
+        tanh_a_three = placed([P, 3, HALF], F32, "tanh_a_three", 18496)
+        tanh_a_fourth = placed([P, HALF], F32, "tanh_a_fourth", 24640)
+        tanh_a_first = [tanh_a_three[:, t, :] for t in range(3)] + [tanh_a_fourth[:]]
         a_first = [bank([P, HALF], t) for t in range(4)]
         b_first = [bank([P, HALF], 4 + t) for t in range(4)]
         for a in range(PASSES):
@@ -207,9 +208,11 @@ def tile_list_record_match_scores_kernel(
             for t in range(4):
                 right_pass(b_first[t][:], a, t, 0, HALF)
         for t in range(4):
-            nc.scalar.activation(tanh_a_first[t][:], a_first[t][:], ACT.Tanh)
+            nc.scalar.activation(tanh_a_first[t], a_first[t][:], ACT.Tanh)
         for t in range(4):
             nc.scalar.activation(tanh_b_first[:, t, :], b_first[t][:], ACT.Tanh)
+        for q in range(4):
+            deal(wk_sc[32 * q : 32 * q + 8], wk_sc_raw[32 * q : 32 * q + 8], 2)
 
         def tanh_of(side_pass, name, j0, width, first_bank):
             result = held([P, 4, width], F32, name)
@@ -232,7 +235,13 @@ def tile_list_record_match_scores_kernel(
         a_third = tanh_of(left_pass, "tanh_a_third", 512, QUARTER, 2)
         gained_third = with_gain(b_third, "gained_third", QUARTER)
         b_last = tanh_of(right_pass, "tanh_b_last", 896, P, 4)
-        a_last = tanh_of(left_pass, "tanh_a_last", 896, P, 5)
+        a_last = [placed([P, 2, P], F32, "tanh_a_last0", 65536), held([P, 2, P], F32, "tanh_a_last1")]
+        acc = bank([P, 4, P], 5)
+        for t in range(4):
+            for a in range(PASSES):
+                left_pass(acc[:, t, :], a, t, 896, P)
+        for pair in range(2):
+            nc.scalar.activation(a_last[pair][:], acc[:, 2 * pair : 2 * pair + 2, :], ACT.Tanh)
         b_sixth = tanh_of(right_pass, "tanh_b_sixth", 768, P, 6)
         a_sixth = tanh_of(left_pass, "tanh_a_sixth", 768, P, 7)
         gained_sixth = with_gain(b_sixth, "gained_sixth", P)
@@ -245,15 +254,15 @@ def tile_list_record_match_scores_kernel(
 
         agree_first = held([P, 4, HALF], F32, "agree_first")
         for t in range(4):
-            product(agree_first[:, t, :], tanh_a_first[t][:], tanh_b_first[:, t, :], t)
-        wo_w = held([P, N], U32, "wo_w", "tanh_a_first2")
+            product(agree_first[:, t, :], tanh_a_first[t], tanh_b_first[:, t, :], t)
+        wo_w = placed([P, N], U32, "wo_w", 18496)
         wo_sc = held([P, N], U8, "wo_sc")
         nc.vector.quantize_mx(out=wo_w[:].bitcast(FP8X4), scales=wo_sc[:], in_=wo_bf[:])
-        agree_third = held([P, 4, QUARTER], F32, "agree_third", "tanh_a_first3")
+        agree_third = placed([P, 4, QUARTER], F32, "agree_third", 24640)
         nc.gpsimd.tensor_tensor(flat(agree_third), flat(a_third), flat(gained_third), ALU.mult)
 
         h_bf = {0: held([P, 4 * HALF], BF16, "h_bf0"), 768: held([P, 4 * QUARTER], BF16, "h_bf768")}
-        h_w = placed([P, S], U32, "h_w", 16320)
+        h_w = placed([P, S], U32, "h_w", 65536)
         h_sc = held([P, S], U8, "h_sc")
         out_v = out.rearrange("(m p) j -> p m j", p=P)
 
@@ -267,7 +276,7 @@ def tile_list_record_match_scores_kernel(
         def quantize_h(j0, j1):
             nc.vector.quantize_mx(out=h_words(j0, j1), scales=h_sc[:, j0:j1], in_=h_values(j0, j1))
 
-        def score(j0, j1, number):
+        def score(j0, j1, number, copy=nc.scalar.copy):
             width = j1 - j0
             acc = bank([P, 2, width], 4 + number)
             for m in range(2):
@@ -281,7 +290,7 @@ def tile_list_record_match_scores_kernel(
                     stop=True,
                 )
             res = res_pool.tile([P, 2, width], F32, name="res")
-            nc.scalar.copy(res[:], acc[:])
+            copy(res[:], acc[:])
             return res
 
         def store(j0, j1, res, queue):
@@ -295,7 +304,7 @@ def tile_list_record_match_scores_kernel(
                         acc[:, t, :],
                         a,
                         wk_w[:, a, t * P : (t + 1) * P].bitcast(FP8X4),
-                        w_sc[4 * a : P, 2, t * 32 : (t + 1) * 32].bitcast(U8),
+                        wk_sc[4 * a : P, 0, t * 32 : (t + 1) * 32].bitcast(U8),
                         key[a][:, j0 : j0 + P].bitcast(FP8X4),
                         key_sc[4 * a : P, j0 : j0 + P],
                     )
@@ -318,20 +327,23 @@ def tile_list_record_match_scores_kernel(
             subtract(block * P, agree_first[:, :, block * P : (block + 1) * P], key_product(block * P, block)[:])
         agree_last = held([P, 4, P], F32, "agree_last", "agree_first")
         for t in range(4):
-            product(agree_last[:, t, :], a_last[:, t, :], b_last[:, t, :], t)
+            product(agree_last[:, t, :], a_last[t // 2][:, t % 2, :], b_last[:, t, :], t)
         quantize_h(0, 512)
         store(0, 256, score(0, 256, 0), nc.sync)
         store(256, 512, score(256, 512, 1), nc.sync)
         agree_sixth = held([P, 4, P], F32, "agree_sixth", "h_bf0")
         nc.gpsimd.tensor_tensor(flat(agree_sixth), flat(a_sixth), flat(gained_sixth), ALU.mult)
-        h_bf[512] = placed([P, 4 * QUARTER], BF16, "h_bf512", 12416)
+        h_bf[512] = placed([P, 4 * QUARTER], BF16, "h_bf512", 59456)
         for block in range(2):
             subtract(512 + block * P, agree_third[:, :, block * P : (block + 1) * P], key_product(512 + block * P, block)[:])
         subtract(896, agree_last[:], key_product(896, 2)[:])
-        finish(512, 768, 2, nc.sync)
+        quantize_h(512, 768)
+        store(512, 640, score(512, 640, 2), nc.sync)
+        store(640, 768, score(640, 768, 3), nc.sync)
         key_sum = key_product(768, 3)
         subtract(768, agree_sixth[:, :, 0:64], key_sum[:, :, 0:64])
-        finish(896, 1024, 3, nc.sync)
+        finish(896, 1024, 0, nc.sync)
         subtract(832, agree_sixth[:, :, 64:128], key_sum[:, :, 64:128])
-        finish(768, 832, 0, nc.sync)
-        finish(832, 896, 1, nc.scalar)
+        finish(768, 832, 1, nc.scalar)
+        quantize_h(832, 896)
+        store(832, 896, score(832, 896, 2, nc.vector.tensor_copy), nc.sync)

@@ -44,17 +44,17 @@ def tile_list_record_match_scores_kernel(
         list_l = keep.tile([P, S // 16], U16, name="list_l")
         list_r = keep.tile([P, S // 16], U16, name="list_r")
         list_k = keep.tile([P, S // 16], U16, name="list_k")
-        tab_sc = placed([P, T // 4], I32, "tab_sc", 54272)
-        tab_sc_flat = placed([P, T // 4], I32, "tab_sc_flat", 44544)
-        tab_w = [held([P, T], I32, "tab_w0"), placed([P, T], I32, "tab_w1", 36864)]
-        wo_raw = placed([P, 4, N], F32, "wo_raw", 24512)
+        tab_sc = placed([P, T // 4], I32, "tab_sc", 57344)
+        tab_sc_flat = placed([P, T // 4], I32, "tab_sc_flat", 78336)
+        tab_w = [held([P, T], I32, "tab_w0"), placed([P, T], I32, "tab_w1", 70656)]
+        wo_raw = placed([P, 4, N], F32, "wo_raw", 61440)
         wr_raw = held([P, PASSES, H // 2], I32, "wr_raw")
         wr_sc_raw = held([P, PASSES, H // 4], I32, "wr_sc_raw")
-        wk_sc_raw = placed([P, 1, H // 4], I32, "wk_sc_raw", 61696)
+        wk_sc_raw = placed([P, 1, H // 4], I32, "wk_sc_raw", 23040)
         wl_raw = [placed([P, 4, H], F32, "wl_raw0", 16384), placed([P, 4, H], F32, "wl_raw1", 0)]
-        right_sc = [placed([P, S // 4], I32, "right_sc0", 45056), placed([P, S // 4], I32, "right_sc1", 54272)]
-        wk_raw = placed([P, PASSES, H], I32, "wk_raw", 46080)
-        gain = [placed([P, 8], F32, "gain%d" % t, (61568, 62208, 61440, 61632)[t]) for t in range(4)]
+        right_sc = [placed([P, S // 4], I32, "right_sc0", 78848), placed([P, S // 4], I32, "right_sc1", 57344)]
+        wk_raw = placed([P, PASSES, H], I32, "wk_raw", 79872)
+        gain = [placed([P, 8], F32, "gain%d" % t, (22656, 22720, 22528, 22784)[t]) for t in range(4)]
 
 
         nc.gpsimd.memset(tab_sc[:], 0)
@@ -90,7 +90,7 @@ def tile_list_record_match_scores_kernel(
             )
         load_wl(1)
 
-        right_flat = held([P, S], U8, "right_flat")
+        right_flat = placed([P, S], U8, "right_flat", 32768)
         left_sc = held([P, S], U8, "left_sc")
         key_sc = held([P, S], U8, "key_sc")
         gather_scales(right_flat[:], tab_sc_flat, list_r)
@@ -106,8 +106,11 @@ def tile_list_record_match_scores_kernel(
         load_table(1)
         nc.sync.dma_start(wk_raw[:], wk_words.rearrange("a p r i -> p a (r i)").bitcast(I32))
         place_right_rows(1)
-        for t in range(4):
-            nc.sync.dma_start(wo_raw[:, t, :], wo.rearrange("(b t e) n -> t b e n", t=4, e=8)[t])
+        for q in range(4):
+            nc.sync.dma_start(wk_sc_raw[32 * q : 32 * q + 8, 0, :], wk_scales[:, 4 * q : 4 * q + 4, :].bitcast(I32))
+        with nc.allow_non_contiguous_dma(reason="one gain to a partition"):
+            for t in range(4):
+                nc.sync.dma_start(gain[t][:, 0:1], g.rearrange("(b t e) -> t b e", t=4, e=8)[t])
 
         wl_w = held([P, PASSES, H], U32, "wl_w")
         wl_sc = held([P, PASSES, H], U8, "wl_sc")
@@ -139,25 +142,17 @@ def tile_list_record_match_scores_kernel(
         deal(wr_sc[:], wr_sc_raw[:], 2)
         round_wl(1)
         deal(wk_w[:], wk_raw[:], 8)
-        wo_bf = held([P, 4 * N], BF16, "wo_bf")
-        nc.scalar.copy(
-            wo_bf[:].rearrange("p (c i t) -> p c t i", i=4, t=4),
-            wo_raw[:].rearrange("p t (c i) -> p c t i", i=4),
-        )
 
         right0 = placed([P, S], U32, "right0", 12352)
         left0 = [held([P, HALF], U32, "left0_0"), placed([P, HALF], U32, "left0_1", 16448)]
         right1 = placed([P, S], U32, "right1", 4096)
         left1 = [placed([P, HALF], U32, "left1_%d" % half, 2048 * half) for half in range(2)]
-        key_words = placed([P, PASSES * S], U32, "key_words", 46080)
+        key_words = placed([P, PASSES * S], U32, "key_words", 32768)
         key = [key_words[:, a * S : (a + 1) * S] for a in range(PASSES)]
         gather_words(left0[0][:], list_l, 0, 0, HALF)
         quantize_wl(0)
-        for q in range(4):
-            nc.sync.dma_start(wk_sc_raw[32 * q : 32 * q + 8, 0, :], wk_scales[:, 4 * q : 4 * q + 4, :].bitcast(I32))
-        with nc.allow_non_contiguous_dma(reason="one gain to a partition"):
-            for t in range(4):
-                nc.sync.dma_start(gain[t][:, 0:1], g.rearrange("(b t e) -> t b e", t=4, e=8)[t])
+        for t in range(4):
+            nc.sync.dma_start(wo_raw[:, t, :], wo.rearrange("(b t e) n -> t b e n", t=4, e=8)[t])
         gather_words(right0[:], list_r, 0, 0, S)
         gather_words(left0[1][:], list_l, 0, HALF, S)
         quantize_wl(1)
@@ -196,19 +191,16 @@ def tile_list_record_match_scores_kernel(
                 left_sc[4 * a : P, j0 : j0 + width],
             )
 
-        tanh_b_first = placed([P, 4, HALF], F32, "tanh_b_first", 26688)
-        tanh_a_three = placed([P, 3, HALF], F32, "tanh_a_three", 18496)
-        tanh_a_fourth = placed([P, HALF], F32, "tanh_a_fourth", 24640)
-        tanh_a_first = [tanh_a_three[:, t, :] for t in range(3)] + [tanh_a_fourth[:]]
+        tanh_b_first = held([P, 4, HALF], F32, "tanh_b_first")
+        tanh_a_first = placed([P, 4, HALF], F32, "tanh_a_first", 79872)
         a_first = [bank([P, HALF], t) for t in range(4)]
         b_first = [bank([P, HALF], 4 + t) for t in range(4)]
         for a in range(PASSES):
-            for t in range(4):
-                left_pass(a_first[t][:], a, t, 0, HALF)
-            for t in range(4):
-                right_pass(b_first[t][:], a, t, 0, HALF)
+            for side_pass, sums in ((left_pass, a_first), (right_pass, b_first)):
+                for t in range(4):
+                    side_pass(sums[t][:], a, t, 0, HALF)
         for t in range(4):
-            nc.scalar.activation(tanh_a_first[t], a_first[t][:], ACT.Tanh)
+            nc.scalar.activation(tanh_a_first[:, t, :], a_first[t][:], ACT.Tanh)
         for t in range(4):
             nc.scalar.activation(tanh_b_first[:, t, :], b_first[t][:], ACT.Tanh)
         for q in range(4):
@@ -232,17 +224,22 @@ def tile_list_record_match_scores_kernel(
             return gained
 
         b_third = tanh_of(right_pass, "tanh_b_third", 512, QUARTER, 0)
-        a_third = tanh_of(left_pass, "tanh_a_third", 512, QUARTER, 2)
+        a_third = tanh_of(left_pass, "tanh_a_third", 512, QUARTER, 4)
         gained_third = with_gain(b_third, "gained_third", QUARTER)
-        b_last = tanh_of(right_pass, "tanh_b_last", 896, P, 4)
+        wo_bf = held([P, 4 * N], BF16, "wo_bf")
+        nc.scalar.copy(
+            wo_bf[:].rearrange("p (c i t) -> p c t i", i=4, t=4),
+            wo_raw[:].rearrange("p t (c i) -> p c t i", i=4),
+        )
+        b_last = tanh_of(right_pass, "tanh_b_last", 896, P, 2)
         a_last = [placed([P, 2, P], F32, "tanh_a_last0", 65536), held([P, 2, P], F32, "tanh_a_last1")]
-        acc = bank([P, 4, P], 5)
+        acc = bank([P, 4, P], 6)
         for t in range(4):
             for a in range(PASSES):
                 left_pass(acc[:, t, :], a, t, 896, P)
         for pair in range(2):
             nc.scalar.activation(a_last[pair][:], acc[:, 2 * pair : 2 * pair + 2, :], ACT.Tanh)
-        b_sixth = tanh_of(right_pass, "tanh_b_sixth", 768, P, 6)
+        b_sixth = tanh_of(right_pass, "tanh_b_sixth", 768, P, 3)
         a_sixth = tanh_of(left_pass, "tanh_a_sixth", 768, P, 7)
         gained_sixth = with_gain(b_sixth, "gained_sixth", P)
 
@@ -252,13 +249,10 @@ def tile_list_record_match_scores_kernel(
         def flat(tile):
             return tile[:].rearrange("p t c -> p (t c)")
 
-        agree_first = held([P, 4, HALF], F32, "agree_first")
-        for t in range(4):
-            product(agree_first[:, t, :], tanh_a_first[t], tanh_b_first[:, t, :], t)
-        wo_w = placed([P, N], U32, "wo_w", 18496)
-        wo_sc = held([P, N], U8, "wo_sc")
-        nc.vector.quantize_mx(out=wo_w[:].bitcast(FP8X4), scales=wo_sc[:], in_=wo_bf[:])
-        agree_third = placed([P, 4, QUARTER], F32, "agree_third", 24640)
+        agree_first = placed([P, 4, HALF], F32, "agree_first", 49152)
+        for t, c0, c1 in ((0, 0, HALF), (1, 0, HALF), (2, 0, HALF), (3, 0, QUARTER), (3, QUARTER, HALF)):
+            product(agree_first[:, t, c0:c1], tanh_a_first[:, t, c0:c1], tanh_b_first[:, t, c0:c1], t)
+        agree_third = held([P, 4, QUARTER], F32, "agree_third", "tanh_b_first")
         nc.gpsimd.tensor_tensor(flat(agree_third), flat(a_third), flat(gained_third), ALU.mult)
 
         h_bf = {0: held([P, 4 * HALF], BF16, "h_bf0"), 768: held([P, 4 * QUARTER], BF16, "h_bf768")}
@@ -278,7 +272,7 @@ def tile_list_record_match_scores_kernel(
 
         def score(j0, j1, number, copy=nc.scalar.copy):
             width = j1 - j0
-            acc = bank([P, 2, width], 4 + number)
+            acc = bank([P, 2, width], (2, 6, 3, 7)[number])
             for m in range(2):
                 nc.tensor.matmul_mx(
                     out=acc[:, m, :],
@@ -297,7 +291,7 @@ def tile_list_record_match_scores_kernel(
             queue.dma_start(out_v[:, :, j0:j1], res[:])
 
         def key_product(j0, number):
-            acc = bank([P, 4, P], number)
+            acc = bank([P, 4, P], (0, 1, 4, 5)[number])
             for t in range(4):
                 for a in range(PASSES):
                     mx(
@@ -325,7 +319,10 @@ def tile_list_record_match_scores_kernel(
 
         for block in range(4):
             subtract(block * P, agree_first[:, :, block * P : (block + 1) * P], key_product(block * P, block)[:])
-        agree_last = held([P, 4, P], F32, "agree_last", "agree_first")
+        wo_w = placed([P, N], U32, "wo_w", 49152)
+        wo_sc = held([P, N], U8, "wo_sc")
+        nc.vector.quantize_mx(out=wo_w[:].bitcast(FP8X4), scales=wo_sc[:], in_=wo_bf[:])
+        agree_last = placed([P, 4, P], F32, "agree_last", 51200)
         for t in range(4):
             product(agree_last[:, t, :], a_last[t // 2][:, t % 2, :], b_last[:, t, :], t)
         quantize_h(0, 512)
@@ -333,7 +330,7 @@ def tile_list_record_match_scores_kernel(
         store(256, 512, score(256, 512, 1), nc.sync)
         agree_sixth = held([P, 4, P], F32, "agree_sixth", "h_bf0")
         nc.gpsimd.tensor_tensor(flat(agree_sixth), flat(a_sixth), flat(gained_sixth), ALU.mult)
-        h_bf[512] = placed([P, 4 * QUARTER], BF16, "h_bf512", 59456)
+        h_bf[512] = placed([P, 4 * QUARTER], BF16, "h_bf512", 20544)
         for block in range(2):
             subtract(512 + block * P, agree_third[:, :, block * P : (block + 1) * P], key_product(512 + block * P, block)[:])
         subtract(896, agree_last[:], key_product(896, 2)[:])

@@ -49,8 +49,7 @@ def tile_list_record_match_scores_kernel(
         tab_w = [held([P, T], I32, "tab_w0"), placed([P, T], I32, "tab_w1", 70656)]
         wo_raw = placed([P, 4, N], F32, "wo_raw", 61440)
         wr_raw = held([P, PASSES, H // 2], I32, "wr_raw")
-        wr_sc_raw = held([P, PASSES, H // 4], I32, "wr_sc_raw")
-        wk_sc_raw = placed([P, 1, H // 4], I32, "wk_sc_raw", 23040)
+        w_sc_raw = held([P, 3, H // 4], I32, "w_sc_raw")
         wl_raw = [placed([P, 4, H], F32, "wl_raw0", 16384), placed([P, 4, H], F32, "wl_raw1", 0)]
         right_sc = [placed([P, S // 4], I32, "right_sc0", 78848), placed([P, S // 4], I32, "right_sc1", 57344)]
         wk_raw = placed([P, PASSES, H], I32, "wk_raw", 79872)
@@ -58,7 +57,7 @@ def tile_list_record_match_scores_kernel(
 
 
         nc.gpsimd.memset(tab_sc[:], 0)
-        nc.vector.memset(wr_sc_raw[:], 0)
+        nc.vector.memset(w_sc_raw[:], 0)
         nc.vector.memset(tab_sc_flat[32:64, :], 0)
         nc.vector.memset(tab_sc_flat[64:128, :], 0)
 
@@ -81,11 +80,13 @@ def tile_list_record_match_scores_kernel(
             nc.sync.dma_start(tab_sc[32 * q : 32 * q + 8, :], tab_scales[:, 4 * q : 4 * q + 4, :].bitcast(I32))
         load_wl(0)
         nc.sync.dma_start(list_k[:], offs3)
+        for q in range(4):
+            nc.sync.dma_start(w_sc_raw[32 * q : 32 * q + 8, 2, :], wk_scales[:, 4 * q : 4 * q + 4, :].bitcast(I32))
         load_table(0)
         nc.sync.dma_start(wr_raw[:], wr_words.bitcast(I32).rearrange("a p w -> p a w"))
         for q in range(4):
             nc.sync.dma_start(
-                wr_sc_raw[32 * q : 32 * q + 4, :, :],
+                w_sc_raw[32 * q : 32 * q + 4, 0:2, :],
                 wr_scales[:, 4 * q : 4 * q + 4, :].bitcast(I32).rearrange("a r w -> r a w"),
             )
         load_wl(1)
@@ -106,8 +107,6 @@ def tile_list_record_match_scores_kernel(
         load_table(1)
         nc.sync.dma_start(wk_raw[:], wk_words.rearrange("a p r i -> p a (r i)").bitcast(I32))
         place_right_rows(1)
-        for q in range(4):
-            nc.sync.dma_start(wk_sc_raw[32 * q : 32 * q + 8, 0, :], wk_scales[:, 4 * q : 4 * q + 4, :].bitcast(I32))
         with nc.allow_non_contiguous_dma(reason="one gain to a partition"):
             for t in range(4):
                 nc.sync.dma_start(gain[t][:, 0:1], g.rearrange("(b t e) -> t b e", t=4, e=8)[t])
@@ -135,17 +134,16 @@ def tile_list_record_match_scores_kernel(
 
         wr_w = held([P, PASSES, H // 2], U32, "wr_w")
         wk_w = held([P, PASSES, H], U32, "wk_w")
-        wr_sc = held([P, PASSES, H // 4], U32, "wr_sc")
-        wk_sc = held([P, 1, H // 4], U32, "wk_sc")
+        w_sc = held([P, 3, H // 4], U32, "w_sc")
         round_wl(0)
         deal(wr_w[:], wr_raw[:], 4)
-        deal(wr_sc[:], wr_sc_raw[:], 2)
+        deal(w_sc[:], w_sc_raw[:], 2)
         round_wl(1)
         deal(wk_w[:], wk_raw[:], 8)
 
         right0 = placed([P, S], U32, "right0", 12352)
         left0 = [held([P, HALF], U32, "left0_0"), placed([P, HALF], U32, "left0_1", 16448)]
-        right1 = placed([P, S], U32, "right1", 4096)
+        right1 = [placed([P, HALF], U32, "right1_%d" % half, 4096 + 2048 * half) for half in range(2)]
         left1 = [placed([P, HALF], U32, "left1_%d" % half, 2048 * half) for half in range(2)]
         key_words = placed([P, PASSES * S], U32, "key_words", 32768)
         key = [key_words[:, a * S : (a + 1) * S] for a in range(PASSES)]
@@ -157,7 +155,8 @@ def tile_list_record_match_scores_kernel(
         gather_words(left0[1][:], list_l, 0, HALF, S)
         quantize_wl(1)
         gather_words(left1[0][:], list_l, 1, 0, HALF)
-        gather_words(right1[:], list_r, 1, 0, S)
+        gather_words(right1[0][:], list_r, 1, 0, HALF)
+        gather_words(right1[1][:], list_r, 1, HALF, S)
         gather_words(left1[1][:], list_l, 1, HALF, S)
         gather_words(key[0], list_k, 0, 0, S)
         gather_words(key[1], list_k, 1, 0, S)
@@ -169,12 +168,12 @@ def tile_list_record_match_scores_kernel(
 
         def right_pass(acc, a, t, j0, width):
             cols = slice(j0, j0 + width)
-            words = [right0[:, cols], right1[:, cols]]
+            words = [right0[:, cols], right1[j0 // HALF][:, j0 % HALF : j0 % HALF + width]]
             mx(
                 acc,
                 a,
                 wr_w[:, a, t * 64 : (t + 1) * 64].bitcast(U8).bitcast(FP4X4),
-                wr_sc[:, a, t * 32 : (t + 1) * 32].bitcast(U8),
+                w_sc[:, a, t * 32 : (t + 1) * 32].bitcast(U8),
                 words[a].bitcast(FP8X4),
                 right_sc[a][:].bitcast(U8)[:, cols],
             )
@@ -203,8 +202,6 @@ def tile_list_record_match_scores_kernel(
             nc.scalar.activation(tanh_a_first[:, t, :], a_first[t][:], ACT.Tanh)
         for t in range(4):
             nc.scalar.activation(tanh_b_first[:, t, :], b_first[t][:], ACT.Tanh)
-        for q in range(4):
-            deal(wk_sc[32 * q : 32 * q + 8], wk_sc_raw[32 * q : 32 * q + 8], 2)
 
         def tanh_of(side_pass, name, j0, width, first_bank):
             result = held([P, 4, width], F32, name)
@@ -298,7 +295,7 @@ def tile_list_record_match_scores_kernel(
                         acc[:, t, :],
                         a,
                         wk_w[:, a, t * P : (t + 1) * P].bitcast(FP8X4),
-                        wk_sc[4 * a : P, 0, t * 32 : (t + 1) * 32].bitcast(U8),
+                        w_sc[4 * a : P, 2, t * 32 : (t + 1) * 32].bitcast(U8),
                         key[a][:, j0 : j0 + P].bitcast(FP8X4),
                         key_sc[4 * a : P, j0 : j0 + P],
                     )

@@ -50,7 +50,7 @@ def tile_list_record_match_scores_kernel(
         wo_raw = placed([P, 4, N], F32, "wo_raw", 61440)
         wr_raw = held([P, PASSES, H // 2], I32, "wr_raw")
         w_sc_raw = held([P, 3, H // 4], I32, "w_sc_raw")
-        wl_raw = [placed([P, 4, H], F32, "wl_raw0", 16384), placed([P, 4, H], F32, "wl_raw1", 0)]
+        wl_raw = [placed([P, 4, H], F32, "wl_raw0", 16384), placed([P, 4, H], F32, "wl_raw1", 1984)]
         right_sc = [placed([P, S // 4], I32, "right_sc0", 78848), placed([P, S // 4], I32, "right_sc1", 57344)]
         wk_raw = placed([P, PASSES, H], I32, "wk_raw", 79872)
         gain = [placed([P, 8], F32, "gain%d" % t, (22656, 22720, 22528, 22784)[t]) for t in range(4)]
@@ -78,11 +78,11 @@ def tile_list_record_match_scores_kernel(
         nc.sync.dma_start(list_l[:], offs)
         for q in range(4):
             nc.sync.dma_start(tab_sc[32 * q : 32 * q + 8, :], tab_scales[:, 4 * q : 4 * q + 4, :].bitcast(I32))
-        load_wl(0)
+        load_table(0)
         nc.sync.dma_start(list_k[:], offs3)
         for q in range(4):
             nc.sync.dma_start(w_sc_raw[32 * q : 32 * q + 8, 2, :], wk_scales[:, 4 * q : 4 * q + 4, :].bitcast(I32))
-        load_table(0)
+        load_wl(0)
         nc.sync.dma_start(wr_raw[:], wr_words.bitcast(I32).rearrange("a p w -> p a w"))
         for q in range(4):
             nc.sync.dma_start(
@@ -132,26 +132,26 @@ def tile_list_record_match_scores_kernel(
                 src.bitcast(U32).rearrange("p a (b t w) -> p a t b w", t=4, w=run),
             )
 
-        wr_w = held([P, PASSES, H // 2], U32, "wr_w")
+        wr_w = placed([P, PASSES, H // 2], U32, "wr_w", 6144)
         wk_w = held([P, PASSES, H], U32, "wk_w")
-        w_sc = held([P, 3, H // 4], U32, "w_sc")
+        w_sc = placed([P, 3, H // 4], U32, "w_sc", 8192)
         round_wl(0)
+        round_wl(1)
         deal(wr_w[:], wr_raw[:], 4)
         deal(w_sc[:], w_sc_raw[:], 2)
-        round_wl(1)
         deal(wk_w[:], wk_raw[:], 8)
 
-        right0 = placed([P, S], U32, "right0", 12352)
+        right0 = held([P, S], U32, "right0")
         left0 = [held([P, HALF], U32, "left0_0"), placed([P, HALF], U32, "left0_1", 16448)]
-        right1 = [placed([P, HALF], U32, "right1_%d" % half, 4096 + 2048 * half) for half in range(2)]
+        right1 = [placed([P, HALF], U32, "right1_%d" % half, (4096, 9728)[half]) for half in range(2)]
         left1 = [placed([P, HALF], U32, "left1_%d" % half, 2048 * half) for half in range(2)]
         key_words = placed([P, PASSES * S], U32, "key_words", 32768)
         key = [key_words[:, a * S : (a + 1) * S] for a in range(PASSES)]
         gather_words(left0[0][:], list_l, 0, 0, HALF)
+        gather_words(right0[:], list_r, 0, 0, S)
         quantize_wl(0)
         for t in range(4):
             nc.sync.dma_start(wo_raw[:, t, :], wo.rearrange("(b t e) n -> t b e n", t=4, e=8)[t])
-        gather_words(right0[:], list_r, 0, 0, S)
         gather_words(left0[1][:], list_l, 0, HALF, S)
         quantize_wl(1)
         gather_words(left1[0][:], list_l, 1, 0, HALF)

@@ -1,6 +1,7 @@
 from contextlib import ExitStack
 
 import concourse.mybir as mybir
+from concourse.masks import make_identity
 
 K, H, N, T, S = 1024, 512, 256, 2048, 1024
 FLOPS = 2 * S * H * (3 * K + N)
@@ -57,6 +58,8 @@ def tile_list_record_match_scores_kernel(
 
 
         nc.gpsimd.memset(tab_sc[:], 0)
+        ident = held([P, P], F32, "ident")
+        make_identity(nc, ident[:])
         nc.vector.memset(w_sc_raw[:], 0)
         nc.vector.memset(tab_sc_flat[32:64, :], 0)
         nc.vector.memset(tab_sc_flat[64:128, :], 0)
@@ -113,7 +116,7 @@ def tile_list_record_match_scores_kernel(
 
         wl_w = held([P, PASSES, H], U32, "wl_w")
         wl_sc = held([P, PASSES, H], U8, "wl_sc")
-        wl_bf = [placed([P, 4, 4 * P], BF16, "wl_bf0", 61440), held([P, 4, 4 * P], BF16, "wl_bf1")]
+        wl_bf = [placed([P, 4, 4 * P], BF16, "wl_bf0", 61440), placed([P, 4, 4 * P], BF16, "wl_bf1", 24576)]
 
         def round_wl(a):
             dst = wl_bf[a][:].rearrange("p t (b y e j) -> p y t b j e", y=2, e=4, j=4)
@@ -141,14 +144,14 @@ def tile_list_record_match_scores_kernel(
         deal(w_sc[:], w_sc_raw[:], 2)
         deal(wk_w[:], wk_raw[:], 8)
 
-        right0 = held([P, S], U32, "right0")
+        right0 = [held([P, HALF], U32, "right0_0"), placed([P, HALF], U32, "right0_1", 25600)]
         left0 = [held([P, HALF], U32, "left0_0"), placed([P, HALF], U32, "left0_1", 16448)]
         right1 = [placed([P, HALF], U32, "right1_%d" % half, (4096, 9728)[half]) for half in range(2)]
         left1 = [placed([P, HALF], U32, "left1_%d" % half, 2048 * half) for half in range(2)]
         key_words = placed([P, PASSES * S], U32, "key_words", 32768)
         key = [key_words[:, a * S : (a + 1) * S] for a in range(PASSES)]
         gather_words(left0[0][:], list_l, 0, 0, HALF)
-        gather_words(right0[:], list_r, 0, 0, S)
+        gather_words(right0[0][:], list_r, 0, 0, HALF)
         quantize_wl(0)
         for t in range(4):
             nc.sync.dma_start(wo_raw[:, t, :], wo.rearrange("(b t e) n -> t b e n", t=4, e=8)[t])
@@ -156,6 +159,7 @@ def tile_list_record_match_scores_kernel(
         quantize_wl(1)
         gather_words(left1[0][:], list_l, 1, 0, HALF)
         gather_words(right1[0][:], list_r, 1, 0, HALF)
+        gather_words(right0[1][:], list_r, 0, HALF, S)
         gather_words(right1[1][:], list_r, 1, HALF, S)
         gather_words(left1[1][:], list_l, 1, HALF, S)
         gather_words(key[0], list_k, 0, 0, S)
@@ -168,7 +172,7 @@ def tile_list_record_match_scores_kernel(
 
         def right_pass(acc, a, t, j0, width):
             cols = slice(j0, j0 + width)
-            words = [right0[:, cols], right1[j0 // HALF][:, j0 % HALF : j0 % HALF + width]]
+            words = [tiles[j0 // HALF][:, j0 % HALF : j0 % HALF + width] for tiles in (right0, right1)]
             mx(
                 acc,
                 a,
@@ -190,16 +194,27 @@ def tile_list_record_match_scores_kernel(
                 left_sc[4 * a : P, j0 : j0 + width],
             )
 
+        def left_pass_turned(acc, a, j0):
+            mx(
+                acc,
+                a,
+                (left0, left1)[a][0][:, j0 : j0 + P].bitcast(FP8X4),
+                left_sc[4 * a : P, j0 : j0 + P],
+                wl_w[:, a, :].bitcast(FP8X4),
+                wl_sc[:, a, :],
+            )
+
         tanh_b_first = held([P, 4, HALF], F32, "tanh_b_first")
-        tanh_a_first = placed([P, 4, HALF], F32, "tanh_a_first", 79872)
-        a_first = [bank([P, HALF], t) for t in range(4)]
+        tanh_a_first = placed([P, 4, H], F32, "tanh_a_first", 79872)
+        a_first = [bank([P, H], block) for block in range(4)]
         b_first = [bank([P, HALF], 4 + t) for t in range(4)]
         for a in range(PASSES):
-            for side_pass, sums in ((left_pass, a_first), (right_pass, b_first)):
-                for t in range(4):
-                    side_pass(sums[t][:], a, t, 0, HALF)
-        for t in range(4):
-            nc.scalar.activation(tanh_a_first[:, t, :], a_first[t][:], ACT.Tanh)
+            for block in range(4):
+                left_pass_turned(a_first[block][:], a, block * P)
+            for t in range(4):
+                right_pass(b_first[t][:], a, t, 0, HALF)
+        for block in range(4):
+            nc.scalar.activation(tanh_a_first[:, block, :], a_first[block][:], ACT.Tanh)
         for t in range(4):
             nc.scalar.activation(tanh_b_first[:, t, :], b_first[t][:], ACT.Tanh)
 
@@ -220,40 +235,45 @@ def tile_list_record_match_scores_kernel(
                 nc.scalar.activation(gained[:, t, :], tanh_b[:, t, :], ACT.Copy, scale=gain[t][:, 0:1])
             return gained
 
-        b_third = tanh_of(right_pass, "tanh_b_third", 512, QUARTER, 0)
-        a_third = tanh_of(left_pass, "tanh_a_third", 512, QUARTER, 4)
+        b_third = tanh_of(right_pass, "tanh_b_third", 512, QUARTER, 4)
+        a_third = tanh_of(left_pass, "tanh_a_third", 512, QUARTER, 6)
+        a_turned = [bank([P, HALF], t) for t in range(4)]
+        for t in range(4):
+            for block in range(4):
+                nc.tensor.transpose(
+                    a_turned[t][:, block * P : (block + 1) * P], tanh_a_first[:, block, t * P : (t + 1) * P], ident[:]
+                )
         gained_third = with_gain(b_third, "gained_third", QUARTER)
-        wo_bf = held([P, 4 * N], BF16, "wo_bf")
+        b_sixth = tanh_of(right_pass, "tanh_b_sixth", 768, P, 4)
+        a_sixth = tanh_of(left_pass, "tanh_a_sixth", 768, P, 5)
+        gained_sixth = with_gain(b_sixth, "gained_sixth", P)
+        wo_bf = held([P, 4 * N], BF16, "wo_bf", "tanh_b_third")
         nc.scalar.copy(
             wo_bf[:].rearrange("p (c i t) -> p c t i", i=4, t=4),
             wo_raw[:].rearrange("p t (c i) -> p c t i", i=4),
         )
-        b_last = tanh_of(right_pass, "tanh_b_last", 896, P, 2)
-        a_last = [placed([P, 2, P], F32, "tanh_a_last0", 65536), held([P, 2, P], F32, "tanh_a_last1")]
-        acc = bank([P, 4, P], 6)
-        for t in range(4):
-            for a in range(PASSES):
-                left_pass(acc[:, t, :], a, t, 896, P)
-        for pair in range(2):
-            nc.scalar.activation(a_last[pair][:], acc[:, 2 * pair : 2 * pair + 2, :], ACT.Tanh)
-        b_sixth = tanh_of(right_pass, "tanh_b_sixth", 768, P, 3)
-        a_sixth = tanh_of(left_pass, "tanh_a_sixth", 768, P, 7)
-        gained_sixth = with_gain(b_sixth, "gained_sixth", P)
-
-        def product(dst, tanh_a, tanh_b, t):
-            nc.vector.scalar_tensor_tensor(dst, tanh_a, gain[t][:, 0:1], tanh_b, ALU.mult, ALU.mult)
+        b_last = tanh_of(right_pass, "tanh_b_last", 896, P, 6)
+        a_last = tanh_of(left_pass, "tanh_a_last", 896, P, 7)
+        gained_last = with_gain(b_last, "gained_last", P)
 
         def flat(tile):
             return tile[:].rearrange("p t c -> p (t c)")
 
-        agree_first = placed([P, 4, HALF], F32, "agree_first", 49152)
-        for t, c0, c1 in ((0, 0, HALF), (1, 0, HALF), (2, 0, HALF), (3, 0, QUARTER), (3, QUARTER, HALF)):
-            product(agree_first[:, t, c0:c1], tanh_a_first[:, t, c0:c1], tanh_b_first[:, t, c0:c1], t)
-        agree_third = held([P, 4, QUARTER], F32, "agree_third", "tanh_b_first")
+        agree_third = placed([P, 4, QUARTER], F32, "agree_third", 70656)
+        agree_sixth = placed([P, 4, P], F32, "agree_sixth", 74752)
         nc.gpsimd.tensor_tensor(flat(agree_third), flat(a_third), flat(gained_third), ALU.mult)
+        nc.gpsimd.tensor_tensor(flat(agree_sixth), flat(a_sixth), flat(gained_sixth), ALU.mult)
+
+        agree_head = placed([P, 4, 3 * P], F32, "agree_head", 79872)
+        agree_fourth = placed([P, 4, P], F32, "agree_fourth", 86016)
+        for t in range(4):
+            for dst, c0, c1 in ((agree_head, 0, 3 * P), (agree_fourth, 3 * P, HALF)):
+                nc.vector.scalar_tensor_tensor(
+                    dst[:, t, :], tanh_b_first[:, t, c0:c1], gain[t][:, 0:1], a_turned[t][:, c0:c1], ALU.mult, ALU.mult
+                )
 
         h_bf = {0: held([P, 4 * HALF], BF16, "h_bf0"), 768: held([P, 4 * QUARTER], BF16, "h_bf768")}
-        h_w = placed([P, S], U32, "h_w", 65536)
+        h_w = placed([P, S], U32, "h_w", 61440)
         h_sc = held([P, S], U8, "h_sc")
         out_v = out.rearrange("(m p) j -> p m j", p=P)
 
@@ -269,7 +289,7 @@ def tile_list_record_match_scores_kernel(
 
         def score(j0, j1, number, copy=nc.scalar.copy):
             width = j1 - j0
-            acc = bank([P, 2, width], (2, 6, 3, 7)[number])
+            acc = bank([P, 2, width], number)
             for m in range(2):
                 nc.tensor.matmul_mx(
                     out=acc[:, m, :],
@@ -288,16 +308,17 @@ def tile_list_record_match_scores_kernel(
             queue.dma_start(out_v[:, :, j0:j1], res[:])
 
         def key_product(j0, number):
-            acc = bank([P, 4, P], (0, 1, 4, 5)[number])
-            for t in range(4):
-                for a in range(PASSES):
-                    mx(
-                        acc[:, t, :],
-                        a,
-                        wk_w[:, a, t * P : (t + 1) * P].bitcast(FP8X4),
-                        w_sc[4 * a : P, 2, t * 32 : (t + 1) * 32].bitcast(U8),
-                        key[a][:, j0 : j0 + P].bitcast(FP8X4),
-                        key_sc[4 * a : P, j0 : j0 + P],
+            acc = bank([P, 4, P], number)
+            for a in range(PASSES):
+                for t in range(4):
+                    nc.tensor.matmul_mx(
+                        out=acc[:, t, :],
+                        lhsT=wk_w[:, a, t * P : (t + 1) * P].bitcast(FP8X4),
+                        lhsT_scale=w_sc[4 * a : P, 2, t * 32 : (t + 1) * 32].bitcast(U8),
+                        rhs=key[a][:, j0 : j0 + P].bitcast(FP8X4),
+                        rhs_scale=key_sc[4 * a : P, j0 : j0 + P],
+                        start=(a == 0 and t == 0),
+                        stop=(a == PASSES - 1 and t == 3),
                     )
             return acc
 
@@ -314,30 +335,28 @@ def tile_list_record_match_scores_kernel(
             quantize_h(j0, j1)
             store(j0, j1, score(j0, j1, number), queue)
 
-        for block in range(4):
-            subtract(block * P, agree_first[:, :, block * P : (block + 1) * P], key_product(block * P, block)[:])
-        wo_w = placed([P, N], U32, "wo_w", 49152)
+        for block in range(3):
+            subtract(block * P, agree_head[:, :, block * P : (block + 1) * P], key_product(block * P, block)[:])
+        subtract(3 * P, agree_fourth[:], key_product(3 * P, 3)[:])
+        wo_w = placed([P, N], U32, "wo_w", 79872)
         wo_sc = held([P, N], U8, "wo_sc")
         nc.vector.quantize_mx(out=wo_w[:].bitcast(FP8X4), scales=wo_sc[:], in_=wo_bf[:])
-        agree_last = placed([P, 4, P], F32, "agree_last", 51200)
-        for t in range(4):
-            product(agree_last[:, t, :], a_last[t // 2][:, t % 2, :], b_last[:, t, :], t)
         quantize_h(0, 512)
-        store(0, 256, score(0, 256, 0), nc.sync)
-        store(256, 512, score(256, 512, 1), nc.sync)
-        agree_sixth = held([P, 4, P], F32, "agree_sixth", "h_bf0")
-        nc.gpsimd.tensor_tensor(flat(agree_sixth), flat(a_sixth), flat(gained_sixth), ALU.mult)
-        h_bf[512] = placed([P, 4 * QUARTER], BF16, "h_bf512", 20544)
+        store(0, 256, score(0, 256, 2), nc.sync)
+        store(256, 512, score(256, 512, 3), nc.sync)
+        agree_last = held([P, 4, P], F32, "agree_last", "h_bf0")
+        nc.gpsimd.tensor_tensor(flat(agree_last), flat(a_last), flat(gained_last), ALU.mult)
+        h_bf[512] = held([P, 4 * QUARTER], BF16, "h_bf512", "tanh_b_third")
         for block in range(2):
-            subtract(512 + block * P, agree_third[:, :, block * P : (block + 1) * P], key_product(512 + block * P, block)[:])
-        subtract(896, agree_last[:], key_product(896, 2)[:])
+            subtract(512 + block * P, agree_third[:, :, block * P : (block + 1) * P], key_product(512 + block * P, 4 + block)[:])
+        subtract(768, agree_sixth[:], key_product(768, 0)[:])
         quantize_h(512, 768)
-        store(512, 640, score(512, 640, 2), nc.sync)
-        store(640, 768, score(640, 768, 3), nc.sync)
-        key_sum = key_product(768, 3)
-        subtract(768, agree_sixth[:, :, 0:64], key_sum[:, :, 0:64])
-        finish(896, 1024, 0, nc.sync)
-        subtract(832, agree_sixth[:, :, 64:128], key_sum[:, :, 64:128])
-        finish(768, 832, 1, nc.scalar)
-        quantize_h(832, 896)
-        store(832, 896, score(832, 896, 2, nc.vector.tensor_copy), nc.sync)
+        store(512, 640, score(512, 640, 6), nc.sync)
+        store(640, 768, score(640, 768, 7), nc.sync)
+        key_sum = key_product(896, 1)
+        subtract(896, agree_last[:, :, 0:64], key_sum[:, :, 0:64])
+        finish(768, 896, 4, nc.sync)
+        subtract(960, agree_last[:, :, 64:128], key_sum[:, :, 64:128])
+        finish(896, 960, 5, nc.scalar)
+        quantize_h(960, 1024)
+        store(960, 1024, score(960, 1024, 0, nc.vector.tensor_copy), nc.sync)

@@ -36,8 +36,8 @@ def tile_list_record_match_scores_kernel(
         def held(shape, dtype, name, slot=None):
             return keep.tile(shape, dtype, name=name, tag=slot or name, align_bytes=64)
 
-        def placed(shape, dtype, name, offset):
-            return laid.tile(shape, dtype, name=name, tag=name, align_bytes=64, offset=offset)
+        def placed(shape, dtype, name, offset, align=64):
+            return laid.tile(shape, dtype, name=name, tag=name, align_bytes=align, offset=offset)
 
         def bank(shape, number):
             return acc_pool.tile(shape, F32, name="acc", tag="bank%d" % number)
@@ -45,24 +45,17 @@ def tile_list_record_match_scores_kernel(
         list_l = keep.tile([P, S // 16], U16, name="list_l")
         list_r = keep.tile([P, S // 16], U16, name="list_r")
         list_k = keep.tile([P, S // 16], U16, name="list_k")
-        tab_sc = placed([P, T // 4], I32, "tab_sc", 57344)
-        tab_sc_flat = placed([P, T // 4], I32, "tab_sc_flat", 78336)
-        tab_w = [held([P, T], I32, "tab_w0"), placed([P, T], I32, "tab_w1", 70656)]
-        wo_raw = placed([P, 4, N], F32, "wo_raw", 61440)
-        wr_raw = held([P, PASSES, H // 2], I32, "wr_raw")
-        w_sc_raw = held([P, 3, H // 4], I32, "w_sc_raw")
-        wl_raw = [placed([P, 4, H], F32, "wl_raw0", 16384), placed([P, 4, H], F32, "wl_raw1", 1984)]
-        right_sc = [placed([P, S // 4], I32, "right_sc0", 78848), placed([P, S // 4], I32, "right_sc1", 57344)]
-        wk_raw = placed([P, PASSES, H], I32, "wk_raw", 79872)
-        gain = [placed([P, 8], F32, "gain%d" % t, (22656, 22720, 22528, 22784)[t]) for t in range(4)]
+        wl_raw = [placed([P, 4, H], F32, "wl_raw%d" % a, 8192 * a, 256) for a in range(PASSES)]
+        tab_w = [placed([P, T], I32, "tab_w%d" % a, 16384 + 8192 * a, 256) for a in range(PASSES)]
+        tab_sc = placed([P, T // 4], I32, "tab_sc", 32768, 256)
+        wr_raw = placed([P, PASSES, H // 2], I32, "wr_raw", 69632, 256)
+        w_sc_raw = held([P, PASSES, H // 4], I32, "w_sc_raw")
 
-
-        nc.gpsimd.memset(tab_sc[:], 0)
+        nc.vector.memset(w_sc_raw[:], 0)
+        nc.vector.memset(tab_sc[32:64, :], 0)
+        nc.vector.memset(tab_sc[64:128, :], 0)
         ident = held([P, P], F32, "ident")
         make_identity(nc, ident[:])
-        nc.vector.memset(w_sc_raw[:], 0)
-        nc.vector.memset(tab_sc_flat[32:64, :], 0)
-        nc.vector.memset(tab_sc_flat[64:128, :], 0)
 
         def load_table(a):
             nc.sync.dma_start(tab_w[a][:], tab_words[a].rearrange("p t i -> p (t i)").bitcast(I32))
@@ -70,53 +63,47 @@ def tile_list_record_match_scores_kernel(
         def load_wl(a):
             nc.sync.dma_start(wl_raw[a][:], wl[512 * a : 512 * (a + 1), :].rearrange("(p j) r -> p j r", j=4))
 
-        def gather_scales(dst, window, lst):
-            nc.vector.tensor_copy(dst, window[:].bitcast(U8).indirect(lst[:]))
+        def gather_scales(name, lst):
+            rows = held([P, S], U8, name)
+            nc.vector.tensor_copy(rows[:], tab_sc[:].bitcast(U8).indirect(lst[:]))
+            return rows
 
         def gather_words(dst, lst, a, j0, j1):
             nc.vector.tensor_copy(dst, tab_w[a][:].bitcast(U32).indirect(lst[:, j0 // 16 : j1 // 16]))
 
-        nc.sync.dma_start(list_r[:], offs2)
-        nc.scalar.dma_start(tab_sc_flat[0:32, :], tab_scales.rearrange("a q t -> (a q) t").bitcast(I32))
         nc.sync.dma_start(list_l[:], offs)
-        for q in range(4):
-            nc.sync.dma_start(tab_sc[32 * q : 32 * q + 8, :], tab_scales[:, 4 * q : 4 * q + 4, :].bitcast(I32))
-        load_table(0)
+        nc.scalar.dma_start(tab_sc[0:32, :], tab_scales.rearrange("a q t -> (a q) t").bitcast(I32))
+        nc.sync.dma_start(list_r[:], offs2)
+        load_wl(0)
         nc.sync.dma_start(list_k[:], offs3)
         for q in range(4):
-            nc.sync.dma_start(w_sc_raw[32 * q : 32 * q + 8, 2, :], wk_scales[:, 4 * q : 4 * q + 4, :].bitcast(I32))
-        load_wl(0)
-        nc.sync.dma_start(wr_raw[:], wr_words.bitcast(I32).rearrange("a p w -> p a w"))
-        for q in range(4):
             nc.sync.dma_start(
-                w_sc_raw[32 * q : 32 * q + 4, 0:2, :],
+                w_sc_raw[32 * q : 32 * q + 4, :, :],
                 wr_scales[:, 4 * q : 4 * q + 4, :].bitcast(I32).rearrange("a r w -> r a w"),
             )
+        load_table(0)
         load_wl(1)
+        load_table(1)
+        nc.sync.dma_start(wr_raw[:], wr_words.bitcast(I32).rearrange("a p w -> p a w"))
 
-        right_flat = placed([P, S], U8, "right_flat", 32768)
-        left_sc = held([P, S], U8, "left_sc")
-        key_sc = held([P, S], U8, "key_sc")
-        gather_scales(right_flat[:], tab_sc_flat, list_r)
-        gather_scales(left_sc[:], tab_sc, list_l)
-        gather_scales(key_sc[:], tab_sc, list_k)
+        left_rows = gather_scales("left_rows", list_l)
+        right_rows = gather_scales("right_rows", list_r)
+        key_rows = gather_scales("key_rows", list_k)
 
-        def place_right_rows(a):
+        def place_rows(plane, first, rows, a):
             for q in range(4):
                 row = 16 * a + 4 * q
-                nc.sync.dma_start(right_sc[a][32 * q : 32 * q + 4, :], right_flat[row : row + 4, :].bitcast(I32))
+                nc.sync.dma_start(plane[32 * q + first : 32 * q + first + 4, :], rows[row : row + 4, :].bitcast(I32))
 
-        place_right_rows(0)
-        load_table(1)
-        nc.sync.dma_start(wk_raw[:], wk_words.rearrange("a p r i -> p a (r i)").bitcast(I32))
-        place_right_rows(1)
-        with nc.allow_non_contiguous_dma(reason="one gain to a partition"):
-            for t in range(4):
-                nc.sync.dma_start(gain[t][:, 0:1], g.rearrange("(b t e) -> t b e", t=4, e=8)[t])
+        left_sc = [held([P, S // 4], I32, "left_sc%d" % a) for a in range(PASSES)]
+        right_sc = [held([P, S // 4], I32, "right_sc%d" % a) for a in range(PASSES)]
+        for planes, rows in ((left_sc, left_rows), (right_sc, right_rows)):
+            for a in range(PASSES):
+                place_rows(planes[a], 0, rows, a)
 
         wl_w = held([P, PASSES, H], U32, "wl_w")
         wl_sc = held([P, PASSES, H], U8, "wl_sc")
-        wl_bf = [placed([P, 4, 4 * P], BF16, "wl_bf0", 61440), placed([P, 4, 4 * P], BF16, "wl_bf1", 24576)]
+        wl_bf = [placed([P, 4, 4 * P], BF16, "wl_bf0", 36864), placed([P, 4, 4 * P], BF16, "wl_bf1", 57344)]
 
         def round_wl(a):
             dst = wl_bf[a][:].rearrange("p t (b y e j) -> p y t b j e", y=2, e=4, j=4)
@@ -135,32 +122,43 @@ def tile_list_record_match_scores_kernel(
                 src.bitcast(U32).rearrange("p a (b t w) -> p a t b w", t=4, w=run),
             )
 
-        wr_w = placed([P, PASSES, H // 2], U32, "wr_w", 6144)
-        wk_w = held([P, PASSES, H], U32, "wk_w")
-        w_sc = placed([P, 3, H // 4], U32, "w_sc", 8192)
+        wr_w = held([P, PASSES, H // 2], U32, "wr_w")
+        wr_sc = held([P, PASSES, H // 4], U32, "wr_sc")
         round_wl(0)
+        deal(wr_sc[:], w_sc_raw[:], 2)
         round_wl(1)
         deal(wr_w[:], wr_raw[:], 4)
-        deal(w_sc[:], w_sc_raw[:], 2)
-        deal(wk_w[:], wk_raw[:], 8)
 
-        right0 = [held([P, HALF], U32, "right0_0"), placed([P, HALF], U32, "right0_1", 25600)]
-        left0 = [held([P, HALF], U32, "left0_0"), placed([P, HALF], U32, "left0_1", 16448)]
-        right1 = [placed([P, HALF], U32, "right1_%d" % half, (4096, 9728)[half]) for half in range(2)]
-        left1 = [placed([P, HALF], U32, "left1_%d" % half, 2048 * half) for half in range(2)]
-        key_words = placed([P, PASSES * S], U32, "key_words", 32768)
+        wk_raw = placed([P, PASSES, H], I32, "wk_raw", 0, 256)
+        gain = [placed([P, 8], F32, "gain%d" % t, 4096 + 64 * t) for t in range(4)]
+        nc.sync.dma_start(wk_raw[:], wk_words.rearrange("a p r i -> p a (r i)").bitcast(I32))
+        with nc.allow_non_contiguous_dma(reason="one gain to a partition"):
+            for t in range(4):
+                nc.sync.dma_start(gain[t][:, 0:1], g.rearrange("(b t e) -> t b e", t=4, e=8)[t])
+        for q in range(4):
+            nc.sync.dma_start(w_sc_raw[32 * q : 32 * q + 8, 0, :], wk_scales[:, 4 * q : 4 * q + 4, :].bitcast(I32))
+
+        left0 = [held([P, HALF], U32, "left0_0"), placed([P, HALF], U32, "left0_1", 57408)]
+        right0 = [held([P, HALF], U32, "right0_0"), placed([P, HALF], U32, "right0_1", 55360)]
+        left1 = [placed([P, HALF], U32, "left1_%d" % half, (8192, 14336)[half]) for half in range(2)]
+        right1 = [placed([P, HALF], U32, "right1_%d" % half, (10240, 12288)[half]) for half in range(2)]
+        key_words = placed([P, PASSES * S], U32, "key_words", 59456)
         key = [key_words[:, a * S : (a + 1) * S] for a in range(PASSES)]
-        gather_words(left0[0][:], list_l, 0, 0, HALF)
-        gather_words(right0[0][:], list_r, 0, 0, HALF)
         quantize_wl(0)
+        wo_raw = placed([P, 4, N], F32, "wo_raw", 37120, 256)
         for t in range(4):
             nc.sync.dma_start(wo_raw[:, t, :], wo.rearrange("(b t e) n -> t b e n", t=4, e=8)[t])
-        gather_words(left0[1][:], list_l, 0, HALF, S)
+        key_sc = placed([P, S // 4], I32, "key_sc", 35904)
+        for a in range(PASSES):
+            place_rows(key_sc, 4 * a, key_rows, a)
+        gather_words(left0[0][:], list_l, 0, 0, HALF)
+        gather_words(right0[0][:], list_r, 0, 0, HALF)
         quantize_wl(1)
         gather_words(left1[0][:], list_l, 1, 0, HALF)
         gather_words(right1[0][:], list_r, 1, 0, HALF)
         gather_words(right0[1][:], list_r, 0, HALF, S)
         gather_words(right1[1][:], list_r, 1, HALF, S)
+        gather_words(left0[1][:], list_l, 0, HALF, S)
         gather_words(left1[1][:], list_l, 1, HALF, S)
         gather_words(key[0], list_k, 0, 0, S)
         gather_words(key[1], list_k, 1, 0, S)
@@ -177,7 +175,7 @@ def tile_list_record_match_scores_kernel(
                 acc,
                 a,
                 wr_w[:, a, t * 64 : (t + 1) * 64].bitcast(U8).bitcast(FP4X4),
-                w_sc[:, a, t * 32 : (t + 1) * 32].bitcast(U8),
+                wr_sc[:, a, t * 32 : (t + 1) * 32].bitcast(U8),
                 words[a].bitcast(FP8X4),
                 right_sc[a][:].bitcast(U8)[:, cols],
             )
@@ -191,7 +189,7 @@ def tile_list_record_match_scores_kernel(
                 wl_w[:, a, cols].bitcast(FP8X4),
                 wl_sc[:, a, cols],
                 words[a].bitcast(FP8X4),
-                left_sc[4 * a : P, j0 : j0 + width],
+                left_sc[a][:].bitcast(U8)[:, j0 : j0 + width],
             )
 
         def left_pass_turned(acc, a, j0):
@@ -199,27 +197,31 @@ def tile_list_record_match_scores_kernel(
                 acc,
                 a,
                 (left0, left1)[a][0][:, j0 : j0 + P].bitcast(FP8X4),
-                left_sc[4 * a : P, j0 : j0 + P],
+                left_sc[a][:].bitcast(U8)[:, j0 : j0 + P],
                 wl_w[:, a, :].bitcast(FP8X4),
                 wl_sc[:, a, :],
             )
 
         tanh_b_first = held([P, 4, HALF], F32, "tanh_b_first")
-        tanh_a_first = placed([P, 4, H], F32, "tanh_a_first", 79872)
+        tanh_a_first = placed([P, 4, H], F32, "tanh_a_first", 45056)
         a_first = [bank([P, H], block) for block in range(4)]
         b_first = [bank([P, HALF], 4 + t) for t in range(4)]
         for a in range(PASSES):
             for block in range(4):
                 left_pass_turned(a_first[block][:], a, block * P)
-            for t in range(4):
+        for t in range(4):
+            for a in range(PASSES):
                 right_pass(b_first[t][:], a, t, 0, HALF)
         for block in range(4):
             nc.scalar.activation(tanh_a_first[:, block, :], a_first[block][:], ACT.Tanh)
         for t in range(4):
             nc.scalar.activation(tanh_b_first[:, t, :], b_first[t][:], ACT.Tanh)
+        wk_w = placed([P, PASSES, H], U32, "wk_w", 8192)
+        deal(wk_w[:], wk_raw[:], 8)
 
-        def tanh_of(side_pass, name, j0, width, first_bank):
-            result = held([P, 4, width], F32, name)
+        def tanh_of(side_pass, name, j0, width, first_bank, offset=None):
+            shape = [P, 4, width]
+            result = held(shape, F32, name) if offset is None else placed(shape, F32, name, offset)
             tiles = HALF // width
             for t0 in range(0, 4, tiles):
                 acc = bank([P, tiles, width], first_bank + t0 // tiles)
@@ -235,37 +237,39 @@ def tile_list_record_match_scores_kernel(
                 nc.scalar.activation(gained[:, t, :], tanh_b[:, t, :], ACT.Copy, scale=gain[t][:, 0:1])
             return gained
 
-        b_third = tanh_of(right_pass, "tanh_b_third", 512, QUARTER, 4)
-        a_third = tanh_of(left_pass, "tanh_a_third", 512, QUARTER, 6)
-        a_turned = [bank([P, HALF], t) for t in range(4)]
+        b_third = tanh_of(right_pass, "tanh_b_third", 512, QUARTER, 0, 71680)
+        a_third = tanh_of(left_pass, "tanh_a_third", 512, QUARTER, 4)
+        a_turned = [bank([P, HALF], (6 + t) % 8) for t in range(4)]
         for t in range(4):
             for block in range(4):
                 nc.tensor.transpose(
                     a_turned[t][:, block * P : (block + 1) * P], tanh_a_first[:, block, t * P : (t + 1) * P], ident[:]
                 )
         gained_third = with_gain(b_third, "gained_third", QUARTER)
-        b_sixth = tanh_of(right_pass, "tanh_b_sixth", 768, P, 4)
-        a_sixth = tanh_of(left_pass, "tanh_a_sixth", 768, P, 5)
+        wk_sc = placed([P, 1, H // 4], U32, "wk_sc", 71680)
+        deal(wk_sc[:], w_sc_raw[:, 0:1, :], 2)
+        b_sixth = tanh_of(right_pass, "tanh_b_sixth", 768, P, 2)
+        a_sixth = tanh_of(left_pass, "tanh_a_sixth", 768, P, 4)
         gained_sixth = with_gain(b_sixth, "gained_sixth", P)
-        wo_bf = held([P, 4 * N], BF16, "wo_bf", "tanh_b_third")
+        wo_bf = placed([P, 4 * N], BF16, "wo_bf", 73728)
         nc.scalar.copy(
             wo_bf[:].rearrange("p (c i t) -> p c t i", i=4, t=4),
             wo_raw[:].rearrange("p t (c i) -> p c t i", i=4),
         )
-        b_last = tanh_of(right_pass, "tanh_b_last", 896, P, 6)
-        a_last = tanh_of(left_pass, "tanh_a_last", 896, P, 7)
+        b_last = tanh_of(right_pass, "tanh_b_last", 896, P, 3)
+        a_last = tanh_of(left_pass, "tanh_a_last", 896, P, 5)
         gained_last = with_gain(b_last, "gained_last", P)
 
         def flat(tile):
             return tile[:].rearrange("p t c -> p (t c)")
 
-        agree_third = placed([P, 4, QUARTER], F32, "agree_third", 70656)
-        agree_sixth = placed([P, 4, P], F32, "agree_sixth", 74752)
+        agree_third = placed([P, 4, QUARTER], F32, "agree_third", 24576)
+        agree_sixth = placed([P, 4, P], F32, "agree_sixth", 28672)
         nc.gpsimd.tensor_tensor(flat(agree_third), flat(a_third), flat(gained_third), ALU.mult)
         nc.gpsimd.tensor_tensor(flat(agree_sixth), flat(a_sixth), flat(gained_sixth), ALU.mult)
 
-        agree_head = placed([P, 4, 3 * P], F32, "agree_head", 79872)
-        agree_fourth = placed([P, 4, P], F32, "agree_fourth", 86016)
+        agree_head = placed([P, 4, 3 * P], F32, "agree_head", 45056)
+        agree_fourth = placed([P, 4, P], F32, "agree_fourth", 51200)
         for t in range(4):
             for dst, c0, c1 in ((agree_head, 0, 3 * P), (agree_fourth, 3 * P, HALF)):
                 nc.vector.scalar_tensor_tensor(
@@ -273,7 +277,7 @@ def tile_list_record_match_scores_kernel(
                 )
 
         h_bf = {0: held([P, 4 * HALF], BF16, "h_bf0"), 768: held([P, 4 * QUARTER], BF16, "h_bf768")}
-        h_w = placed([P, S], U32, "h_w", 61440)
+        h_w = placed([P, S], U32, "h_w", 37120)
         h_sc = held([P, S], U8, "h_sc")
         out_v = out.rearrange("(m p) j -> p m j", p=P)
 
@@ -314,9 +318,9 @@ def tile_list_record_match_scores_kernel(
                     nc.tensor.matmul_mx(
                         out=acc[:, t, :],
                         lhsT=wk_w[:, a, t * P : (t + 1) * P].bitcast(FP8X4),
-                        lhsT_scale=w_sc[4 * a : P, 2, t * 32 : (t + 1) * 32].bitcast(U8),
+                        lhsT_scale=wk_sc[4 * a : P, 0, t * 32 : (t + 1) * 32].bitcast(U8),
                         rhs=key[a][:, j0 : j0 + P].bitcast(FP8X4),
-                        rhs_scale=key_sc[4 * a : P, j0 : j0 + P],
+                        rhs_scale=key_sc[4 * a : P, :].bitcast(U8)[:, j0 : j0 + P],
                         start=(a == 0 and t == 0),
                         stop=(a == PASSES - 1 and t == 3),
                     )
@@ -336,27 +340,27 @@ def tile_list_record_match_scores_kernel(
             store(j0, j1, score(j0, j1, number), queue)
 
         for block in range(3):
-            subtract(block * P, agree_head[:, :, block * P : (block + 1) * P], key_product(block * P, block)[:])
-        subtract(3 * P, agree_fourth[:], key_product(3 * P, 3)[:])
-        wo_w = placed([P, N], U32, "wo_w", 79872)
+            subtract(block * P, agree_head[:, :, block * P : (block + 1) * P], key_product(block * P, (6 + block) % 8)[:])
+        subtract(3 * P, agree_fourth[:], key_product(3 * P, 1)[:])
+        wo_w = placed([P, N], U32, "wo_w", 45056)
         wo_sc = held([P, N], U8, "wo_sc")
         nc.vector.quantize_mx(out=wo_w[:].bitcast(FP8X4), scales=wo_sc[:], in_=wo_bf[:])
         quantize_h(0, 512)
-        store(0, 256, score(0, 256, 2), nc.sync)
-        store(256, 512, score(256, 512, 3), nc.sync)
+        store(0, 256, score(0, 256, 0), nc.sync)
+        store(256, 512, score(256, 512, 1), nc.sync)
         agree_last = held([P, 4, P], F32, "agree_last", "h_bf0")
         nc.gpsimd.tensor_tensor(flat(agree_last), flat(a_last), flat(gained_last), ALU.mult)
-        h_bf[512] = held([P, 4 * QUARTER], BF16, "h_bf512", "tanh_b_third")
+        h_bf[512] = placed([P, 4 * QUARTER], BF16, "h_bf512", 73728)
         for block in range(2):
-            subtract(512 + block * P, agree_third[:, :, block * P : (block + 1) * P], key_product(512 + block * P, 4 + block)[:])
-        subtract(768, agree_sixth[:], key_product(768, 0)[:])
+            subtract(512 + block * P, agree_third[:, :, block * P : (block + 1) * P], key_product(512 + block * P, 2 + 2 * block)[:])
+        subtract(768, agree_sixth[:], key_product(768, 6)[:])
         quantize_h(512, 768)
-        store(512, 640, score(512, 640, 6), nc.sync)
-        store(640, 768, score(640, 768, 7), nc.sync)
-        key_sum = key_product(896, 1)
+        store(512, 640, score(512, 640, 3), nc.sync)
+        store(640, 768, score(640, 768, 5), nc.sync)
+        key_sum = key_product(896, 7)
         subtract(896, agree_last[:, :, 0:64], key_sum[:, :, 0:64])
-        finish(768, 896, 4, nc.sync)
+        finish(768, 896, 2, nc.sync)
         subtract(960, agree_last[:, :, 64:128], key_sum[:, :, 64:128])
-        finish(896, 960, 5, nc.scalar)
+        finish(896, 960, 4, nc.scalar)
         quantize_h(960, 1024)
-        store(960, 1024, score(960, 1024, 0, nc.vector.tensor_copy), nc.sync)
+        store(960, 1024, score(960, 1024, 6, nc.vector.tensor_copy), nc.sync)

@@ -45,10 +45,10 @@ def tile_list_record_match_scores_kernel(
         list_l = keep.tile([P, S // 16], U16, name="list_l")
         list_r = keep.tile([P, S // 16], U16, name="list_r")
         list_k = keep.tile([P, S // 16], U16, name="list_k")
-        wl_raw = [placed([P, 4, H], F32, "wl_raw%d" % a, 8192 * a, 256) for a in range(PASSES)]
-        tab_w = [placed([P, T], I32, "tab_w%d" % a, 16384 + 8192 * a, 256) for a in range(PASSES)]
-        tab_sc = placed([P, T // 4], I32, "tab_sc", 32768, 256)
-        wr_raw = placed([P, PASSES, H // 2], I32, "wr_raw", 69632, 256)
+        wl_raw = [placed([P, 4, H], F32, "wl_raw%d" % a, (7936, 32768)[a], 256) for a in range(PASSES)]
+        tab_w = [placed([P, T], I32, "tab_w%d" % a, (75776, 0)[a], 256) for a in range(PASSES)]
+        tab_sc = placed([P, T // 4], I32, "tab_sc", 41472, 256)
+        wr_raw = placed([P, PASSES, H // 2], I32, "wr_raw", 15872, 256)
         w_sc_raw = held([P, PASSES, H // 4], I32, "w_sc_raw")
 
         nc.vector.memset(w_sc_raw[:], 0)
@@ -83,8 +83,6 @@ def tile_list_record_match_scores_kernel(
             )
         load_table(0)
         load_wl(1)
-        load_table(1)
-        nc.sync.dma_start(wr_raw[:], wr_words.bitcast(I32).rearrange("a p w -> p a w"))
 
         left_rows = gather_scales("left_rows", list_l)
         right_rows = gather_scales("right_rows", list_r)
@@ -95,15 +93,13 @@ def tile_list_record_match_scores_kernel(
                 row = 16 * a + 4 * q
                 nc.sync.dma_start(plane[32 * q + first : 32 * q + first + 4, :], rows[row : row + 4, :].bitcast(I32))
 
-        left_sc = [held([P, S // 4], I32, "left_sc%d" % a) for a in range(PASSES)]
-        right_sc = [held([P, S // 4], I32, "right_sc%d" % a) for a in range(PASSES)]
-        for planes, rows in ((left_sc, left_rows), (right_sc, right_rows)):
-            for a in range(PASSES):
-                place_rows(planes[a], 0, rows, a)
+        left_sc = [held([P, S // 4], I32, "left_sc0"), placed([P, S // 4], I32, "left_sc1", 8192)]
+        right_sc = [placed([P, S // 4], I32, "right_sc%d" % a, 9216 + 1024 * a) for a in range(PASSES)]
+        place_rows(left_sc[0], 0, left_rows, 0)
 
         wl_w = held([P, PASSES, H], U32, "wl_w")
         wl_sc = held([P, PASSES, H], U8, "wl_sc")
-        wl_bf = [placed([P, 4, 4 * P], BF16, "wl_bf0", 36864), placed([P, 4, 4 * P], BF16, "wl_bf1", 57344)]
+        wl_bf = [held([P, 4, 4 * P], BF16, "wl_bf0"), placed([P, 4, 4 * P], BF16, "wl_bf1", 53248)]
 
         def round_wl(a):
             dst = wl_bf[a][:].rearrange("p t (b y e j) -> p y t b j e", y=2, e=4, j=4)
@@ -123,14 +119,19 @@ def tile_list_record_match_scores_kernel(
             )
 
         wr_w = held([P, PASSES, H // 2], U32, "wr_w")
-        wr_sc = held([P, PASSES, H // 4], U32, "wr_sc")
+        wr_sc = placed([P, PASSES, H // 4], U32, "wr_sc", 11264)
         round_wl(0)
+        load_table(1)
+        nc.sync.dma_start(wr_raw[:], wr_words.bitcast(I32).rearrange("a p w -> p a w"))
+        place_rows(left_sc[1], 0, left_rows, 1)
+        for a in range(PASSES):
+            place_rows(right_sc[a], 0, right_rows, a)
         deal(wr_sc[:], w_sc_raw[:], 2)
         round_wl(1)
         deal(wr_w[:], wr_raw[:], 4)
 
-        wk_raw = placed([P, PASSES, H], I32, "wk_raw", 0, 256)
-        gain = [placed([P, 8], F32, "gain%d" % t, 4096 + 64 * t) for t in range(4)]
+        wk_raw = placed([P, PASSES, H], I32, "wk_raw", 28928, 256)
+        gain = [placed([P, 8], F32, "gain%d" % t, 33024 + 64 * t) for t in range(4)]
         nc.sync.dma_start(wk_raw[:], wk_words.rearrange("a p r i -> p a (r i)").bitcast(I32))
         with nc.allow_non_contiguous_dma(reason="one gain to a partition"):
             for t in range(4):
@@ -138,37 +139,36 @@ def tile_list_record_match_scores_kernel(
         for q in range(4):
             nc.sync.dma_start(w_sc_raw[32 * q : 32 * q + 8, 0, :], wk_scales[:, 4 * q : 4 * q + 4, :].bitcast(I32))
 
-        left0 = [held([P, HALF], U32, "left0_0"), placed([P, HALF], U32, "left0_1", 57408)]
-        right0 = [held([P, HALF], U32, "right0_0"), placed([P, HALF], U32, "right0_1", 55360)]
-        left1 = [placed([P, HALF], U32, "left1_%d" % half, (8192, 14336)[half]) for half in range(2)]
-        right1 = [placed([P, HALF], U32, "right1_%d" % half, (10240, 12288)[half]) for half in range(2)]
-        key_words = placed([P, PASSES * S], U32, "key_words", 59456)
+        second0 = placed([P, S], U32, "second0", 12288)
+        left0 = [held([P, HALF], U32, "left0_0"), second0[:, HALF:S]]
+        right0 = [placed([P, HALF], U32, "right0_0", 59392), second0[:, 0:HALF]]
+        left1 = [placed([P, HALF], U32, "left1_%d" % half, (33280, 16384)[half]) for half in range(2)]
+        right1 = [placed([P, HALF], U32, "right1_%d" % half, (35328, 37376)[half]) for half in range(2)]
+        key_words = placed([P, PASSES * S], U32, "key_words", 59392)
         key = [key_words[:, a * S : (a + 1) * S] for a in range(PASSES)]
         quantize_wl(0)
-        wo_raw = placed([P, 4, N], F32, "wo_raw", 37120, 256)
-        for t in range(4):
-            nc.sync.dma_start(wo_raw[:, t, :], wo.rearrange("(b t e) n -> t b e n", t=4, e=8)[t])
-        key_sc = placed([P, S // 4], I32, "key_sc", 35904)
-        for a in range(PASSES):
-            place_rows(key_sc, 4 * a, key_rows, a)
         gather_words(left0[0][:], list_l, 0, 0, HALF)
         gather_words(right0[0][:], list_r, 0, 0, HALF)
         quantize_wl(1)
+        wo_raw = placed([P, 4, N], F32, "wo_raw", 49408, 256)
+        for t in range(4):
+            nc.sync.dma_start(wo_raw[:, t, :], wo.rearrange("(b t e) n -> t b e n", t=4, e=8)[t])
+        key_sc = placed([P, S // 4], I32, "key_sc", 53504)
+        for a in range(PASSES):
+            place_rows(key_sc, 4 * a, key_rows, a)
         gather_words(left1[0][:], list_l, 1, 0, HALF)
         gather_words(right1[0][:], list_r, 1, 0, HALF)
-        gather_words(right0[1][:], list_r, 0, HALF, S)
         gather_words(right1[1][:], list_r, 1, HALF, S)
-        gather_words(left0[1][:], list_l, 0, HALF, S)
+        gather_words(right0[1], list_r, 0, HALF, S)
         gather_words(left1[1][:], list_l, 1, HALF, S)
-        gather_words(key[0], list_k, 0, 0, S)
-        gather_words(key[1], list_k, 1, 0, S)
+        gather_words(left0[1], list_l, 0, HALF, S)
 
-        def mx(acc, a, lhs, lhs_sc, rhs, rhs_sc):
+        def mx(acc, a, lhs, lhs_sc, rhs, rhs_sc, first=0):
             nc.tensor.matmul_mx(
-                out=acc, lhsT=lhs, lhsT_scale=lhs_sc, rhs=rhs, rhs_scale=rhs_sc, start=(a == 0), stop=(a == PASSES - 1)
+                out=acc, lhsT=lhs, lhsT_scale=lhs_sc, rhs=rhs, rhs_scale=rhs_sc, start=(a == first), stop=(a != first)
             )
 
-        def right_pass(acc, a, t, j0, width):
+        def right_pass(acc, a, t, j0, width, first=0):
             cols = slice(j0, j0 + width)
             words = [tiles[j0 // HALF][:, j0 % HALF : j0 % HALF + width] for tiles in (right0, right1)]
             mx(
@@ -178,9 +178,10 @@ def tile_list_record_match_scores_kernel(
                 wr_sc[:, a, t * 32 : (t + 1) * 32].bitcast(U8),
                 words[a].bitcast(FP8X4),
                 right_sc[a][:].bitcast(U8)[:, cols],
+                first,
             )
 
-        def left_pass(acc, a, t, j0, width):
+        def left_pass(acc, a, t, j0, width, first=0):
             cols = slice(t * P, (t + 1) * P)
             words = [tiles[j0 // HALF][:, j0 % HALF : j0 % HALF + width] for tiles in (left0, left1)]
             mx(
@@ -190,6 +191,7 @@ def tile_list_record_match_scores_kernel(
                 wl_sc[:, a, cols],
                 words[a].bitcast(FP8X4),
                 left_sc[a][:].bitcast(U8)[:, j0 : j0 + width],
+                first,
             )
 
         def left_pass_turned(acc, a, j0):
@@ -203,7 +205,7 @@ def tile_list_record_match_scores_kernel(
             )
 
         tanh_b_first = held([P, 4, HALF], F32, "tanh_b_first")
-        tanh_a_first = placed([P, 4, H], F32, "tanh_a_first", 45056)
+        tanh_a_first = placed([P, 4, H], F32, "tanh_a_first", 18432)
         a_first = [bank([P, H], block) for block in range(4)]
         b_first = [bank([P, HALF], 4 + t) for t in range(4)]
         for a in range(PASSES):
@@ -216,7 +218,9 @@ def tile_list_record_match_scores_kernel(
             nc.scalar.activation(tanh_a_first[:, block, :], a_first[block][:], ACT.Tanh)
         for t in range(4):
             nc.scalar.activation(tanh_b_first[:, t, :], b_first[t][:], ACT.Tanh)
-        wk_w = placed([P, PASSES, H], U32, "wk_w", 8192)
+        gather_words(key[0], list_k, 0, 0, S)
+        gather_words(key[1], list_k, 1, 0, S)
+        wk_w = placed([P, PASSES, H], U32, "wk_w", 33280)
         deal(wk_w[:], wk_raw[:], 8)
 
         def tanh_of(side_pass, name, j0, width, first_bank, offset=None):
@@ -226,8 +230,8 @@ def tile_list_record_match_scores_kernel(
             for t0 in range(0, 4, tiles):
                 acc = bank([P, tiles, width], first_bank + t0 // tiles)
                 for i in range(tiles):
-                    for a in range(PASSES):
-                        side_pass(acc[:, i, :], a, t0 + i, j0, width)
+                    for a in (1, 0):
+                        side_pass(acc[:, i, :], a, t0 + i, j0, width, 1)
                 nc.scalar.activation(result[:, t0 : t0 + tiles, :], acc[:], ACT.Tanh)
             return result
 
@@ -263,13 +267,13 @@ def tile_list_record_match_scores_kernel(
         def flat(tile):
             return tile[:].rearrange("p t c -> p (t c)")
 
-        agree_third = placed([P, 4, QUARTER], F32, "agree_third", 24576)
-        agree_sixth = placed([P, 4, P], F32, "agree_sixth", 28672)
+        agree_third = placed([P, 4, QUARTER], F32, "agree_third", 0)
+        agree_sixth = placed([P, 4, P], F32, "agree_sixth", 4096)
         nc.gpsimd.tensor_tensor(flat(agree_third), flat(a_third), flat(gained_third), ALU.mult)
         nc.gpsimd.tensor_tensor(flat(agree_sixth), flat(a_sixth), flat(gained_sixth), ALU.mult)
 
-        agree_head = placed([P, 4, 3 * P], F32, "agree_head", 45056)
-        agree_fourth = placed([P, 4, P], F32, "agree_fourth", 51200)
+        agree_head = placed([P, 4, 3 * P], F32, "agree_head", 18432)
+        agree_fourth = placed([P, 4, P], F32, "agree_fourth", 24576)
         for t in range(4):
             for dst, c0, c1 in ((agree_head, 0, 3 * P), (agree_fourth, 3 * P, HALF)):
                 nc.vector.scalar_tensor_tensor(
@@ -277,7 +281,7 @@ def tile_list_record_match_scores_kernel(
                 )
 
         h_bf = {0: held([P, 4 * HALF], BF16, "h_bf0"), 768: held([P, 4 * QUARTER], BF16, "h_bf768")}
-        h_w = placed([P, S], U32, "h_w", 37120)
+        h_w = placed([P, S], U32, "h_w", 49408)
         h_sc = held([P, S], U8, "h_sc")
         out_v = out.rearrange("(m p) j -> p m j", p=P)
 
@@ -342,7 +346,7 @@ def tile_list_record_match_scores_kernel(
         for block in range(3):
             subtract(block * P, agree_head[:, :, block * P : (block + 1) * P], key_product(block * P, (6 + block) % 8)[:])
         subtract(3 * P, agree_fourth[:], key_product(3 * P, 1)[:])
-        wo_w = placed([P, N], U32, "wo_w", 45056)
+        wo_w = placed([P, N], U32, "wo_w", 18432)
         wo_sc = held([P, N], U8, "wo_sc")
         nc.vector.quantize_mx(out=wo_w[:].bitcast(FP8X4), scales=wo_sc[:], in_=wo_bf[:])
         quantize_h(0, 512)

@@ -139,8 +139,10 @@ def tile_list_record_match_scores_kernel(
         for q in range(4):
             nc.sync.dma_start(w_sc_raw[32 * q : 32 * q + 8, 0, :], wk_scales[:, 4 * q : 4 * q + 4, :].bitcast(I32))
 
-        second0 = placed([P, S], U32, "second0", 12288)
-        left0 = [held([P, HALF], U32, "left0_0"), second0[:, HALF:S]]
+        second0 = placed([P, HALF + QUARTER], U32, "second0", 13312)
+        left0_third = placed([P, QUARTER], U32, "left0_third", 39424)
+        left0 = [held([P, HALF], U32, "left0_0")]
+        left0_late = {HALF: left0_third[:], HALF + QUARTER: second0[:, HALF : HALF + QUARTER]}
         right0 = [placed([P, HALF], U32, "right0_0", 59392), second0[:, 0:HALF]]
         left1 = [placed([P, HALF], U32, "left1_%d" % half, (33280, 16384)[half]) for half in range(2)]
         right1 = [placed([P, HALF], U32, "right1_%d" % half, (35328, 37376)[half]) for half in range(2)]
@@ -156,12 +158,13 @@ def tile_list_record_match_scores_kernel(
         key_sc = placed([P, S // 4], I32, "key_sc", 53504)
         for a in range(PASSES):
             place_rows(key_sc, 4 * a, key_rows, a)
+        gather_words(left0_late[HALF], list_l, 0, HALF, HALF + QUARTER)
         gather_words(left1[0][:], list_l, 1, 0, HALF)
         gather_words(right1[0][:], list_r, 1, 0, HALF)
         gather_words(right1[1][:], list_r, 1, HALF, S)
         gather_words(right0[1], list_r, 0, HALF, S)
         gather_words(left1[1][:], list_l, 1, HALF, S)
-        gather_words(left0[1], list_l, 0, HALF, S)
+        gather_words(left0_late[HALF + QUARTER], list_l, 0, HALF + QUARTER, S)
 
         def mx(acc, a, lhs, lhs_sc, rhs, rhs_sc, first=0):
             nc.tensor.matmul_mx(
@@ -183,7 +186,11 @@ def tile_list_record_match_scores_kernel(
 
         def left_pass(acc, a, t, j0, width, first=0):
             cols = slice(t * P, (t + 1) * P)
-            words = [tiles[j0 // HALF][:, j0 % HALF : j0 % HALF + width] for tiles in (left0, left1)]
+            in_quarter = j0 % QUARTER
+            words = [
+                left0_late[j0 - in_quarter][:, in_quarter : in_quarter + width],
+                left1[1][:, j0 - HALF : j0 - HALF + width],
+            ]
             mx(
                 acc,
                 a,

@@ -140,7 +140,7 @@ def tile_list_record_match_scores_kernel(
             nc.sync.dma_start(w_sc_raw[32 * q : 32 * q + 8, 0, :], wk_scales[:, 4 * q : 4 * q + 4, :].bitcast(I32))
 
         second0 = placed([P, HALF + QUARTER], U32, "second0", 13312)
-        left0_third = placed([P, QUARTER], U32, "left0_third", 39424)
+        left0_third = held([P, QUARTER], U32, "left0_third")
         left0 = [held([P, HALF], U32, "left0_0")]
         left0_late = {HALF: left0_third[:], HALF + QUARTER: second0[:, HALF : HALF + QUARTER]}
         right0 = [placed([P, HALF], U32, "right0_0", 59392), second0[:, 0:HALF]]
@@ -151,6 +151,7 @@ def tile_list_record_match_scores_kernel(
         quantize_wl(0)
         gather_words(left0[0][:], list_l, 0, 0, HALF)
         gather_words(right0[0][:], list_r, 0, 0, HALF)
+        gather_words(left0_late[HALF], list_l, 0, HALF, HALF + QUARTER)
         quantize_wl(1)
         wo_raw = placed([P, 4, N], F32, "wo_raw", 49408, 256)
         for t in range(4):
@@ -158,7 +159,6 @@ def tile_list_record_match_scores_kernel(
         key_sc = placed([P, S // 4], I32, "key_sc", 53504)
         for a in range(PASSES):
             place_rows(key_sc, 4 * a, key_rows, a)
-        gather_words(left0_late[HALF], list_l, 0, HALF, HALF + QUARTER)
         gather_words(left1[0][:], list_l, 1, 0, HALF)
         gather_words(right1[0][:], list_r, 1, 0, HALF)
         gather_words(right1[1][:], list_r, 1, HALF, S)

from contextlib import ExitStack

import concourse.mybir as mybir
from concourse.masks import make_identity

K, H, N, T, S = 1024, 512, 256, 2048, 1024
FLOPS = 2 * S * H * (3 * K + N)

F32 = mybir.dt.float32
BF16 = mybir.dt.bfloat16
I32 = mybir.dt.int32
U32 = mybir.dt.uint32
U16 = mybir.dt.uint16
U8 = mybir.dt.uint8
FP8X4 = mybir.dt.float8_e4m3fn_x4
FP4X4 = mybir.dt.float4_e2m1fn_x4
ALU = mybir.AluOpType
ACT = mybir.ActivationFunctionType

P = 128
PASSES = K // 512
HALF = S // 2
QUARTER = S // 4


def tile_list_record_match_scores_kernel(
    tc, tab_words, tab_scales, offs, offs2, offs3, wl, wr_words, wr_scales, wk_words, wk_scales, g, wo, out
):
    nc = tc.nc
    with ExitStack() as ctx:
        keep = ctx.enter_context(tc.tile_pool(name="keep", bufs=1))
        laid = ctx.enter_context(tc.tile_pool(name="laid", bufs=1))
        res_pool = ctx.enter_context(tc.tile_pool(name="res", bufs=7))
        acc_pool = ctx.enter_context(tc.psum_pool(name="acc", bufs=1))

        def held(shape, dtype, name, slot=None):
            return keep.tile(shape, dtype, name=name, tag=slot or name, align_bytes=64)

        def placed(shape, dtype, name, offset, align=64):
            return laid.tile(shape, dtype, name=name, tag=name, align_bytes=align, offset=offset)

        def bank(shape, number):
            return acc_pool.tile(shape, F32, name="acc", tag="bank%d" % number)

        list_l = keep.tile([P, S // 16], U16, name="list_l")
        list_r = keep.tile([P, S // 16], U16, name="list_r")
        list_k = keep.tile([P, S // 16], U16, name="list_k")
        wl_raw = [placed([P, 4, H], F32, "wl_raw%d" % a, (7936, 32768)[a], 256) for a in range(PASSES)]
        tab_w = [placed([P, T], I32, "tab_w%d" % a, (75776, 0)[a], 256) for a in range(PASSES)]
        tab_sc = placed([P, T // 4], I32, "tab_sc", 41472, 256)
        wr_raw = placed([P, PASSES, H // 2], I32, "wr_raw", 15872, 256)
        w_sc_raw = held([P, PASSES, H // 4], I32, "w_sc_raw")

        nc.vector.memset(w_sc_raw[:], 0)
        nc.vector.memset(tab_sc[32:64, :], 0)
        nc.vector.memset(tab_sc[64:128, :], 0)
        ident = held([P, P], F32, "ident")
        make_identity(nc, ident[:])

        def load_table(a):
            nc.sync.dma_start(tab_w[a][:], tab_words[a].rearrange("p t i -> p (t i)").bitcast(I32))

        def load_wl(a):
            nc.sync.dma_start(wl_raw[a][:], wl[512 * a : 512 * (a + 1), :].rearrange("(p j) r -> p j r", j=4))

        def gather_scales(name, lst):
            rows = held([P, S], U8, name)
            nc.vector.tensor_copy(rows[:], tab_sc[:].bitcast(U8).indirect(lst[:]))
            return rows

        def gather_words(dst, lst, a, j0, j1):
            nc.vector.tensor_copy(dst, tab_w[a][:].bitcast(U32).indirect(lst[:, j0 // 16 : j1 // 16]))

        nc.sync.dma_start(list_l[:], offs)
        nc.scalar.dma_start(tab_sc[0:32, :], tab_scales.rearrange("a q t -> (a q) t").bitcast(I32))
        nc.sync.dma_start(list_r[:], offs2)
        load_wl(0)
        nc.sync.dma_start(list_k[:], offs3)
        for q in range(4):
            nc.sync.dma_start(
                w_sc_raw[32 * q : 32 * q + 4, :, :],
                wr_scales[:, 4 * q : 4 * q + 4, :].bitcast(I32).rearrange("a r w -> r a w"),
            )
        load_table(0)
        load_wl(1)

        left_rows = gather_scales("left_rows", list_l)
        right_rows = gather_scales("right_rows", list_r)
        key_rows = gather_scales("key_rows", list_k)

        def place_rows(plane, first, rows, a):
            for q in range(4):
                row = 16 * a + 4 * q
                nc.sync.dma_start(plane[32 * q + first : 32 * q + first + 4, :], rows[row : row + 4, :].bitcast(I32))

        left_sc = [held([P, S // 4], I32, "left_sc0"), placed([P, S // 4], I32, "left_sc1", 8192)]
        right_sc = [placed([P, S // 4], I32, "right_sc%d" % a, 9216 + 1024 * a) for a in range(PASSES)]
        place_rows(left_sc[0], 0, left_rows, 0)

        wl_w = held([P, PASSES, H], U32, "wl_w")
        wl_sc = held([P, PASSES, H], U8, "wl_sc")
        wl_bf = [held([P, 4, 4 * P], BF16, "wl_bf0"), placed([P, 4, 4 * P], BF16, "wl_bf1", 53248)]

        def round_wl(a):
            dst = wl_bf[a][:].rearrange("p t (b y e j) -> p y t b j e", y=2, e=4, j=4)
            src = wl_raw[a][:].rearrange("p j (b t y e) -> p y t b j e", t=4, y=2, e=4)
            for y in range(2):
                nc.scalar.copy(dst[:, y], src[:, y])

        def quantize_wl(a):
            nc.vector.quantize_mx(
                out=wl_w[:, a, :].bitcast(FP8X4), scales=wl_sc[:, a, :], in_=wl_bf[a][:].rearrange("p t x -> p (t x)")
            )

        def deal(dst, src, run):
            nc.scalar.copy(
                dst.bitcast(U32).rearrange("p a (t b w) -> p a t b w", t=4, w=run),
                src.bitcast(U32).rearrange("p a (b t w) -> p a t b w", t=4, w=run),
            )

        wr_w = held([P, PASSES, H // 2], U32, "wr_w")
        wr_sc = placed([P, PASSES, H // 4], U32, "wr_sc", 11264)
        round_wl(0)
        load_table(1)
        nc.sync.dma_start(wr_raw[:], wr_words.bitcast(I32).rearrange("a p w -> p a w"))
        place_rows(left_sc[1], 0, left_rows, 1)
        for a in range(PASSES):
            place_rows(right_sc[a], 0, right_rows, a)
        deal(wr_sc[:], w_sc_raw[:], 2)
        round_wl(1)
        deal(wr_w[:], wr_raw[:], 4)

        wk_raw = placed([P, PASSES, H], I32, "wk_raw", 28928, 256)
        gain = [placed([P, 8], F32, "gain%d" % t, 33024 + 64 * t) for t in range(4)]
        nc.sync.dma_start(wk_raw[:], wk_words.rearrange("a p r i -> p a (r i)").bitcast(I32))
        with nc.allow_non_contiguous_dma(reason="one gain to a partition"):
            for t in range(4):
                nc.sync.dma_start(gain[t][:, 0:1], g.rearrange("(b t e) -> t b e", t=4, e=8)[t])
        for q in range(4):
            nc.sync.dma_start(w_sc_raw[32 * q : 32 * q + 8, 0, :], wk_scales[:, 4 * q : 4 * q + 4, :].bitcast(I32))

        second0 = placed([P, HALF + QUARTER], U32, "second0", 13312)
        left0_third = held([P, QUARTER], U32, "left0_third")
        left0 = [held([P, HALF], U32, "left0_0")]
        left0_late = {HALF: left0_third[:], HALF + QUARTER: second0[:, HALF : HALF + QUARTER]}
        right0 = [placed([P, HALF], U32, "right0_0", 59392), second0[:, 0:HALF]]
        left1 = [placed([P, HALF], U32, "left1_%d" % half, (33280, 16384)[half]) for half in range(2)]
        right1 = [placed([P, HALF], U32, "right1_%d" % half, (35328, 37376)[half]) for half in range(2)]
        key_words = placed([P, PASSES * S], U32, "key_words", 59392)
        key = [key_words[:, a * S : (a + 1) * S] for a in range(PASSES)]
        quantize_wl(0)
        gather_words(left0[0][:], list_l, 0, 0, HALF)
        gather_words(right0[0][:], list_r, 0, 0, HALF)
        gather_words(left0_late[HALF], list_l, 0, HALF, HALF + QUARTER)
        quantize_wl(1)
        wo_raw = placed([P, 4, N], F32, "wo_raw", 49408, 256)
        for t in range(4):
            nc.sync.dma_start(wo_raw[:, t, :], wo.rearrange("(b t e) n -> t b e n", t=4, e=8)[t])
        key_sc = placed([P, S // 4], I32, "key_sc", 53504)
        for a in range(PASSES):
            place_rows(key_sc, 4 * a, key_rows, a)
        gather_words(left1[0][:], list_l, 1, 0, HALF)
        gather_words(right1[0][:], list_r, 1, 0, HALF)
        gather_words(right1[1][:], list_r, 1, HALF, S)
        gather_words(right0[1], list_r, 0, HALF, S)
        gather_words(left1[1][:], list_l, 1, HALF, S)
        gather_words(left0_late[HALF + QUARTER], list_l, 0, HALF + QUARTER, S)

        def mx(acc, a, lhs, lhs_sc, rhs, rhs_sc, first=0):
            nc.tensor.matmul_mx(
                out=acc, lhsT=lhs, lhsT_scale=lhs_sc, rhs=rhs, rhs_scale=rhs_sc, start=(a == first), stop=(a != first)
            )

        def right_pass(acc, a, t, j0, width, first=0):
            cols = slice(j0, j0 + width)
            words = [tiles[j0 // HALF][:, j0 % HALF : j0 % HALF + width] for tiles in (right0, right1)]
            mx(
                acc,
                a,
                wr_w[:, a, t * 64 : (t + 1) * 64].bitcast(U8).bitcast(FP4X4),
                wr_sc[:, a, t * 32 : (t + 1) * 32].bitcast(U8),
                words[a].bitcast(FP8X4),
                right_sc[a][:].bitcast(U8)[:, cols],
                first,
            )

        def left_pass(acc, a, t, j0, width, first=0):
            cols = slice(t * P, (t + 1) * P)
            in_quarter = j0 % QUARTER
            words = [
                left0_late[j0 - in_quarter][:, in_quarter : in_quarter + width],
                left1[1][:, j0 - HALF : j0 - HALF + width],
            ]
            mx(
                acc,
                a,
                wl_w[:, a, cols].bitcast(FP8X4),
                wl_sc[:, a, cols],
                words[a].bitcast(FP8X4),
                left_sc[a][:].bitcast(U8)[:, j0 : j0 + width],
                first,
            )

        def left_pass_turned(acc, a, j0):
            mx(
                acc,
                a,
                (left0, left1)[a][0][:, j0 : j0 + P].bitcast(FP8X4),
                left_sc[a][:].bitcast(U8)[:, j0 : j0 + P],
                wl_w[:, a, :].bitcast(FP8X4),
                wl_sc[:, a, :],
            )

        tanh_b_first = held([P, 4, HALF], F32, "tanh_b_first")
        tanh_a_first = placed([P, 4, H], F32, "tanh_a_first", 18432)
        a_first = [bank([P, H], block) for block in range(4)]
        b_first = [bank([P, HALF], 4 + t) for t in range(4)]
        for a in range(PASSES):
            for block in range(4):
                left_pass_turned(a_first[block][:], a, block * P)
        for t in range(4):
            for a in range(PASSES):
                right_pass(b_first[t][:], a, t, 0, HALF)
        for block in range(4):
            nc.scalar.activation(tanh_a_first[:, block, :], a_first[block][:], ACT.Tanh)
        for t in range(4):
            nc.scalar.activation(tanh_b_first[:, t, :], b_first[t][:], ACT.Tanh)
        gather_words(key[0], list_k, 0, 0, S)
        gather_words(key[1], list_k, 1, 0, S)
        wk_w = placed([P, PASSES, H], U32, "wk_w", 33280)
        deal(wk_w[:], wk_raw[:], 8)

        def tanh_of(side_pass, name, j0, width, first_bank, offset=None):
            shape = [P, 4, width]
            result = held(shape, F32, name) if offset is None else placed(shape, F32, name, offset)
            tiles = HALF // width
            for t0 in range(0, 4, tiles):
                acc = bank([P, tiles, width], first_bank + t0 // tiles)
                for i in range(tiles):
                    for a in (1, 0):
                        side_pass(acc[:, i, :], a, t0 + i, j0, width, 1)
                nc.scalar.activation(result[:, t0 : t0 + tiles, :], acc[:], ACT.Tanh)
            return result

        def with_gain(tanh_b, name, width):
            gained = held([P, 4, width], F32, name)
            for t in range(4):
                nc.scalar.activation(gained[:, t, :], tanh_b[:, t, :], ACT.Copy, scale=gain[t][:, 0:1])
            return gained

        b_third = tanh_of(right_pass, "tanh_b_third", 512, QUARTER, 0, 71680)
        a_third = tanh_of(left_pass, "tanh_a_third", 512, QUARTER, 4)
        a_turned = [bank([P, HALF], (6 + t) % 8) for t in range(4)]
        for t in range(4):
            for block in range(4):
                nc.tensor.transpose(
                    a_turned[t][:, block * P : (block + 1) * P], tanh_a_first[:, block, t * P : (t + 1) * P], ident[:]
                )
        gained_third = with_gain(b_third, "gained_third", QUARTER)
        wk_sc = placed([P, 1, H // 4], U32, "wk_sc", 71680)
        deal(wk_sc[:], w_sc_raw[:, 0:1, :], 2)
        b_sixth = tanh_of(right_pass, "tanh_b_sixth", 768, P, 2)
        a_sixth = tanh_of(left_pass, "tanh_a_sixth", 768, P, 4)
        gained_sixth = with_gain(b_sixth, "gained_sixth", P)
        wo_bf = placed([P, 4 * N], BF16, "wo_bf", 73728)
        nc.scalar.copy(
            wo_bf[:].rearrange("p (c i t) -> p c t i", i=4, t=4),
            wo_raw[:].rearrange("p t (c i) -> p c t i", i=4),
        )
        b_last = tanh_of(right_pass, "tanh_b_last", 896, P, 3)
        a_last = tanh_of(left_pass, "tanh_a_last", 896, P, 5)
        gained_last = with_gain(b_last, "gained_last", P)

        def flat(tile):
            return tile[:].rearrange("p t c -> p (t c)")

        agree_third = placed([P, 4, QUARTER], F32, "agree_third", 0)
        agree_sixth = placed([P, 4, P], F32, "agree_sixth", 4096)
        nc.gpsimd.tensor_tensor(flat(agree_third), flat(a_third), flat(gained_third), ALU.mult)
        nc.gpsimd.tensor_tensor(flat(agree_sixth), flat(a_sixth), flat(gained_sixth), ALU.mult)

        agree_head = placed([P, 4, 3 * P], F32, "agree_head", 18432)
        agree_fourth = placed([P, 4, P], F32, "agree_fourth", 24576)
        for t in range(4):
            for dst, c0, c1 in ((agree_head, 0, 3 * P), (agree_fourth, 3 * P, HALF)):
                nc.vector.scalar_tensor_tensor(
                    dst[:, t, :], tanh_b_first[:, t, c0:c1], gain[t][:, 0:1], a_turned[t][:, c0:c1], ALU.mult, ALU.mult
                )

        h_bf = {0: held([P, 4 * HALF], BF16, "h_bf0"), 768: held([P, 4 * QUARTER], BF16, "h_bf768")}
        h_w = placed([P, S], U32, "h_w", 49408)
        h_sc = held([P, S], U8, "h_sc")
        out_v = out.rearrange("(m p) j -> p m j", p=P)

        def h_words(j0, j1):
            return h_w[:, j0:j1].bitcast(FP8X4)

        def h_values(j0, j1):
            start = max(j for j in h_bf if j <= j0)
            return h_bf[start][:, 4 * (j0 - start) : 4 * (j1 - start)]

        def quantize_h(j0, j1):
            nc.vector.quantize_mx(out=h_words(j0, j1), scales=h_sc[:, j0:j1], in_=h_values(j0, j1))

        def score(j0, j1, number, copy=nc.scalar.copy):
            width = j1 - j0
            acc = bank([P, 2, width], number)
            for m in range(2):
                nc.tensor.matmul_mx(
                    out=acc[:, m, :],
                    lhsT=wo_w[:, m * P : (m + 1) * P].bitcast(FP8X4),
                    lhsT_scale=wo_sc[:, m * P : (m + 1) * P],
                    rhs=h_words(j0, j1),
                    rhs_scale=h_sc[:, j0:j1],
                    start=True,
                    stop=True,
                )
            res = res_pool.tile([P, 2, width], F32, name="res")
            copy(res[:], acc[:])
            return res

        def store(j0, j1, res, queue):
            queue.dma_start(out_v[:, :, j0:j1], res[:])

        def key_product(j0, number):
            acc = bank([P, 4, P], number)
            for a in range(PASSES):
                for t in range(4):
                    nc.tensor.matmul_mx(
                        out=acc[:, t, :],
                        lhsT=wk_w[:, a, t * P : (t + 1) * P].bitcast(FP8X4),
                        lhsT_scale=wk_sc[4 * a : P, 0, t * 32 : (t + 1) * 32].bitcast(U8),
                        rhs=key[a][:, j0 : j0 + P].bitcast(FP8X4),
                        rhs_scale=key_sc[4 * a : P, :].bitcast(U8)[:, j0 : j0 + P],
                        start=(a == 0 and t == 0),
                        stop=(a == PASSES - 1 and t == 3),
                    )
            return acc

        def subtract(j0, agree, key_sum):
            width = agree.shape[2]
            nc.vector.tensor_tensor(
                h_values(j0, j0 + width).rearrange("p (c i t) -> p c t i", i=2, t=4),
                agree.rearrange("p t (c i) -> p c t i", i=2),
                key_sum.rearrange("p t (c i) -> p c t i", i=2),
                ALU.subtract,
            )

        def finish(j0, j1, number, queue):
            quantize_h(j0, j1)
            store(j0, j1, score(j0, j1, number), queue)

        for block in range(3):
            subtract(block * P, agree_head[:, :, block * P : (block + 1) * P], key_product(block * P, (6 + block) % 8)[:])
        subtract(3 * P, agree_fourth[:], key_product(3 * P, 1)[:])
        wo_w = placed([P, N], U32, "wo_w", 18432)
        wo_sc = held([P, N], U8, "wo_sc")
        nc.vector.quantize_mx(out=wo_w[:].bitcast(FP8X4), scales=wo_sc[:], in_=wo_bf[:])
        quantize_h(0, 512)
        store(0, 256, score(0, 256, 0), nc.sync)
        store(256, 512, score(256, 512, 1), nc.sync)
        agree_last = held([P, 4, P], F32, "agree_last", "h_bf0")
        nc.gpsimd.tensor_tensor(flat(agree_last), flat(a_last), flat(gained_last), ALU.mult)
        h_bf[512] = placed([P, 4 * QUARTER], BF16, "h_bf512", 73728)
        for block in range(2):
            subtract(512 + block * P, agree_third[:, :, block * P : (block + 1) * P], key_product(512 + block * P, 2 + 2 * block)[:])
        subtract(768, agree_sixth[:], key_product(768, 6)[:])
        quantize_h(512, 768)
        store(512, 640, score(512, 640, 3), nc.sync)
        store(640, 768, score(640, 768, 5), nc.sync)
        key_sum = key_product(896, 7)
        subtract(896, agree_last[:, :, 0:64], key_sum[:, :, 0:64])
        finish(768, 896, 2, nc.sync)
        subtract(960, agree_last[:, :, 64:128], key_sum[:, :, 64:128])
        finish(896, 960, 4, nc.scalar)
        quantize_h(960, 1024)
        store(960, 1024, score(960, 1024, 6, nc.vector.tensor_copy), nc.sync)
